import numpy as np
import ml_dtypes


def mxq(x, axis, fmt="e4m3"):
    dtype, down = {"e4m3": (ml_dtypes.float8_e4m3fn, 7), "e5m2": (ml_dtypes.float8_e5m2, 14)}[fmt]
    v = np.moveaxis(np.asarray(x, np.float32).astype(ml_dtypes.bfloat16).astype(np.float64), axis, -1)
    blocks = v.reshape(v.shape[:-1] + (-1, 32))
    amax = np.abs(blocks).max(-1, keepdims=True)
    byte = np.maximum(np.where(amax > 0, np.frexp(amax)[1] - 1 + 127, 0) - down, 1)
    scale = np.exp2(byte - 127.0)
    codes = (blocks / scale).astype(np.float32).astype(dtype).astype(np.float64)
    return np.moveaxis((codes * scale).reshape(v.shape), -1, axis)


WIDE = False


def mx_kscale(k):
    if not WIDE:
        return np.ones(k)
    levels = np.array([10, -10, 5, -5, 0])
    if k % 512:
        return np.exp2(np.random.permutation(np.resize(levels, k // 32))).repeat(32)
    a = np.empty((k // 512, 16))
    for p in range(k // 512):
        a[p, :8] = np.random.permutation(np.resize(levels, 8))
        for g in range(8):
            far = levels[np.abs(levels - a[p, g]) >= 10]
            a[p, g + 8] = far[np.random.randint(len(far))]
    return np.exp2(a.ravel()).repeat(32)


def f64(x):
    return np.asarray(x).astype(np.float64)


def striped(idx):
    return np.tile(idx.reshape(-1, 16).T, (8, 1)).astype(np.uint16)


def unstriped(offs):
    return offs[:16].T.reshape(-1).astype(np.int64)


E2M1 = np.array([0.0, 0.5, 1.0, 1.5, 2.0, 3.0, 4.0, 6.0, -0.0, -0.5, -1.0, -1.5, -2.0, -3.0, -4.0, -6.0])


def pack_weight(w, fmt):
    k, n = w.shape
    w = f64(np.asarray(w, np.float32).astype(ml_dtypes.bfloat16)).reshape(k // 32, 32, n)
    amax = np.abs(w).max(1)
    if fmt == "e4m3":
        byte = np.frexp(amax)[1] - 1 + 127 - 7
    else:
        mant, ex = np.frexp(amax / 6.0)
        byte = np.where(mant > 0.5, ex, ex - 1) + 127
    byte = np.clip(np.where(amax > 0, byte, 1), 1, 254)
    scaled = (w * np.exp2(127.0 - byte)[:, None, :]).reshape(k, n).astype(np.float32)
    by_word = np.ascontiguousarray(scaled.reshape(k // 512, 128, 4, n).transpose(0, 1, 3, 2))
    if fmt == "e4m3":
        words = by_word.astype(ml_dtypes.float8_e4m3fn).view(np.uint8)
    else:
        c = by_word.astype(ml_dtypes.float4_e2m1fn).view(np.uint8) & 0xF
        words = (c[..., 0::2] | (c[..., 1::2] << 4)).reshape(k // 512, 128, 2 * n)
    return np.ascontiguousarray(words), np.ascontiguousarray(byte.astype(np.uint8).reshape(k // 512, 16, n))


def unpack_weight(words, scales, fmt):
    g, _, n = scales.shape
    words = np.ascontiguousarray(words).reshape(g, 128, n, -1)
    if fmt == "e4m3":
        vals = words.view(ml_dtypes.float8_e4m3fn).astype(np.float64)
    else:
        nib = np.empty((g, 128, n, 4), np.uint8)
        nib[..., 0::2] = words & 0xF
        nib[..., 1::2] = words >> 4
        vals = E2M1[nib]
    vals = vals * np.repeat(np.exp2(scales.astype(np.float64) - 127.0), 8, axis=1)[..., None]
    return vals.transpose(0, 1, 3, 2).reshape(g * 512, n)


def silu(v):
    return v / (1.0 + np.exp(-np.maximum(v, -700.0)))


K, T, E, C, N = 1024, 1280, 10, 256, 128


def by_expert(wq, xq):
    return np.concatenate([wq[e].T @ xq[:, e * C:(e + 1) * C] for e in range(E)], axis=1)


def setup_inputs():
    n = np.random.standard_normal
    s = mx_kscale(K)[:, None]
    first = np.random.permutation(np.repeat(np.arange(E), T // E))
    second = (first + 1 + np.random.permutation(np.repeat(np.arange(E - 1), -(-T // (E - 1)))[:T])) % E
    while np.bincount(second, minlength=E).max() != T // E:
        load = np.bincount(second, minlength=E); hi, lo = int(load.argmax()), int(load.argmin())
        t = np.flatnonzero((second == hi) & (first != lo))[0]; second[t] = lo
    slot_token = np.empty(E * C, np.int64); pos = np.empty((2, T), np.int64); fill = np.zeros(E, np.int64)
    place = np.stack([np.random.permutation(C) for _ in range(E)])
    for r, deal in enumerate((first, second)):
        for t in np.random.permutation(T):
            e = deal[t]; j = e * C + place[e, fill[e]]; fill[e] += 1; slot_token[j] = t; pos[r, t] = j
    g = np.random.uniform(0.2, 0.8, T)
    w = [pack_weight(m, "e2m1") for m in n((E, K, N)) / np.sqrt(K) / s[None]]
    w_slot = np.empty(E * C); w_slot[pos[0]] = g; w_slot[pos[1]] = 1.0 - g
    return {
        "xT": (n((K, T)) * s).astype(np.float32),
        "w_words": np.stack([m[0] for m in w]),
        "w_scales": np.stack([m[1] for m in w]),
        "b": (0.3 * n((N, E))).astype(np.float32),
        "gate": np.tile(w_slot, (K, 1)).astype(np.float32),
        "offs": striped(slot_token),
        "pos1": striped(pos[0]),
        "pos2": striped(pos[1]),
    }


def reference(xT, w_words, w_scales, b, gate, offs, pos1, pos2):
    idx = unstriped(offs)
    w = np.stack([unpack_weight(w_words[e], w_scales[e], "e2m1") for e in range(E)])
    xq = mxq(f64(gate) * f64(xT)[:, idx], 0, "e4m3")
    y = by_expert(w, xq)
    y = silu(y + np.repeat(f64(b), C, axis=1))
    return y[:, unstriped(pos1)] + y[:, unstriped(pos2)]

@@ -1,0 +1,159 @@
+from contextlib import ExitStack
+
+import concourse.mybir as mybir
+
+K, T, E, C, N = 1024, 1280, 10, 256, 128
+S = E * C
+FLOPS = 2 * K * N * S
+BYTES = 4 * K * T + E * K * N // 2 + E * K * N // 32 + 4 * N * E + 4 * S + 2 * 128 * (S + 2 * T) // 16 + 4 * N * T
+
+F32 = mybir.dt.float32
+BF16 = mybir.dt.bfloat16
+I32 = mybir.dt.int32
+U32 = mybir.dt.uint32
+U16 = mybir.dt.uint16
+U8 = mybir.dt.uint8
+FP8X4 = mybir.dt.float8_e4m3fn_x4
+FP4X4 = mybir.dt.float4_e2m1fn_x4
+MULT = mybir.AluOpType.mult
+ADD = mybir.AluOpType.add
+SILU = mybir.ActivationFunctionType.Silu
+
+P = 128
+PACK = 4
+PASSES = K // (P * PACK)
+LIST = 16
+UNIT = 128
+QUANT = 512
+
+GROUPS = [
+    (0, 0, 1024),
+    (1, 0, 1024),
+    (0, 1024, 2048),
+    (1, 1024, 1536),
+    (0, 2048, 2560),
+    (1, 1536, 2048),
+    (1, 2048, 2304),
+    (1, 2304, 2432),
+    (1, 2432, 2560),
+]
+FIRST = 384
+COMBINE = [(0, 640), (640, 960), (960, 1280)]
+
+
+def tile_moe_pre_lin_silu_kernel(tc, xT, w_words, w_scales, b, gate, offs, pos1, pos2, out):
+    nc = tc.nc
+    with ExitStack() as ctx:
+        keep = ctx.enter_context(tc.tile_pool(name="keep", bufs=1))
+        psum = ctx.enter_context(tc.psum_pool(name="psum", bufs=8))
+
+        offs_sb = keep.tile([P, S // LIST], U16, name="offs_sb")
+        pos1_sb = keep.tile([P, T // LIST], U16, name="pos1_sb")
+        pos2_sb = keep.tile([P, T // LIST], U16, name="pos2_sb")
+        gate_sb = keep.tile([P, S], F32, name="gate_sb")
+        x_sb = [keep.tile([P, T], F32, name="x%d" % r) for r in range(PASSES * PACK)]
+        w_sb = keep.tile([P, E * PASSES, 2 * N], U8, name="w_sb", align_bytes=64)
+        ws_sb = keep.tile([P, E * PASSES, N], U8, name="ws_sb", align_bytes=64)
+        b_sb = keep.tile([P, E], F32, name="b_sb")
+        codes = [keep.tile([P, S], U32, name="codes%d" % a, align_bytes=64) for a in range(PASSES)]
+        scales = [keep.tile([P, S], U8, name="scales%d" % a, align_bytes=64) for a in range(PASSES)]
+        y_sb = keep.tile([P, S], F32, name="y_sb")
+
+        x_rows = xT.rearrange("(a p j) t -> a j p t", a=PASSES, j=PACK)
+
+        def load_x(r):
+            nc.sync.dma_start(out=x_sb[r][:], in_=x_rows[r // PACK, r % PACK])
+
+        def load_gate(lo, hi):
+            nc.sync.dma_start(out=gate_sb[:, lo:hi], in_=gate[0:P, lo:hi])
+
+        nc.vector.memset(ws_sb[:].bitcast(I32), 0)
+
+        load_x(0)
+        nc.sync.dma_start(offs_sb[:], offs)
+        load_gate(0, FIRST)
+        load_gate(FIRST, 1024)
+        for r in range(1, PASSES * PACK):
+            load_x(r)
+        load_gate(1024, S)
+        nc.sync.dma_start(out=w_sb[:].bitcast(I32), in_=w_words.rearrange("e a p c -> p (e a) c").bitcast(I32))
+        scale_rows = w_scales.rearrange("e a q n -> q (e a) n").bitcast(I32)
+        for quad in range(4):
+            nc.sync.dma_start(out=ws_sb[32 * quad : 32 * quad + 4].bitcast(I32), in_=scale_rows[4 * quad : 4 * quad + 4])
+        nc.sync.dma_start(out=b_sb[:], in_=b)
+        nc.sync.dma_start(pos1_sb[:], pos1)
+        nc.sync.dma_start(pos2_sb[:], pos2)
+
+        def gather_and_round(g):
+            a, lo, hi = GROUPS[g]
+            planes = keep.tile([P, PACK, hi - lo], F32, name="planes%d" % g)
+            for j in range(PACK):
+                cuts = [lo, FIRST, hi] if (g, j) == (0, 0) else [lo, hi]
+                for c0, c1 in zip(cuts, cuts[1:]):
+                    nc.vector.tensor_tensor(
+                        planes[:, j, c0 - lo : c1 - lo],
+                        x_sb[a * PACK + j][:].indirect(offs_sb[:, c0 // LIST : c1 // LIST]),
+                        gate_sb[:, c0:c1],
+                        MULT,
+                    )
+            pieces = []
+            for c0 in range(lo, hi, QUANT):
+                c1 = min(hi, c0 + QUANT)
+                rounded = keep.tile([P, c1 - c0, PACK], BF16, name="rounded%d_%d" % (g, c0), align_bytes=64)
+                nc.scalar.copy(
+                    out=rounded[:].rearrange("p (c i) j -> p c j i", i=4),
+                    in_=planes[:, :, c0 - lo : c1 - lo].rearrange("p j (c i) -> p c j i", i=4),
+                )
+                pieces.append((a, c0, c1, rounded))
+            return pieces
+
+        def quantize(pieces):
+            for a, c0, c1, rounded in pieces:
+                nc.vector.quantize_mx(
+                    out=codes[a][:, c0:c1].bitcast(FP8X4),
+                    scales=scales[a][:, c0:c1],
+                    in_=rounded[:].rearrange("p c j -> p (c j)"),
+                )
+
+        waiting = []
+        for g in range(len(GROUPS)):
+            fresh = gather_and_round(g)
+            quantize(waiting)
+            waiting = fresh
+        quantize(waiting)
+
+        for c0 in range(0, S, UNIT):
+            e = c0 // C
+            cols = slice(c0, c0 + UNIT)
+            acc = psum.tile([P, UNIT], F32, name="acc")
+            for a in range(PASSES):
+                nc.tensor.matmul_mx(
+                    out=acc[:],
+                    lhsT=w_sb[:, e * PASSES + a, :].bitcast(FP4X4),
+                    lhsT_scale=ws_sb[:, e * PASSES + a, :],
+                    rhs=codes[a][:, cols].bitcast(FP8X4),
+                    rhs_scale=scales[a][:, cols],
+                    start=(a == 0),
+                    stop=(a == PASSES - 1),
+                )
+            nc.scalar.activation(out=y_sb[:, cols], in_=acc[:], func=SILU, bias=b_sb[:, e : e + 1])
+
+        first = keep.tile([P, T], F32, name="first")
+        second = keep.tile([P, T], F32, name="second")
+        total = keep.tile([P, T], F32, name="total")
+
+        def fetch(dst, lst, lo, hi):
+            nc.vector.tensor_copy(dst[:, lo:hi], y_sb[:].indirect(lst[:, lo // LIST : hi // LIST]))
+
+        def combine(lo, hi):
+            nc.vector.tensor_tensor(total[:, lo:hi], first[:, lo:hi], second[:, lo:hi], ADD)
+            nc.sync.dma_start(out=out[:, lo:hi], in_=total[:, lo:hi])
+
+        fetch(first, pos1_sb, 0, 640)
+        fetch(second, pos2_sb, *COMBINE[0])
+        fetch(first, pos1_sb, 640, T)
+        combine(*COMBINE[0])
+        fetch(second, pos2_sb, *COMBINE[1])
+        fetch(second, pos2_sb, *COMBINE[2])
+        combine(*COMBINE[1])
+        combine(*COMBINE[2])

@@ -24,19 +24,18 @@ PACK = 4
 PASSES = K // (P * PACK)
 LIST = 16
 UNIT = 128
-QUANT = 512
+QUANT = (128, 256, 512)
 
 GROUPS = [
-    (0, 0, 1024),
+    (0, 0, 1280),
     (1, 0, 1024),
-    (0, 1024, 2048),
-    (1, 1024, 1536),
-    (0, 2048, 2560),
-    (1, 1536, 2048),
-    (1, 2048, 2304),
-    (1, 2304, 2432),
+    (0, 1280, 2560),
+    (1, 1024, 1792),
+    (1, 1792, 2176),
+    (1, 2176, 2432),
     (1, 2432, 2560),
 ]
+WINDOW = T + 32
 FIRST = 384
 COMBINE = [(0, 640), (640, 960), (960, 1280)]
 
@@ -45,13 +44,14 @@ def tile_moe_pre_lin_silu_kernel(tc, xT, w_words, w_scales, b, gate, offs, pos1,
     nc = tc.nc
     with ExitStack() as ctx:
         keep = ctx.enter_context(tc.tile_pool(name="keep", bufs=1))
+        stage = ctx.enter_context(tc.tile_pool(name="stage", bufs=2))
         psum = ctx.enter_context(tc.psum_pool(name="psum", bufs=8))
 
         offs_sb = keep.tile([P, S // LIST], U16, name="offs_sb")
         pos1_sb = keep.tile([P, T // LIST], U16, name="pos1_sb")
         pos2_sb = keep.tile([P, T // LIST], U16, name="pos2_sb")
         gate_sb = keep.tile([P, S], F32, name="gate_sb")
-        x_sb = [keep.tile([P, T], F32, name="x%d" % r) for r in range(PASSES * PACK)]
+        x_sb = [keep.tile([P, WINDOW], F32, name="x%d" % r) for r in range(PASSES * PACK)]
         w_sb = keep.tile([P, E * PASSES, 2 * N], U8, name="w_sb", align_bytes=64)
         ws_sb = keep.tile([P, E * PASSES, N], U8, name="ws_sb", align_bytes=64)
         b_sb = keep.tile([P, E], F32, name="b_sb")
@@ -62,7 +62,7 @@ def tile_moe_pre_lin_silu_kernel(tc, xT, w_words, w_scales, b, gate, offs, pos1,
         x_rows = xT.rearrange("(a p j) t -> a j p t", a=PASSES, j=PACK)
 
         def load_x(r):
-            nc.sync.dma_start(out=x_sb[r][:], in_=x_rows[r // PACK, r % PACK])
+            nc.sync.dma_start(out=x_sb[r][:, 0:T], in_=x_rows[r // PACK, r % PACK])
 
         def load_gate(lo, hi):
             nc.sync.dma_start(out=gate_sb[:, lo:hi], in_=gate[0:P, lo:hi])
@@ -72,10 +72,10 @@ def tile_moe_pre_lin_silu_kernel(tc, xT, w_words, w_scales, b, gate, offs, pos1,
         load_x(0)
         nc.sync.dma_start(offs_sb[:], offs)
         load_gate(0, FIRST)
-        load_gate(FIRST, 1024)
+        load_gate(FIRST, T)
         for r in range(1, PASSES * PACK):
             load_x(r)
-        load_gate(1024, S)
+        load_gate(T, S)
         nc.sync.dma_start(out=w_sb[:].bitcast(I32), in_=w_words.rearrange("e a p c -> p (e a) c").bitcast(I32))
         scale_rows = w_scales.rearrange("e a q n -> q (e a) n").bitcast(I32)
         for quad in range(4):
@@ -86,7 +86,7 @@ def tile_moe_pre_lin_silu_kernel(tc, xT, w_words, w_scales, b, gate, offs, pos1,
 
         def gather_and_round(g):
             a, lo, hi = GROUPS[g]
-            planes = keep.tile([P, PACK, hi - lo], F32, name="planes%d" % g)
+            planes = stage.tile([P, PACK, hi - lo], F32, name="planes")
             for j in range(PACK):
                 cuts = [lo, FIRST, hi] if (g, j) == (0, 0) else [lo, hi]
                 for c0, c1 in zip(cuts, cuts[1:]):
@@ -97,8 +97,10 @@ def tile_moe_pre_lin_silu_kernel(tc, xT, w_words, w_scales, b, gate, offs, pos1,
                         MULT,
                     )
             pieces = []
-            for c0 in range(lo, hi, QUANT):
-                c1 = min(hi, c0 + QUANT)
+            c1 = lo
+            while c1 < hi:
+                c0 = c1
+                c1 = c0 + max(w for w in QUANT if c0 + w <= hi)
                 rounded = keep.tile([P, c1 - c0, PACK], BF16, name="rounded%d_%d" % (g, c0), align_bytes=64)
                 nc.scalar.copy(
                     out=rounded[:].rearrange("p (c i) j -> p c j i", i=4),
@@ -115,14 +117,7 @@ def tile_moe_pre_lin_silu_kernel(tc, xT, w_words, w_scales, b, gate, offs, pos1,
                     in_=rounded[:].rearrange("p c j -> p (c j)"),
                 )
 
-        waiting = []
-        for g in range(len(GROUPS)):
-            fresh = gather_and_round(g)
-            quantize(waiting)
-            waiting = fresh
-        quantize(waiting)
-
-        for c0 in range(0, S, UNIT):
+        def multiply(c0):
             e = c0 // C
             cols = slice(c0, c0 + UNIT)
             acc = psum.tile([P, UNIT], F32, name="acc")
@@ -138,22 +133,36 @@ def tile_moe_pre_lin_silu_kernel(tc, xT, w_words, w_scales, b, gate, offs, pos1,
                 )
             nc.scalar.activation(out=y_sb[:, cols], in_=acc[:], func=SILU, bias=b_sb[:, e : e + 1])
 
+        def finish(pieces):
+            quantize(pieces)
+            for a, c0, c1, rounded in pieces:
+                if a == PASSES - 1:
+                    for u in range(c0, c1, UNIT):
+                        multiply(u)
+
+        waiting = []
+        for g in range(len(GROUPS)):
+            fresh = gather_and_round(g)
+            finish(waiting)
+            waiting = fresh
+        finish(waiting)
+
         first = keep.tile([P, T], F32, name="first")
         second = keep.tile([P, T], F32, name="second")
-        total = keep.tile([P, T], F32, name="total")
 
         def fetch(dst, lst, lo, hi):
             nc.vector.tensor_copy(dst[:, lo:hi], y_sb[:].indirect(lst[:, lo // LIST : hi // LIST]))
 
-        def combine(lo, hi):
-            nc.vector.tensor_tensor(total[:, lo:hi], first[:, lo:hi], second[:, lo:hi], ADD)
-            nc.sync.dma_start(out=out[:, lo:hi], in_=total[:, lo:hi])
+        def combine(engine, lo, hi):
+            total = keep.tile([P, hi - lo], F32, name="total%d" % lo)
+            engine.tensor_tensor(total[:], first[:, lo:hi], second[:, lo:hi], ADD)
+            nc.sync.dma_start(out=out[:, lo:hi], in_=total[:])
 
         fetch(first, pos1_sb, 0, 640)
         fetch(second, pos2_sb, *COMBINE[0])
         fetch(first, pos1_sb, 640, T)
-        combine(*COMBINE[0])
+        combine(nc.gpsimd, *COMBINE[0])
         fetch(second, pos2_sb, *COMBINE[1])
         fetch(second, pos2_sb, *COMBINE[2])
-        combine(*COMBINE[1])
-        combine(*COMBINE[2])
+        combine(nc.gpsimd, *COMBINE[1])
+        combine(nc.vector, *COMBINE[2])

@@ -24,34 +24,30 @@ PACK = 4
 PASSES = K // (P * PACK)
 LIST = 16
 UNIT = 128
-QUANT = (128, 256, 512)
-
+WIDE = S + 32
+HEAD = [0, 256, 1024, S]
 GROUPS = [
-    (0, 0, 1280),
-    (1, 0, 1024),
-    (0, 1280, 2560),
-    (1, 1024, 1792),
-    (1, 1792, 2176),
-    (1, 2176, 2432),
-    (1, 2432, 2560),
+    (0, 1024, (1024,)),
+    (1024, 1792, (512, 256)),
+    (1792, 2176, (256, 128)),
+    (2304, 2560, (256,)),
+    (2176, 2304, (128,)),
 ]
-WINDOW = T + 32
-FIRST = 384
-COMBINE = [(0, 640), (640, 960), (960, 1280)]
+FETCH = [(0, 704), (704, 1280)]
+COMBINE = [(0, 0, 704), (1, 704, 1088), (1, 1088, 1280)]
 
 
 def tile_moe_pre_lin_silu_kernel(tc, xT, w_words, w_scales, b, gate, offs, pos1, pos2, out):
     nc = tc.nc
     with ExitStack() as ctx:
         keep = ctx.enter_context(tc.tile_pool(name="keep", bufs=1))
-        stage = ctx.enter_context(tc.tile_pool(name="stage", bufs=2))
         psum = ctx.enter_context(tc.psum_pool(name="psum", bufs=8))
 
         offs_sb = keep.tile([P, S // LIST], U16, name="offs_sb")
         pos1_sb = keep.tile([P, T // LIST], U16, name="pos1_sb")
         pos2_sb = keep.tile([P, T // LIST], U16, name="pos2_sb")
         gate_sb = keep.tile([P, S], F32, name="gate_sb")
-        x_sb = [keep.tile([P, WINDOW], F32, name="x%d" % r) for r in range(PASSES * PACK)]
+        x_sb = [keep.tile([P, WIDE if r < PACK else T], F32, name="x%d" % r) for r in range(PASSES * PACK)]
         w_sb = keep.tile([P, E * PASSES, 2 * N], U8, name="w_sb", align_bytes=64)
         ws_sb = keep.tile([P, E * PASSES, N], U8, name="ws_sb", align_bytes=64)
         b_sb = keep.tile([P, E], F32, name="b_sb")
@@ -71,11 +67,10 @@ def tile_moe_pre_lin_silu_kernel(tc, xT, w_words, w_scales, b, gate, offs, pos1,
 
         load_x(0)
         nc.sync.dma_start(offs_sb[:], offs)
-        load_gate(0, FIRST)
-        load_gate(FIRST, T)
+        for lo, hi in zip(HEAD, HEAD[1:]):
+            load_gate(lo, hi)
         for r in range(1, PASSES * PACK):
             load_x(r)
-        load_gate(T, S)
         nc.sync.dma_start(out=w_sb[:].bitcast(I32), in_=w_words.rearrange("e a p c -> p (e a) c").bitcast(I32))
         scale_rows = w_scales.rearrange("e a q n -> q (e a) n").bitcast(I32)
         for quad in range(4):
@@ -84,11 +79,13 @@ def tile_moe_pre_lin_silu_kernel(tc, xT, w_words, w_scales, b, gate, offs, pos1,
         nc.sync.dma_start(pos1_sb[:], pos1)
         nc.sync.dma_start(pos2_sb[:], pos2)
 
-        def gather_and_round(g):
-            a, lo, hi = GROUPS[g]
-            planes = stage.tile([P, PACK, hi - lo], F32, name="planes")
+        def room(slots, tag):
+            return keep.tile([P, PACK * slots], F32, name="planes" + tag, tag=tag, align_bytes=64)
+
+        def gather(a, lo, hi, tile, at):
+            planes = tile[:, PACK * at : PACK * (at + hi - lo)].rearrange("p (j c) -> p j c", j=PACK)
             for j in range(PACK):
-                cuts = [lo, FIRST, hi] if (g, j) == (0, 0) else [lo, hi]
+                cuts = HEAD if (a, j) == (0, 0) else [lo, hi]
                 for c0, c1 in zip(cuts, cuts[1:]):
                     nc.vector.tensor_tensor(
                         planes[:, j, c0 - lo : c1 - lo],
@@ -96,73 +93,83 @@ def tile_moe_pre_lin_silu_kernel(tc, xT, w_words, w_scales, b, gate, offs, pos1,
                         gate_sb[:, c0:c1],
                         MULT,
                     )
-            pieces = []
-            c1 = lo
-            while c1 < hi:
-                c0 = c1
-                c1 = c0 + max(w for w in QUANT if c0 + w <= hi)
-                rounded = keep.tile([P, c1 - c0, PACK], BF16, name="rounded%d_%d" % (g, c0), align_bytes=64)
+            return planes
+
+        def round_slots(planes, base, lo, widths, tag):
+            rounded = keep.tile([P, sum(widths) * PACK], BF16, name="rounded" + tag, tag=tag, align_bytes=64)
+            at = 0
+            for w in widths:
                 nc.scalar.copy(
-                    out=rounded[:].rearrange("p (c i) j -> p c j i", i=4),
-                    in_=planes[:, :, c0 - lo : c1 - lo].rearrange("p j (c i) -> p c j i", i=4),
+                    out=rounded[:, at * PACK : (at + w) * PACK].rearrange("p (c i j) -> p c j i", i=4, j=PACK),
+                    in_=planes[:, :, lo - base + at : lo - base + at + w].rearrange("p j (c i) -> p c j i", i=4),
                 )
-                pieces.append((a, c0, c1, rounded))
-            return pieces
+                at = at + w
+            return rounded
 
-        def quantize(pieces):
-            for a, c0, c1, rounded in pieces:
+        def quantize(a, rounded, lo, widths):
+            at = 0
+            for w in widths:
                 nc.vector.quantize_mx(
-                    out=codes[a][:, c0:c1].bitcast(FP8X4),
-                    scales=scales[a][:, c0:c1],
-                    in_=rounded[:].rearrange("p c j -> p (c j)"),
+                    out=codes[a][:, lo + at : lo + at + w].bitcast(FP8X4),
+                    scales=scales[a][:, lo + at : lo + at + w],
+                    in_=rounded[:, at * PACK : (at + w) * PACK],
                 )
+                at = at + w
 
-        def multiply(c0):
-            e = c0 // C
-            cols = slice(c0, c0 + UNIT)
-            acc = psum.tile([P, UNIT], F32, name="acc")
-            for a in range(PASSES):
-                nc.tensor.matmul_mx(
-                    out=acc[:],
-                    lhsT=w_sb[:, e * PASSES + a, :].bitcast(FP4X4),
-                    lhsT_scale=ws_sb[:, e * PASSES + a, :],
-                    rhs=codes[a][:, cols].bitcast(FP8X4),
-                    rhs_scale=scales[a][:, cols],
-                    start=(a == 0),
-                    stop=(a == PASSES - 1),
-                )
-            nc.scalar.activation(out=y_sb[:, cols], in_=acc[:], func=SILU, bias=b_sb[:, e : e + 1])
+        def multiply(lo, hi):
+            e = lo // C
+            acc = psum.tile([P, C], F32, name="acc")
+            for u in range(lo, hi, UNIT):
+                for a in range(PASSES):
+                    nc.tensor.matmul_mx(
+                        out=acc[:, u - lo : u - lo + UNIT],
+                        lhsT=w_sb[:, e * PASSES + a, :].bitcast(FP4X4),
+                        lhsT_scale=ws_sb[:, e * PASSES + a, :],
+                        rhs=codes[a][:, u : u + UNIT].bitcast(FP8X4),
+                        rhs_scale=scales[a][:, u : u + UNIT],
+                        start=(a == 0),
+                        stop=(a == PASSES - 1),
+                    )
+            nc.scalar.activation(out=y_sb[:, lo:hi], in_=acc[:, 0 : hi - lo], func=SILU, bias=b_sb[:, e : e + 1])
 
-        def finish(pieces):
-            quantize(pieces)
-            for a, c0, c1, rounded in pieces:
-                if a == PASSES - 1:
-                    for u in range(c0, c1, UNIT):
-                        multiply(u)
+        def finish(g, rounded):
+            lo, hi, widths = GROUPS[g]
+            quantize(1, rounded, lo, widths)
+            while lo < hi:
+                end = min(hi, (lo // C + 1) * C)
+                multiply(lo, end)
+                lo = end
 
-        waiting = []
-        for g in range(len(GROUPS)):
-            fresh = gather_and_round(g)
-            finish(waiting)
-            waiting = fresh
-        finish(waiting)
+        planes0 = gather(0, 0, S, room(S, "planes0"), 0)
+        early = round_slots(planes0, 0, 0, (1024, 1024), "hold1")
+        late = round_slots(planes0, 0, 2048, (512,), "late")
+        last = len(GROUPS) - 1
+        done = []
+        for g, (lo, hi, widths) in enumerate(GROUPS):
+            if g < last - 1:
+                planes = gather(1, lo, hi, room(hi - lo, "hold%d" % g), 0)
+            elif g < last:
+                shared = room(C + UNIT, "hold%d" % g)
+                planes = gather(1, lo, hi, shared, 0)
+            else:
+                planes = gather(1, lo, hi, shared, C)
+            done.append(round_slots(planes, lo, lo, widths, "hold%d" % (g + 2)))
+            if g == 0:
+                quantize(0, early, 0, (1024, 1024))
+            if g == 1:
+                quantize(0, late, 2048, (512,))
+            if 0 < g < last - 1:
+                finish(g - 1, done[g - 1])
+        for g in range(last - 2, last + 1):
+            finish(g, done[g])
 
-        first = keep.tile([P, T], F32, name="first")
-        second = keep.tile([P, T], F32, name="second")
-
-        def fetch(dst, lst, lo, hi):
-            nc.vector.tensor_copy(dst[:, lo:hi], y_sb[:].indirect(lst[:, lo // LIST : hi // LIST]))
-
-        def combine(engine, lo, hi):
+        first = [keep.tile([P, hi - lo], F32, name="first%d" % lo) for lo, hi in FETCH]
+        for tile, (lo, hi) in zip(first, FETCH):
+            nc.vector.tensor_copy(tile[:], y_sb[:].indirect(pos1_sb[:, lo // LIST : hi // LIST]))
+        for piece, lo, hi in COMBINE:
+            base = FETCH[piece][0]
             total = keep.tile([P, hi - lo], F32, name="total%d" % lo)
-            engine.tensor_tensor(total[:], first[:, lo:hi], second[:, lo:hi], ADD)
+            nc.vector.tensor_tensor(
+                total[:], y_sb[:].indirect(pos2_sb[:, lo // LIST : hi // LIST]), first[piece][:, lo - base : hi - base], ADD
+            )
             nc.sync.dma_start(out=out[:, lo:hi], in_=total[:])
-
-        fetch(first, pos1_sb, 0, 640)
-        fetch(second, pos2_sb, *COMBINE[0])
-        fetch(first, pos1_sb, 640, T)
-        combine(nc.gpsimd, *COMBINE[0])
-        fetch(second, pos2_sb, *COMBINE[1])
-        fetch(second, pos2_sb, *COMBINE[2])
-        combine(nc.gpsimd, *COMBINE[1])
-        combine(nc.vector, *COMBINE[2])

@@ -27,8 +27,8 @@ UNIT = 128
 WIDE = S + 32
 HEAD = [0, 256, 1024, S]
 GROUPS = [
-    (0, 1024, (1024,)),
-    (1024, 1792, (512, 256)),
+    (0, 1280, (1024, 256)),
+    (1280, 1792, (512,)),
     (1792, 2176, (256, 128)),
     (2304, 2560, (256,)),
     (2176, 2304, (128,)),
@@ -47,7 +47,7 @@ def tile_moe_pre_lin_silu_kernel(tc, xT, w_words, w_scales, b, gate, offs, pos1,
         pos1_sb = keep.tile([P, T // LIST], U16, name="pos1_sb")
         pos2_sb = keep.tile([P, T // LIST], U16, name="pos2_sb")
         gate_sb = keep.tile([P, S], F32, name="gate_sb")
-        x_sb = [keep.tile([P, WIDE if r < PACK else T], F32, name="x%d" % r) for r in range(PASSES * PACK)]
+        x_sb = [keep.tile([P, WIDE if r < PACK else T + 32], F32, name="x%d" % r) for r in range(PASSES * PACK)]
         w_sb = keep.tile([P, E * PASSES, 2 * N], U8, name="w_sb", align_bytes=64)
         ws_sb = keep.tile([P, E * PASSES, N], U8, name="ws_sb", align_bytes=64)
         b_sb = keep.tile([P, E], F32, name="b_sb")
@@ -119,16 +119,16 @@ def tile_moe_pre_lin_silu_kernel(tc, xT, w_words, w_scales, b, gate, offs, pos1,
         def multiply(lo, hi):
             e = lo // C
             acc = psum.tile([P, C], F32, name="acc")
-            for u in range(lo, hi, UNIT):
-                for a in range(PASSES):
+            for a in range(PASSES):
+                for u in range(lo, hi, UNIT):
                     nc.tensor.matmul_mx(
                         out=acc[:, u - lo : u - lo + UNIT],
                         lhsT=w_sb[:, e * PASSES + a, :].bitcast(FP4X4),
                         lhsT_scale=ws_sb[:, e * PASSES + a, :],
                         rhs=codes[a][:, u : u + UNIT].bitcast(FP8X4),
                         rhs_scale=scales[a][:, u : u + UNIT],
-                        start=(a == 0),
-                        stop=(a == PASSES - 1),
+                        start=(a == 0 and u == lo),
+                        stop=(a == PASSES - 1 and u + UNIT == hi),
                     )
             nc.scalar.activation(out=y_sb[:, lo:hi], in_=acc[:, 0 : hi - lo], func=SILU, bias=b_sb[:, e : e + 1])
 
@@ -140,24 +140,22 @@ def tile_moe_pre_lin_silu_kernel(tc, xT, w_words, w_scales, b, gate, offs, pos1,
                 multiply(lo, end)
                 lo = end
 
-        planes0 = gather(0, 0, S, room(S, "planes0"), 0)
-        early = round_slots(planes0, 0, 0, (1024, 1024), "hold1")
-        late = round_slots(planes0, 0, 2048, (512,), "late")
+        planes0 = gather(0, 0, S, room(S, "odd"), 0)
+        rounded0 = round_slots(planes0, 0, 0, (1024, 1024, 512), "rounded0")
         last = len(GROUPS) - 1
         done = []
         for g, (lo, hi, widths) in enumerate(GROUPS):
+            tag = "odd" if g % 2 else "even"
             if g < last - 1:
-                planes = gather(1, lo, hi, room(hi - lo, "hold%d" % g), 0)
+                planes = gather(1, lo, hi, room(hi - lo, tag), 0)
             elif g < last:
-                shared = room(C + UNIT, "hold%d" % g)
+                shared = room(C + UNIT, tag)
                 planes = gather(1, lo, hi, shared, 0)
             else:
                 planes = gather(1, lo, hi, shared, C)
-            done.append(round_slots(planes, lo, lo, widths, "hold%d" % (g + 2)))
+            done.append(round_slots(planes, lo, lo, widths, "rounded1_%d" % g))
             if g == 0:
-                quantize(0, early, 0, (1024, 1024))
-            if g == 1:
-                quantize(0, late, 2048, (512,))
+                quantize(0, rounded0, 0, (1024, 1024, 512))
             if 0 < g < last - 1:
                 finish(g - 1, done[g - 1])
         for g in range(last - 2, last + 1):

@@ -1,6 +1,7 @@
 from contextlib import ExitStack
 
 import concourse.mybir as mybir
+from concourse.masks import make_identity
 
 K, T, E, C, N = 1024, 1280, 10, 256, 128
 S = E * C
@@ -17,6 +18,7 @@ FP8X4 = mybir.dt.float8_e4m3fn_x4
 FP4X4 = mybir.dt.float4_e2m1fn_x4
 MULT = mybir.AluOpType.mult
 ADD = mybir.AluOpType.add
+COPY = mybir.ActivationFunctionType.Copy
 SILU = mybir.ActivationFunctionType.Silu
 
 P = 128
@@ -25,7 +27,8 @@ PASSES = K // (P * PACK)
 LIST = 16
 UNIT = 128
 WIDE = S + 32
-HEAD = [0, 256, 1024, S]
+BARE = 1024
+BANK = 512
 GROUPS = [
     (0, 1280, (1024, 256)),
     (1280, 1792, (512,)),
@@ -67,9 +70,10 @@ def tile_moe_pre_lin_silu_kernel(tc, xT, w_words, w_scales, b, gate, offs, pos1,
 
         load_x(0)
         nc.sync.dma_start(offs_sb[:], offs)
-        for lo, hi in zip(HEAD, HEAD[1:]):
-            load_gate(lo, hi)
-        for r in range(1, PASSES * PACK):
+        load_gate(BARE, S)
+        load_x(1)
+        load_gate(0, BARE)
+        for r in range(2, PASSES * PACK):
             load_x(r)
         nc.sync.dma_start(out=w_sb[:].bitcast(I32), in_=w_words.rearrange("e a p c -> p (e a) c").bitcast(I32))
         scale_rows = w_scales.rearrange("e a q n -> q (e a) n").bitcast(I32)
@@ -79,20 +83,45 @@ def tile_moe_pre_lin_silu_kernel(tc, xT, w_words, w_scales, b, gate, offs, pos1,
         nc.sync.dma_start(pos1_sb[:], pos1)
         nc.sync.dma_start(pos2_sb[:], pos2)
 
+        identity = keep.tile([P, P], F32, name="identity")
+        make_identity(nc, identity[:])
+        bare = keep.tile([P, BARE], F32, name="bare")
+        turned = keep.tile([P, BARE], F32, name="turned")
+        gate_col = keep.tile([P, BARE // P], F32, name="gate_col")
+
+        def turn(source, lo):
+            bank = psum.tile([P, BANK], F32, name="acc")
+            for u in range(0, BANK, P):
+                nc.tensor.transpose(bank[:, u : u + P], source[:, lo + u : lo + u + P], identity[:])
+            return bank
+
+        def gate_bare(plane):
+            for lo in range(0, BARE, BANK):
+                nc.scalar.copy(out=gate_col[:, lo // P : (lo + BANK) // P], in_=turn(gate_sb, lo)[:, 0:BANK:P])
+            for lo in range(0, BARE, BANK):
+                bank = turn(bare, lo)
+                for u in range(0, BANK, P):
+                    m = (lo + u) // P
+                    nc.scalar.activation(out=turned[:, lo + u : lo + u + P], in_=bank[:, u : u + P], func=COPY, scale=gate_col[:, m : m + 1])
+            for lo in range(0, BARE, BANK):
+                nc.scalar.copy(out=plane[:, lo : lo + BANK], in_=turn(turned, lo)[:])
+
         def room(slots, tag):
             return keep.tile([P, PACK * slots], F32, name="planes" + tag, tag=tag, align_bytes=64)
 
         def gather(a, lo, hi, tile, at):
             planes = tile[:, PACK * at : PACK * (at + hi - lo)].rearrange("p (j c) -> p j c", j=PACK)
             for j in range(PACK):
-                cuts = HEAD if (a, j) == (0, 0) else [lo, hi]
-                for c0, c1 in zip(cuts, cuts[1:]):
-                    nc.vector.tensor_tensor(
-                        planes[:, j, c0 - lo : c1 - lo],
-                        x_sb[a * PACK + j][:].indirect(offs_sb[:, c0 // LIST : c1 // LIST]),
-                        gate_sb[:, c0:c1],
-                        MULT,
-                    )
+                c0 = lo
+                if (a, j) == (0, 0):
+                    nc.vector.tensor_copy(bare[:], x_sb[0][:].indirect(offs_sb[:, 0 : BARE // LIST]))
+                    c0 = BARE
+                nc.vector.tensor_tensor(
+                    planes[:, j, c0 - lo : hi - lo],
+                    x_sb[a * PACK + j][:].indirect(offs_sb[:, c0 // LIST : hi // LIST]),
+                    gate_sb[:, c0:hi],
+                    MULT,
+                )
             return planes
 
         def round_slots(planes, base, lo, widths, tag):
@@ -118,7 +147,7 @@ def tile_moe_pre_lin_silu_kernel(tc, xT, w_words, w_scales, b, gate, offs, pos1,
 
         def multiply(lo, hi):
             e = lo // C
-            acc = psum.tile([P, C], F32, name="acc")
+            acc = psum.tile([P, BANK], F32, name="acc")
             for a in range(PASSES):
                 for u in range(lo, hi, UNIT):
                     nc.tensor.matmul_mx(
@@ -141,6 +170,7 @@ def tile_moe_pre_lin_silu_kernel(tc, xT, w_words, w_scales, b, gate, offs, pos1,
                 lo = end
 
         planes0 = gather(0, 0, S, room(S, "odd"), 0)
+        gate_bare(planes0[:, 0, :])
         rounded0 = round_slots(planes0, 0, 0, (1024, 1024, 512), "rounded0")
         last = len(GROUPS) - 1
         done = []

@@ -26,18 +26,12 @@ PACK = 4
 PASSES = K // (P * PACK)
 LIST = 16
 UNIT = 128
-WIDE = S + 32
-BARE = 1024
 BANK = 512
-GROUPS = [
-    (0, 1280, (1024, 256)),
-    (1280, 1792, (512,)),
-    (1792, 2176, (256, 128)),
-    (2304, 2560, (256,)),
-    (2176, 2304, (128,)),
-]
-FETCH = [(0, 704), (704, 1280)]
-COMBINE = [(0, 0, 704), (1, 704, 1088), (1, 1088, 1280)]
+SPARE = 32
+BARE = 1024
+GROUPS = [(0, (1024, 256)), (1280, (512,)), (1792, (256, 128)), (2304, (256,)), (2176, (128,))]
+FETCH = [0, 704, T]
+COMBINE = [0, 704, 1088, T]
 
 
 def tile_moe_pre_lin_silu_kernel(tc, xT, w_words, w_scales, b, gate, offs, pos1, pos2, out):
@@ -50,13 +44,17 @@ def tile_moe_pre_lin_silu_kernel(tc, xT, w_words, w_scales, b, gate, offs, pos1,
         pos1_sb = keep.tile([P, T // LIST], U16, name="pos1_sb")
         pos2_sb = keep.tile([P, T // LIST], U16, name="pos2_sb")
         gate_sb = keep.tile([P, S], F32, name="gate_sb")
-        x_sb = [keep.tile([P, WIDE if r < PACK else T + 32], F32, name="x%d" % r) for r in range(PASSES * PACK)]
+        x_sb = [keep.tile([P, n + SPARE], F32, name="x%d" % r, align_bytes=64) for r, n in enumerate([S] * PACK + [T] * PACK)]
         w_sb = keep.tile([P, E * PASSES, 2 * N], U8, name="w_sb", align_bytes=64)
         ws_sb = keep.tile([P, E * PASSES, N], U8, name="ws_sb", align_bytes=64)
         b_sb = keep.tile([P, E], F32, name="b_sb")
-        codes = [keep.tile([P, S], U32, name="codes%d" % a, align_bytes=64) for a in range(PASSES)]
+        rounded = [keep.tile([P, PACK * S], BF16, name="rounded%d" % a, align_bytes=64) for a in range(PASSES)]
         scales = [keep.tile([P, S], U8, name="scales%d" % a, align_bytes=64) for a in range(PASSES)]
         y_sb = keep.tile([P, S], F32, name="y_sb")
+        identity = keep.tile([P, P], F32, name="identity")
+        bare = keep.tile([P, BARE], F32, name="bare")
+        turned = keep.tile([P, BARE], F32, name="turned")
+        gate_col = keep.tile([P, BARE // P], F32, name="gate_col")
 
         x_rows = xT.rearrange("(a p j) t -> a j p t", a=PASSES, j=PACK)
 
@@ -67,6 +65,7 @@ def tile_moe_pre_lin_silu_kernel(tc, xT, w_words, w_scales, b, gate, offs, pos1,
             nc.sync.dma_start(out=gate_sb[:, lo:hi], in_=gate[0:P, lo:hi])
 
         nc.vector.memset(ws_sb[:].bitcast(I32), 0)
+        make_identity(nc, identity[:])
 
         load_x(0)
         nc.sync.dma_start(offs_sb[:], offs)
@@ -83,14 +82,8 @@ def tile_moe_pre_lin_silu_kernel(tc, xT, w_words, w_scales, b, gate, offs, pos1,
         nc.sync.dma_start(pos1_sb[:], pos1)
         nc.sync.dma_start(pos2_sb[:], pos2)
 
-        identity = keep.tile([P, P], F32, name="identity")
-        make_identity(nc, identity[:])
-        bare = keep.tile([P, BARE], F32, name="bare")
-        turned = keep.tile([P, BARE], F32, name="turned")
-        gate_col = keep.tile([P, BARE // P], F32, name="gate_col")
-
         def turn(source, lo):
-            bank = psum.tile([P, BANK], F32, name="acc")
+            bank = psum.tile([P, BANK], F32, name="bank")
             for u in range(0, BANK, P):
                 nc.tensor.transpose(bank[:, u : u + P], source[:, lo + u : lo + u + P], identity[:])
             return bank
@@ -107,97 +100,94 @@ def tile_moe_pre_lin_silu_kernel(tc, xT, w_words, w_scales, b, gate, offs, pos1,
                 nc.scalar.copy(out=plane[:, lo : lo + BANK], in_=turn(turned, lo)[:])
 
         def room(slots, tag):
-            return keep.tile([P, PACK * slots], F32, name="planes" + tag, tag=tag, align_bytes=64)
+            return keep.tile([P, PACK * slots], F32, name="planes_" + tag, tag=tag, align_bytes=64)
 
-        def gather(a, lo, hi, tile, at):
-            planes = tile[:, PACK * at : PACK * (at + hi - lo)].rearrange("p (j c) -> p j c", j=PACK)
+        def planes_in(tile, at, slots):
+            return tile[:, PACK * at : PACK * (at + slots)].rearrange("p (j c) -> p j c", j=PACK)
+
+        def gather_plane(a, j, lo, hi, into):
+            nc.vector.tensor_tensor(into, x_sb[a * PACK + j][:].indirect(offs_sb[:, lo // LIST : hi // LIST]), gate_sb[:, lo:hi], MULT)
+
+        def gather(a, lo, hi, planes):
             for j in range(PACK):
-                c0 = lo
-                if (a, j) == (0, 0):
-                    nc.vector.tensor_copy(bare[:], x_sb[0][:].indirect(offs_sb[:, 0 : BARE // LIST]))
-                    c0 = BARE
-                nc.vector.tensor_tensor(
-                    planes[:, j, c0 - lo : hi - lo],
-                    x_sb[a * PACK + j][:].indirect(offs_sb[:, c0 // LIST : hi // LIST]),
-                    gate_sb[:, c0:hi],
-                    MULT,
-                )
-            return planes
+                gather_plane(a, j, lo, hi, planes[:, j, :])
 
-        def round_slots(planes, base, lo, widths, tag):
-            rounded = keep.tile([P, sum(widths) * PACK], BF16, name="rounded" + tag, tag=tag, align_bytes=64)
+        def round_slots(a, planes, lo, widths):
             at = 0
             for w in widths:
                 nc.scalar.copy(
-                    out=rounded[:, at * PACK : (at + w) * PACK].rearrange("p (c i j) -> p c j i", i=4, j=PACK),
-                    in_=planes[:, :, lo - base + at : lo - base + at + w].rearrange("p j (c i) -> p c j i", i=4),
+                    out=rounded[a][:, (lo + at) * PACK : (lo + at + w) * PACK].rearrange("p (c i j) -> p c j i", i=4, j=PACK),
+                    in_=planes[:, :, at : at + w].rearrange("p j (c i) -> p c j i", i=4),
                 )
                 at = at + w
-            return rounded
 
-        def quantize(a, rounded, lo, widths):
-            at = 0
+        codes = {}
+
+        def quantize(a, lo, widths, tag=None):
             for w in widths:
-                nc.vector.quantize_mx(
-                    out=codes[a][:, lo + at : lo + at + w].bitcast(FP8X4),
-                    scales=scales[a][:, lo + at : lo + at + w],
-                    in_=rounded[:, at * PACK : (at + w) * PACK],
-                )
-                at = at + w
+                words = keep.tile([P, w], U32, name="codes", tag=tag or "codes%d_%d" % (a, lo), align_bytes=64)
+                nc.vector.quantize_mx(out=words[:].bitcast(FP8X4), scales=scales[a][:, lo : lo + w], in_=rounded[a][:, lo * PACK : (lo + w) * PACK])
+                for u in range(0, w, UNIT):
+                    codes[a, lo + u] = words[:, u : u + UNIT].bitcast(FP8X4)
+                lo = lo + w
 
         def multiply(lo, hi):
             e = lo // C
-            acc = psum.tile([P, BANK], F32, name="acc")
+            acc = psum.tile([P, BANK], F32, name="bank")
             for a in range(PASSES):
                 for u in range(lo, hi, UNIT):
                     nc.tensor.matmul_mx(
                         out=acc[:, u - lo : u - lo + UNIT],
                         lhsT=w_sb[:, e * PASSES + a, :].bitcast(FP4X4),
                         lhsT_scale=ws_sb[:, e * PASSES + a, :],
-                        rhs=codes[a][:, u : u + UNIT].bitcast(FP8X4),
+                        rhs=codes[a, u],
                         rhs_scale=scales[a][:, u : u + UNIT],
                         start=(a == 0 and u == lo),
                         stop=(a == PASSES - 1 and u + UNIT == hi),
                     )
             nc.scalar.activation(out=y_sb[:, lo:hi], in_=acc[:, 0 : hi - lo], func=SILU, bias=b_sb[:, e : e + 1])
 
-        def finish(g, rounded):
-            lo, hi, widths = GROUPS[g]
-            quantize(1, rounded, lo, widths)
+        def finish(lo, widths):
+            quantize(1, lo, widths)
+            hi = lo + sum(widths)
             while lo < hi:
                 end = min(hi, (lo // C + 1) * C)
                 multiply(lo, end)
                 lo = end
 
-        planes0 = gather(0, 0, S, room(S, "odd"), 0)
-        gate_bare(planes0[:, 0, :])
-        rounded0 = round_slots(planes0, 0, 0, (1024, 1024, 512), "rounded0")
-        last = len(GROUPS) - 1
-        done = []
-        for g, (lo, hi, widths) in enumerate(GROUPS):
-            tag = "odd" if g % 2 else "even"
-            if g < last - 1:
-                planes = gather(1, lo, hi, room(hi - lo, tag), 0)
-            elif g < last:
-                shared = room(C + UNIT, tag)
-                planes = gather(1, lo, hi, shared, 0)
-            else:
-                planes = gather(1, lo, hi, shared, C)
-            done.append(round_slots(planes, lo, lo, widths, "rounded1_%d" % g))
-            if g == 0:
-                quantize(0, rounded0, 0, (1024, 1024, 512))
-            if 0 < g < last - 1:
-                finish(g - 1, done[g - 1])
-        for g in range(last - 2, last + 1):
-            finish(g, done[g])
+        planes = planes_in(room(S, "odd"), 0, S)
+        nc.vector.tensor_copy(bare[:], x_sb[0][:].indirect(offs_sb[:, 0 : BARE // LIST]))
+        gather_plane(0, 0, BARE, S, planes[:, 0, BARE:S])
+        for j in range(1, PACK):
+            gather_plane(0, j, 0, S, planes[:, j, :])
+        gate_bare(planes[:, 0, :])
+        round_slots(0, planes, 0, (1024, 1024, 512))
 
-        first = [keep.tile([P, hi - lo], F32, name="first%d" % lo) for lo, hi in FETCH]
-        for tile, (lo, hi) in zip(first, FETCH):
-            nc.vector.tensor_copy(tile[:], y_sb[:].indirect(pos1_sb[:, lo // LIST : hi // LIST]))
-        for piece, lo, hi in COMBINE:
-            base = FETCH[piece][0]
-            total = keep.tile([P, hi - lo], F32, name="total%d" % lo)
-            nc.vector.tensor_tensor(
-                total[:], y_sb[:].indirect(pos2_sb[:, lo // LIST : hi // LIST]), first[piece][:, lo - base : hi - base], ADD
-            )
-            nc.sync.dma_start(out=out[:, lo:hi], in_=total[:])
+        def fetch(g, tile, at):
+            lo, widths = GROUPS[g]
+            planes = planes_in(tile, at, sum(widths))
+            gather(1, lo, lo + sum(widths), planes)
+            round_slots(1, planes, lo, widths)
+
+        for g in range(3):
+            fetch(g, room(sum(GROUPS[g][1]), "odd" if g % 2 else "even"), 0)
+            if g == 0:
+                quantize(0, 0, (1024, 1024, UNIT))
+            else:
+                finish(*GROUPS[g - 1])
+        shared = room(C + UNIT, "odd")
+        fetch(3, shared, 0)
+        quantize(0, GROUPS[3][0], GROUPS[3][1], "codes1_%d" % GROUPS[1][0])
+        fetch(4, shared, C)
+        finish(*GROUPS[2])
+        quantize(0, GROUPS[4][0], GROUPS[4][1], "even")
+        finish(*GROUPS[3])
+        finish(*GROUPS[4])
+
+        both = keep.tile([P, 2 * T], F32, name="both", tag="x3", align_bytes=64)
+        for lo, hi in zip(FETCH, FETCH[1:]):
+            nc.vector.tensor_copy(both[:, lo:hi], y_sb[:].indirect(pos1_sb[:, lo // LIST : hi // LIST]))
+        for lo, hi in zip(COMBINE, COMBINE[1:]):
+            total = both[:, T + lo : T + hi]
+            nc.vector.tensor_tensor(total, y_sb[:].indirect(pos2_sb[:, lo // LIST : hi // LIST]), both[:, lo:hi], ADD)
+            nc.sync.dma_start(out=out[:, lo:hi], in_=total)

@@ -1,7 +1,6 @@
 from contextlib import ExitStack
 
 import concourse.mybir as mybir
-from concourse.masks import make_identity
 
 K, T, E, C, N = 1024, 1280, 10, 256, 128
 S = E * C
@@ -25,13 +24,13 @@ P = 128
 PACK = 4
 PASSES = K // (P * PACK)
 LIST = 16
-UNIT = 128
 BANK = 512
 SPARE = 32
-BARE = 1024
-GROUPS = [(0, (1024, 256)), (1280, (512,)), (1792, (256, 128)), (2304, (256,)), (2176, (128,))]
-FETCH = [0, 704, T]
-COMBINE = [0, 704, 1088, T]
+OWN = 1280
+EARLY = 512
+HELP = 256
+GROUPS = [(0, (512, 512)), (1024, (512, 512)), (2048, (256, 256))]
+COMBINE = [0, 128, 384, 704, 1088, T]
 
 
 def tile_moe_pre_lin_silu_kernel(tc, xT, w_words, w_scales, b, gate, offs, pos1, pos2, out):
@@ -44,17 +43,14 @@ def tile_moe_pre_lin_silu_kernel(tc, xT, w_words, w_scales, b, gate, offs, pos1,
         pos1_sb = keep.tile([P, T // LIST], U16, name="pos1_sb")
         pos2_sb = keep.tile([P, T // LIST], U16, name="pos2_sb")
         gate_sb = keep.tile([P, S], F32, name="gate_sb")
-        x_sb = [keep.tile([P, n + SPARE], F32, name="x%d" % r, align_bytes=64) for r, n in enumerate([S] * PACK + [T] * PACK)]
+        x_sb = [keep.tile([P, T + SPARE], F32, name="x%d" % r, align_bytes=64) for r in range(PASSES * PACK)]
         w_sb = keep.tile([P, E * PASSES, 2 * N], U8, name="w_sb", align_bytes=64)
         ws_sb = keep.tile([P, E * PASSES, N], U8, name="ws_sb", align_bytes=64)
         b_sb = keep.tile([P, E], F32, name="b_sb")
         rounded = [keep.tile([P, PACK * S], BF16, name="rounded%d" % a, align_bytes=64) for a in range(PASSES)]
+        codes = [keep.tile([P, S], U32, name="codes%d" % a, align_bytes=64) for a in range(PASSES)]
         scales = [keep.tile([P, S], U8, name="scales%d" % a, align_bytes=64) for a in range(PASSES)]
         y_sb = keep.tile([P, S], F32, name="y_sb")
-        identity = keep.tile([P, P], F32, name="identity")
-        bare = keep.tile([P, BARE], F32, name="bare")
-        turned = keep.tile([P, BARE], F32, name="turned")
-        gate_col = keep.tile([P, BARE // P], F32, name="gate_col")
 
         x_rows = xT.rearrange("(a p j) t -> a j p t", a=PASSES, j=PACK)
 
@@ -65,14 +61,16 @@ def tile_moe_pre_lin_silu_kernel(tc, xT, w_words, w_scales, b, gate, offs, pos1,
             nc.sync.dma_start(out=gate_sb[:, lo:hi], in_=gate[0:P, lo:hi])
 
         nc.vector.memset(ws_sb[:].bitcast(I32), 0)
-        make_identity(nc, identity[:])
 
         load_x(0)
         nc.sync.dma_start(offs_sb[:], offs)
-        load_gate(BARE, S)
+        load_gate(0, EARLY)
         load_x(1)
-        load_gate(0, BARE)
-        for r in range(2, PASSES * PACK):
+        load_gate(EARLY, OWN)
+        load_x(2)
+        load_x(3)
+        load_gate(OWN, S)
+        for r in range(PACK, PASSES * PACK):
             load_x(r)
         nc.sync.dma_start(out=w_sb[:].bitcast(I32), in_=w_words.rearrange("e a p c -> p (e a) c").bitcast(I32))
         scale_rows = w_scales.rearrange("e a q n -> q (e a) n").bitcast(I32)
@@ -82,112 +80,80 @@ def tile_moe_pre_lin_silu_kernel(tc, xT, w_words, w_scales, b, gate, offs, pos1,
         nc.sync.dma_start(pos1_sb[:], pos1)
         nc.sync.dma_start(pos2_sb[:], pos2)
 
-        def turn(source, lo):
-            bank = psum.tile([P, BANK], F32, name="bank")
-            for u in range(0, BANK, P):
-                nc.tensor.transpose(bank[:, u : u + P], source[:, lo + u : lo + u + P], identity[:])
-            return bank
+        def room(slots, name):
+            tile = keep.tile([P, PACK * slots], F32, name=name, align_bytes=64)
+            return tile[:].rearrange("p (j c) -> p j c", j=PACK)
 
-        def gate_bare(plane):
-            for lo in range(0, BARE, BANK):
-                nc.scalar.copy(out=gate_col[:, lo // P : (lo + BANK) // P], in_=turn(gate_sb, lo)[:, 0:BANK:P])
-            for lo in range(0, BARE, BANK):
-                bank = turn(bare, lo)
-                for u in range(0, BANK, P):
-                    m = (lo + u) // P
-                    nc.scalar.activation(out=turned[:, lo + u : lo + u + P], in_=bank[:, u : u + P], func=COPY, scale=gate_col[:, m : m + 1])
-            for lo in range(0, BARE, BANK):
-                nc.scalar.copy(out=plane[:, lo : lo + BANK], in_=turn(turned, lo)[:])
+        def window(r, lo, hi):
+            return x_sb[r][:].indirect(offs_sb[:, lo // LIST : hi // LIST])
 
-        def room(slots, tag):
-            return keep.tile([P, PACK * slots], F32, name="planes_" + tag, tag=tag, align_bytes=64)
+        def woven(a, lo, w):
+            return rounded[a][:, lo * PACK : (lo + w) * PACK].rearrange("p (c i j) -> p c j i", i=4, j=PACK)
 
-        def planes_in(tile, at, slots):
-            return tile[:, PACK * at : PACK * (at + slots)].rearrange("p (j c) -> p j c", j=PACK)
+        def by_four(planes, at, w):
+            return planes[:, :, at : at + w].rearrange("p j (c i) -> p c j i", i=4)
 
-        def gather_plane(a, j, lo, hi, into):
-            nc.vector.tensor_tensor(into, x_sb[a * PACK + j][:].indirect(offs_sb[:, lo // LIST : hi // LIST]), gate_sb[:, lo:hi], MULT)
+        def gate_and_round(a, planes, at, lo, w):
+            weights = gate_sb[:, lo : lo + w].rearrange("p (c i) -> p c i", i=4).unsqueeze(2).to_broadcast([P, w // 4, PACK, 4])
+            nc.vector.tensor_tensor(woven(a, lo, w), by_four(planes, at, w), weights, MULT)
 
-        def gather(a, lo, hi, planes):
-            for j in range(PACK):
-                gather_plane(a, j, lo, hi, planes[:, j, :])
+        def quantize(a, lo, w):
+            nc.vector.quantize_mx(out=codes[a][:, lo : lo + w].bitcast(FP8X4), scales=scales[a][:, lo : lo + w], in_=rounded[a][:, lo * PACK : (lo + w) * PACK])
 
-        def round_slots(a, planes, lo, widths):
-            at = 0
-            for w in widths:
-                nc.scalar.copy(
-                    out=rounded[a][:, (lo + at) * PACK : (lo + at + w) * PACK].rearrange("p (c i j) -> p c j i", i=4, j=PACK),
-                    in_=planes[:, :, at : at + w].rearrange("p j (c i) -> p c j i", i=4),
-                )
-                at = at + w
-
-        codes = {}
-
-        def quantize(a, lo, widths, tag=None):
-            for w in widths:
-                words = keep.tile([P, w], U32, name="codes", tag=tag or "codes%d_%d" % (a, lo), align_bytes=64)
-                nc.vector.quantize_mx(out=words[:].bitcast(FP8X4), scales=scales[a][:, lo : lo + w], in_=rounded[a][:, lo * PACK : (lo + w) * PACK])
-                for u in range(0, w, UNIT):
-                    codes[a, lo + u] = words[:, u : u + UNIT].bitcast(FP8X4)
-                lo = lo + w
-
-        def multiply(lo, hi):
-            e = lo // C
+        def multiply(e):
+            cols = slice(e * C, (e + 1) * C)
             acc = psum.tile([P, BANK], F32, name="bank")
             for a in range(PASSES):
-                for u in range(lo, hi, UNIT):
-                    nc.tensor.matmul_mx(
-                        out=acc[:, u - lo : u - lo + UNIT],
-                        lhsT=w_sb[:, e * PASSES + a, :].bitcast(FP4X4),
-                        lhsT_scale=ws_sb[:, e * PASSES + a, :],
-                        rhs=codes[a, u],
-                        rhs_scale=scales[a][:, u : u + UNIT],
-                        start=(a == 0 and u == lo),
-                        stop=(a == PASSES - 1 and u + UNIT == hi),
-                    )
-            nc.scalar.activation(out=y_sb[:, lo:hi], in_=acc[:, 0 : hi - lo], func=SILU, bias=b_sb[:, e : e + 1])
+                nc.tensor.matmul_mx(
+                    out=acc[:, 0:C],
+                    lhsT=w_sb[:, e * PASSES + a, :].bitcast(FP4X4),
+                    lhsT_scale=ws_sb[:, e * PASSES + a, :],
+                    rhs=codes[a][:, cols].bitcast(FP8X4),
+                    rhs_scale=scales[a][:, cols],
+                    start=(a == 0),
+                    stop=(a == PASSES - 1),
+                )
+            nc.scalar.activation(out=y_sb[:, cols], in_=acc[:, 0:C], func=SILU, bias=b_sb[:, e : e + 1])
 
-        def finish(lo, widths):
-            quantize(1, lo, widths)
-            hi = lo + sum(widths)
-            while lo < hi:
-                end = min(hi, (lo // C + 1) * C)
-                multiply(lo, end)
-                lo = end
-
-        planes = planes_in(room(S, "odd"), 0, S)
-        nc.vector.tensor_copy(bare[:], x_sb[0][:].indirect(offs_sb[:, 0 : BARE // LIST]))
-        gather_plane(0, 0, BARE, S, planes[:, 0, BARE:S])
+        gated = room(OWN, "gated")
+        bare = room(S - OWN, "bare")
+        nc.vector.tensor_copy(bare[:, 0, 0:HELP], window(0, OWN, OWN + HELP))
+        nc.scalar.activation(bare[:, 0, HELP:], window(0, OWN + HELP, S), COPY)
         for j in range(1, PACK):
-            gather_plane(0, j, 0, S, planes[:, j, :])
-        gate_bare(planes[:, 0, :])
-        round_slots(0, planes, 0, (1024, 1024, 512))
+            nc.scalar.activation(bare[:, j, :], window(j, OWN, S), COPY)
+        for j, lo, hi in [(0, 0, EARLY), (1, 0, EARLY), (0, EARLY, OWN), (1, EARLY, OWN), (2, 0, OWN), (3, 0, OWN)]:
+            nc.vector.tensor_tensor(gated[:, j, lo:hi], window(j, lo, hi), gate_sb[:, lo:hi], MULT)
 
-        def fetch(g, tile, at):
-            lo, widths = GROUPS[g]
-            planes = planes_in(tile, at, sum(widths))
-            gather(1, lo, lo + sum(widths), planes)
-            round_slots(1, planes, lo, widths)
+        later = []
+        for lo, widths in GROUPS:
+            planes = room(sum(widths), "planes%d" % lo)
+            for j in range(PACK):
+                nc.scalar.activation(planes[:, j, :], window(PACK + j, lo, lo + sum(widths)), COPY)
+            at = 0
+            for w in widths:
+                later.append((planes, at, lo + at, w))
+                at = at + w
 
-        for g in range(3):
-            fetch(g, room(sum(GROUPS[g][1]), "odd" if g % 2 else "even"), 0)
-            if g == 0:
-                quantize(0, 0, (1024, 1024, UNIT))
-            else:
-                finish(*GROUPS[g - 1])
-        shared = room(C + UNIT, "odd")
-        fetch(3, shared, 0)
-        quantize(0, GROUPS[3][0], GROUPS[3][1], "codes1_%d" % GROUPS[1][0])
-        fetch(4, shared, C)
-        finish(*GROUPS[2])
-        quantize(0, GROUPS[4][0], GROUPS[4][1], "even")
-        finish(*GROUPS[3])
-        finish(*GROUPS[4])
+        nc.vector.tensor_copy(woven(0, 0, 1024), by_four(gated, 0, 1024))
+        nc.vector.tensor_copy(woven(0, 1024, 256), by_four(gated, 1024, 256))
+        quantize(0, 0, 1024)
+        gate_and_round(0, bare, 0, OWN, 768)
+        gate_and_round(0, bare, 768, OWN + 768, 512)
+        quantize(0, 1024, 1024)
+        waiting = (0, 2048, 512)
+        for planes, at, lo, w in later:
+            gate_and_round(1, planes, at, lo, w)
+            quantize(*waiting)
+            if waiting[0] == 1:
+                for e in range(waiting[1] // C, (waiting[1] + waiting[2]) // C):
+                    multiply(e)
+            waiting = (1, lo, w)
+        quantize(*waiting)
+        multiply(E - 1)
 
-        both = keep.tile([P, 2 * T], F32, name="both", tag="x3", align_bytes=64)
-        for lo, hi in zip(FETCH, FETCH[1:]):
-            nc.vector.tensor_copy(both[:, lo:hi], y_sb[:].indirect(pos1_sb[:, lo // LIST : hi // LIST]))
+        first = keep.tile([P, T], F32, name="first", tag="x0", align_bytes=64)
+        total = keep.tile([P, T], F32, name="total", tag="x1", align_bytes=64)
         for lo, hi in zip(COMBINE, COMBINE[1:]):
-            total = both[:, T + lo : T + hi]
-            nc.vector.tensor_tensor(total, y_sb[:].indirect(pos2_sb[:, lo // LIST : hi // LIST]), both[:, lo:hi], ADD)
-            nc.sync.dma_start(out=out[:, lo:hi], in_=total)
+            nc.scalar.activation(first[:, lo:hi], y_sb[:].indirect(pos1_sb[:, lo // LIST : hi // LIST]), COPY)
+            nc.vector.tensor_tensor(total[:, lo:hi], y_sb[:].indirect(pos2_sb[:, lo // LIST : hi // LIST]), first[:, lo:hi], ADD)
+            nc.sync.dma_start(out=out[:, lo:hi], in_=total[:, lo:hi])

@@ -61,6 +61,9 @@ def tile_moe_pre_lin_silu_kernel(tc, xT, w_words, w_scales, b, gate, offs, pos1,
             nc.sync.dma_start(out=gate_sb[:, lo:hi], in_=gate[0:P, lo:hi])
 
         nc.vector.memset(ws_sb[:].bitcast(I32), 0)
+        warm = keep.tile([P, 2], F32, name="warm")
+        nc.vector.memset(warm[:, 0:1], 0.0)
+        nc.scalar.activation(out=warm[:, 1:2], in_=warm[:, 0:1], func=SILU)
 
         load_x(0)
         nc.sync.dma_start(offs_sb[:], offs)

@@ -25,12 +25,13 @@ PACK = 4
 PASSES = K // (P * PACK)
 LIST = 16
 BANK = 512
-SPARE = 32
-OWN = 1280
+SPARE = 160
+OWN = 1152
 EARLY = 512
 HELP = 256
-GROUPS = [(0, (512, 512)), (1024, (512, 512)), (2048, (256, 256))]
-COMBINE = [0, 128, 384, 704, 1088, T]
+GROUPS = [(0, (1024,)), (1024, (512, 256)), (1792, (256, 256)), (2304, (128, 128))]
+ALONE = 160
+COMBINE = [0, ALONE, 480, 800, 1120, T]
 
 
 def tile_moe_pre_lin_silu_kernel(tc, xT, w_words, w_scales, b, gate, offs, pos1, pos2, out):
@@ -83,8 +84,8 @@ def tile_moe_pre_lin_silu_kernel(tc, xT, w_words, w_scales, b, gate, offs, pos1,
         nc.sync.dma_start(pos1_sb[:], pos1)
         nc.sync.dma_start(pos2_sb[:], pos2)
 
-        def room(slots, name):
-            tile = keep.tile([P, PACK * slots], F32, name=name, align_bytes=64)
+        def room(slots, tag):
+            tile = keep.tile([P, PACK * slots], F32, name=tag, tag=tag, align_bytes=64)
             return tile[:].rearrange("p (j c) -> p j c", j=PACK)
 
         def window(r, lo, hi):
@@ -103,20 +104,22 @@ def tile_moe_pre_lin_silu_kernel(tc, xT, w_words, w_scales, b, gate, offs, pos1,
         def quantize(a, lo, w):
             nc.vector.quantize_mx(out=codes[a][:, lo : lo + w].bitcast(FP8X4), scales=scales[a][:, lo : lo + w], in_=rounded[a][:, lo * PACK : (lo + w) * PACK])
 
-        def multiply(e):
-            cols = slice(e * C, (e + 1) * C)
-            acc = psum.tile([P, BANK], F32, name="bank")
-            for a in range(PASSES):
-                nc.tensor.matmul_mx(
-                    out=acc[:, 0:C],
-                    lhsT=w_sb[:, e * PASSES + a, :].bitcast(FP4X4),
-                    lhsT_scale=ws_sb[:, e * PASSES + a, :],
-                    rhs=codes[a][:, cols].bitcast(FP8X4),
-                    rhs_scale=scales[a][:, cols],
-                    start=(a == 0),
-                    stop=(a == PASSES - 1),
-                )
-            nc.scalar.activation(out=y_sb[:, cols], in_=acc[:, 0:C], func=SILU, bias=b_sb[:, e : e + 1])
+        def finish(lo, w):
+            for at in range(lo, lo + w, C):
+                e = at // C
+                cols = slice(at, at + min(w, C))
+                acc = psum.tile([P, BANK], F32, name="bank")
+                for a in range(PASSES):
+                    nc.tensor.matmul_mx(
+                        out=acc[:, 0 : min(w, C)],
+                        lhsT=w_sb[:, e * PASSES + a, :].bitcast(FP4X4),
+                        lhsT_scale=ws_sb[:, e * PASSES + a, :],
+                        rhs=codes[a][:, cols].bitcast(FP8X4),
+                        rhs_scale=scales[a][:, cols],
+                        start=(a == 0),
+                        stop=(a == PASSES - 1),
+                    )
+                nc.scalar.activation(out=y_sb[:, cols], in_=acc[:, 0 : min(w, C)], func=SILU, bias=b_sb[:, e : e + 1])
 
         gated = room(OWN, "gated")
         bare = room(S - OWN, "bare")
@@ -127,36 +130,41 @@ def tile_moe_pre_lin_silu_kernel(tc, xT, w_words, w_scales, b, gate, offs, pos1,
         for j, lo, hi in [(0, 0, EARLY), (1, 0, EARLY), (0, EARLY, OWN), (1, EARLY, OWN), (2, 0, OWN), (3, 0, OWN)]:
             nc.vector.tensor_tensor(gated[:, j, lo:hi], window(j, lo, hi), gate_sb[:, lo:hi], MULT)
 
-        later = []
-        for lo, widths in GROUPS:
-            planes = room(sum(widths), "planes%d" % lo)
+        def fetch(g):
+            lo, widths = GROUPS[g]
+            planes = room(sum(widths), "bare" if g % 2 else "other")
             for j in range(PACK):
                 nc.scalar.activation(planes[:, j, :], window(PACK + j, lo, lo + sum(widths)), COPY)
-            at = 0
-            for w in widths:
-                later.append((planes, at, lo + at, w))
-                at = at + w
+            return planes
 
-        nc.vector.tensor_copy(woven(0, 0, 1024), by_four(gated, 0, 1024))
-        nc.vector.tensor_copy(woven(0, 1024, 256), by_four(gated, 1024, 256))
+        ahead = fetch(0)
+        nc.vector.tensor_copy(woven(0, 0, OWN), by_four(gated, 0, OWN))
+        gate_and_round(0, bare, 0, OWN, S - OWN)
         quantize(0, 0, 1024)
-        gate_and_round(0, bare, 0, OWN, 768)
-        gate_and_round(0, bare, 768, OWN + 768, 512)
         quantize(0, 1024, 1024)
         waiting = (0, 2048, 512)
-        for planes, at, lo, w in later:
-            gate_and_round(1, planes, at, lo, w)
-            quantize(*waiting)
-            if waiting[0] == 1:
-                for e in range(waiting[1] // C, (waiting[1] + waiting[2]) // C):
-                    multiply(e)
-            waiting = (1, lo, w)
+        for g, (lo, widths) in enumerate(GROUPS):
+            planes = ahead
+            if g + 1 < len(GROUPS):
+                ahead = fetch(g + 1)
+            at = 0
+            for w in widths:
+                gate_and_round(1, planes, at, lo + at, w)
+                quantize(*waiting)
+                if waiting[0] == 1:
+                    finish(*waiting[1:])
+                waiting = (1, lo + at, w)
+                at = at + w
         quantize(*waiting)
-        multiply(E - 1)
+        finish(*waiting[1:])
 
         first = keep.tile([P, T], F32, name="first", tag="x0", align_bytes=64)
         total = keep.tile([P, T], F32, name="total", tag="x1", align_bytes=64)
         for lo, hi in zip(COMBINE, COMBINE[1:]):
-            nc.scalar.activation(first[:, lo:hi], y_sb[:].indirect(pos1_sb[:, lo // LIST : hi // LIST]), COPY)
+            fetched = y_sb[:].indirect(pos1_sb[:, lo // LIST : hi // LIST])
+            if hi == ALONE:
+                nc.vector.tensor_copy(first[:, lo:hi], fetched)
+            else:
+                nc.scalar.activation(first[:, lo:hi], fetched, COPY)
             nc.vector.tensor_tensor(total[:, lo:hi], y_sb[:].indirect(pos2_sb[:, lo // LIST : hi // LIST]), first[:, lo:hi], ADD)
             nc.sync.dma_start(out=out[:, lo:hi], in_=total[:, lo:hi])

@@ -1,6 +1,7 @@
 from contextlib import ExitStack
 
 import concourse.mybir as mybir
+from concourse.masks import make_identity
 
 K, T, E, C, N = 1024, 1280, 10, 256, 128
 S = E * C
@@ -25,11 +26,8 @@ PACK = 4
 PASSES = K // (P * PACK)
 LIST = 16
 BANK = 512
-SPARE = 160
-OWN = 1152
-EARLY = 512
-HELP = 256
-GROUPS = [(0, (1024,)), (1024, (512, 256)), (1792, (256, 256)), (2304, (128, 128))]
+CHUNK = 512
+SIDE = 1024
 ALONE = 160
 COMBINE = [0, ALONE, 480, 800, 1120, T]
 
@@ -38,43 +36,47 @@ def tile_moe_pre_lin_silu_kernel(tc, xT, w_words, w_scales, b, gate, offs, pos1,
     nc = tc.nc
     with ExitStack() as ctx:
         keep = ctx.enter_context(tc.tile_pool(name="keep", bufs=1))
-        psum = ctx.enter_context(tc.psum_pool(name="psum", bufs=8))
+        held = ctx.enter_context(tc.psum_pool(name="held", bufs=1))
+        psum = ctx.enter_context(tc.psum_pool(name="psum", bufs=5))
 
         offs_sb = keep.tile([P, S // LIST], U16, name="offs_sb")
         pos1_sb = keep.tile([P, T // LIST], U16, name="pos1_sb")
         pos2_sb = keep.tile([P, T // LIST], U16, name="pos2_sb")
-        gate_sb = keep.tile([P, S], F32, name="gate_sb")
-        x_sb = [keep.tile([P, T + SPARE], F32, name="x%d" % r, align_bytes=64) for r in range(PASSES * PACK)]
+        gate_sb = keep.tile([P, SIDE], F32, name="gate_sb")
+        gate_rows = keep.tile([P, P], F32, name="gate_rows", tag="odd", align_bytes=64)
+        gate_col = keep.tile([P, (S - SIDE) // P], F32, name="gate_col")
+        gate_ps = [held.tile([P, BANK], F32, name="gate_ps%d" % m) for m in range((S - SIDE) // BANK)]
+        identity = keep.tile([P, P], F32, name="identity")
+        x_sb = [keep.tile([P, T], F32, name="x%d" % r, align_bytes=64) for r in range(PASSES * PACK)]
         w_sb = keep.tile([P, E * PASSES, 2 * N], U8, name="w_sb", align_bytes=64)
         ws_sb = keep.tile([P, E * PASSES, N], U8, name="ws_sb", align_bytes=64)
         b_sb = keep.tile([P, E], F32, name="b_sb")
-        rounded = [keep.tile([P, PACK * S], BF16, name="rounded%d" % a, align_bytes=64) for a in range(PASSES)]
-        codes = [keep.tile([P, S], U32, name="codes%d" % a, align_bytes=64) for a in range(PASSES)]
-        scales = [keep.tile([P, S], U8, name="scales%d" % a, align_bytes=64) for a in range(PASSES)]
         y_sb = keep.tile([P, S], F32, name="y_sb")
 
         x_rows = xT.rearrange("(a p j) t -> a j p t", a=PASSES, j=PACK)
 
         def load_x(r):
-            nc.sync.dma_start(out=x_sb[r][:, 0:T], in_=x_rows[r // PACK, r % PACK])
+            nc.sync.dma_start(out=x_sb[r][:], in_=x_rows[r // PACK, r % PACK])
 
         def load_gate(lo, hi):
             nc.sync.dma_start(out=gate_sb[:, lo:hi], in_=gate[0:P, lo:hi])
 
+        nc.vector.memset(gate_rows[:], 0.0)
         nc.vector.memset(ws_sb[:].bitcast(I32), 0)
         warm = keep.tile([P, 2], F32, name="warm")
         nc.vector.memset(warm[:, 0:1], 0.0)
         nc.scalar.activation(out=warm[:, 1:2], in_=warm[:, 0:1], func=SILU)
+        make_identity(nc, identity[:])
 
         load_x(0)
         nc.sync.dma_start(offs_sb[:], offs)
-        load_gate(0, EARLY)
-        load_x(1)
-        load_gate(EARLY, OWN)
-        load_x(2)
-        load_x(3)
-        load_gate(OWN, S)
-        for r in range(PACK, PASSES * PACK):
+        for r in range(1, PACK):
+            load_x(r)
+        nc.sync.dma_start(out=gate_rows[0 : (S - SIDE) // P, :], in_=gate[0, SIDE:S].rearrange("(m c) -> m c", c=P))
+        load_gate(0, CHUNK)
+        load_x(PACK)
+        load_gate(CHUNK, SIDE)
+        for r in range(PACK + 1, PASSES * PACK):
             load_x(r)
         nc.sync.dma_start(out=w_sb[:].bitcast(I32), in_=w_words.rearrange("e a p c -> p (e a) c").bitcast(I32))
         scale_rows = w_scales.rearrange("e a q n -> q (e a) n").bitcast(I32)
@@ -88,75 +90,124 @@ def tile_moe_pre_lin_silu_kernel(tc, xT, w_words, w_scales, b, gate, offs, pos1,
             tile = keep.tile([P, PACK * slots], F32, name=tag, tag=tag, align_bytes=64)
             return tile[:].rearrange("p (j c) -> p j c", j=PACK)
 
-        def window(r, lo, hi):
-            return x_sb[r][:].indirect(offs_sb[:, lo // LIST : hi // LIST])
+        def stage(slots):
+            return keep.tile([P, PACK * slots], BF16, name="stage", tag="stage", align_bytes=64)
 
-        def woven(a, lo, w):
-            return rounded[a][:, lo * PACK : (lo + w) * PACK].rearrange("p (c i j) -> p c j i", i=4, j=PACK)
+        def window(a, j, lo, w):
+            return x_sb[a * PACK + j][:].indirect(offs_sb[:, lo // LIST : (lo + w) // LIST])
 
-        def by_four(planes, at, w):
-            return planes[:, :, at : at + w].rearrange("p j (c i) -> p c j i", i=4)
+        def on_scalar(planes, a, js, lo, w):
+            for j in js:
+                nc.scalar.activation(planes[:, j, :], window(a, j, lo, w), COPY)
 
-        def gate_and_round(a, planes, at, lo, w):
-            weights = gate_sb[:, lo : lo + w].rearrange("p (c i) -> p c i", i=4).unsqueeze(2).to_broadcast([P, w // 4, PACK, 4])
-            nc.vector.tensor_tensor(woven(a, lo, w), by_four(planes, at, w), weights, MULT)
+        def on_vector(planes, a, js, lo, w):
+            for j in js:
+                nc.vector.tensor_copy(planes[:, j, :], window(a, j, lo, w))
 
-        def quantize(a, lo, w):
-            nc.vector.quantize_mx(out=codes[a][:, lo : lo + w].bitcast(FP8X4), scales=scales[a][:, lo : lo + w], in_=rounded[a][:, lo * PACK : (lo + w) * PACK])
+        def gate_and_round(engine, into, to, planes, at, weights):
+            w = weights.shape[1]
+            engine.tensor_tensor(
+                into[:, to * PACK : (to + w) * PACK].rearrange("p (c i j) -> p c j i", i=4, j=PACK),
+                planes[:, :, at : at + w].rearrange("p j (c i) -> p c j i", i=4),
+                weights.rearrange("p (c i) -> p c i", i=4).unsqueeze(2).to_broadcast([P, w // 4, PACK, 4]),
+                MULT,
+            )
+
+        def gate_in_psum(lo, w):
+            return gate_ps[(lo - SIDE) // BANK][:, lo % BANK : lo % BANK + w]
+
+        codes = {}
+
+        def quantize(source, at, parts):
+            w = sum(part[2] for part in parts)
+            name = "%d_%d" % parts[0][:2]
+            words = keep.tile([P, w], U32, name="codes" + name, align_bytes=64)
+            scales = keep.tile([P, w], U8, name="scales" + name, align_bytes=64)
+            nc.vector.quantize_mx(out=words[:].bitcast(FP8X4), scales=scales[:], in_=source[:, at * PACK : (at + w) * PACK])
+            to = 0
+            for a, lo, part in parts:
+                for u in range(0, part, P):
+                    codes[a, lo + u] = (words, scales, to + u)
+                to = to + part
 
         def finish(lo, w):
             for at in range(lo, lo + w, C):
                 e = at // C
-                cols = slice(at, at + min(w, C))
+                n = min(w, C)
                 acc = psum.tile([P, BANK], F32, name="bank")
                 for a in range(PASSES):
+                    words, scales, to = codes[a, at]
                     nc.tensor.matmul_mx(
-                        out=acc[:, 0 : min(w, C)],
+                        out=acc[:, 0:n],
                         lhsT=w_sb[:, e * PASSES + a, :].bitcast(FP4X4),
                         lhsT_scale=ws_sb[:, e * PASSES + a, :],
-                        rhs=codes[a][:, cols].bitcast(FP8X4),
-                        rhs_scale=scales[a][:, cols],
+                        rhs=words[:, to : to + n].bitcast(FP8X4),
+                        rhs_scale=scales[:, to : to + n],
                         start=(a == 0),
                         stop=(a == PASSES - 1),
                     )
-                nc.scalar.activation(out=y_sb[:, cols], in_=acc[:, 0 : min(w, C)], func=SILU, bias=b_sb[:, e : e + 1])
+                nc.scalar.activation(out=y_sb[:, at : at + n], in_=acc[:, 0:n], func=SILU, bias=b_sb[:, e : e + 1])
 
-        gated = room(OWN, "gated")
-        bare = room(S - OWN, "bare")
-        nc.vector.tensor_copy(bare[:, 0, 0:HELP], window(0, OWN, OWN + HELP))
-        nc.scalar.activation(bare[:, 0, HELP:], window(0, OWN + HELP, S), COPY)
-        for j in range(1, PACK):
-            nc.scalar.activation(bare[:, j, :], window(j, OWN, S), COPY)
-        for j, lo, hi in [(0, 0, EARLY), (1, 0, EARLY), (0, EARLY, OWN), (1, EARLY, OWN), (2, 0, OWN), (3, 0, OWN)]:
-            nc.vector.tensor_tensor(gated[:, j, lo:hi], window(j, lo, hi), gate_sb[:, lo:hi], MULT)
+        side = room(CHUNK, "even")
+        on_vector(side, 0, range(PACK), 0, CHUNK)
+        main = room(2 * CHUNK, "near")
+        on_scalar(main, 0, range(PACK), SIDE, 2 * CHUNK)
 
-        def fetch(g):
-            lo, widths = GROUPS[g]
-            planes = room(sum(widths), "bare" if g % 2 else "other")
-            for j in range(PACK):
-                nc.scalar.activation(planes[:, j, :], window(PACK + j, lo, lo + sum(widths)), COPY)
+        turned = psum.tile([P, BANK], F32, name="bank")
+        nc.tensor.transpose(turned[:, 0:P], gate_rows[:], identity[:])
+        nc.vector.tensor_copy(gate_col[:], turned[:, 0 : (S - SIDE) // P])
+        for m in range((S - SIDE) // P):
+            nc.tensor.transpose(gate_ps[m // 4][:, m % 4 * P : (m % 4 + 1) * P], gate_col[:, m : m + 1].to_broadcast([P, P]), identity[:])
+
+        def fetch_side(a, lo, tag):
+            planes = room(CHUNK, tag)
+            on_scalar(planes, a, [PACK - 1], lo, CHUNK)
+            on_vector(planes, a, range(PACK - 1), lo, CHUNK)
             return planes
 
-        ahead = fetch(0)
-        nc.vector.tensor_copy(woven(0, 0, OWN), by_four(gated, 0, OWN))
-        gate_and_round(0, bare, 0, OWN, S - OWN)
-        quantize(0, 0, 1024)
-        quantize(0, 1024, 1024)
-        waiting = (0, 2048, 512)
-        for g, (lo, widths) in enumerate(GROUPS):
-            planes = ahead
-            if g + 1 < len(GROUPS):
-                ahead = fetch(g + 1)
-            at = 0
-            for w in widths:
-                gate_and_round(1, planes, at, lo + at, w)
-                quantize(*waiting)
-                if waiting[0] == 1:
-                    finish(*waiting[1:])
-                waiting = (1, lo + at, w)
-                at = at + w
-        quantize(*waiting)
-        finish(*waiting[1:])
+        rounded = stage(2 * CHUNK)
+        gate_and_round(nc.gpsimd, rounded, 0, side, 0, gate_sb[:, 0:CHUNK])
+        side = fetch_side(0, CHUNK, "odd")
+        gate_and_round(nc.vector, rounded, CHUNK, main, 0, gate_in_psum(SIDE, CHUNK))
+        quantize(rounded, 0, [(0, 0, CHUNK), (0, SIDE, CHUNK)])
+
+        rounded = stage(2 * CHUNK)
+        gate_and_round(nc.gpsimd, rounded, 0, side, 0, gate_sb[:, CHUNK:SIDE])
+        side = fetch_side(1, 0, "even")
+        far = room(2 * CHUNK, "far")
+        on_scalar(far, 1, range(PACK), SIDE, 2 * CHUNK)
+        gate_and_round(nc.vector, rounded, CHUNK, main, CHUNK, gate_in_psum(SIDE + CHUNK, CHUNK))
+        quantize(rounded, 0, [(0, CHUNK, CHUNK), (0, SIDE + CHUNK, CHUNK)])
+
+        rounded = stage(2 * CHUNK)
+        gate_and_round(nc.gpsimd, rounded, 0, side, 0, gate_sb[:, 0:CHUNK])
+        side = fetch_side(1, CHUNK, "odd")
+        main = room(CHUNK, "near")
+        on_scalar(main, 0, range(PACK), S - CHUNK, CHUNK)
+        gate_and_round(nc.vector, rounded, CHUNK, far, 0, gate_in_psum(SIDE, CHUNK))
+        quantize(rounded, 0, [(1, 0, CHUNK), (1, SIDE, CHUNK)])
+        finish(0, CHUNK)
+        finish(SIDE, CHUNK)
+
+        rounded = stage(3 * CHUNK)
+        gate_and_round(nc.gpsimd, rounded, 0, side, 0, gate_sb[:, CHUNK:SIDE])
+        gate_and_round(nc.vector, rounded, CHUNK, far, CHUNK, gate_in_psum(SIDE + CHUNK, CHUNK))
+        last = room(CHUNK, "far")
+        on_scalar(last, 1, range(PACK), S - CHUNK, CHUNK)
+        gate_and_round(nc.vector, rounded, 2 * CHUNK, main, 0, gate_in_psum(S - CHUNK, CHUNK))
+        quantize(rounded, 0, [(1, CHUNK, CHUNK), (1, SIDE + CHUNK, CHUNK)])
+        quantize(rounded, 2 * CHUNK, [(0, S - CHUNK, CHUNK)])
+        finish(CHUNK, CHUNK)
+        finish(SIDE + CHUNK, CHUNK)
+
+        rounded = stage(CHUNK)
+        pieces = [(0, C), (C, P), (C + P, P)]
+        for (at, w), before in zip(pieces + [(None, None)], [None] + pieces):
+            if w:
+                gate_and_round(nc.vector, rounded, at, last, at, gate_in_psum(S - CHUNK + at, w))
+            if before:
+                quantize(rounded, before[0], [(1, S - CHUNK + before[0], before[1])])
+                finish(S - CHUNK + before[0], before[1])
 
         first = keep.tile([P, T], F32, name="first", tag="x0", align_bytes=64)
         total = keep.tile([P, T], F32, name="total", tag="x1", align_bytes=64)

@@ -26,40 +26,42 @@ PACK = 4
 PASSES = K // (P * PACK)
 LIST = 16
 BANK = 512
-CHUNK = 512
-SIDE = 1024
+ROUND = 1024
+HALF = ROUND // 2
+POOL = 448
+POOL_LAST = 288
+SHARE = 1120
 ALONE = 160
 COMBINE = [0, ALONE, 480, 800, 1120, T]
+LOW, MID, HIGH = 0, ROUND, ROUND + HALF
+ROW0 = POOL // P
+ROWS = S // P - 2 * ROW0
 
 
 def tile_moe_pre_lin_silu_kernel(tc, xT, w_words, w_scales, b, gate, offs, pos1, pos2, out):
     nc = tc.nc
     with ExitStack() as ctx:
         keep = ctx.enter_context(tc.tile_pool(name="keep", bufs=1))
-        held = ctx.enter_context(tc.psum_pool(name="held", bufs=1))
-        psum = ctx.enter_context(tc.psum_pool(name="psum", bufs=5))
+        psum = ctx.enter_context(tc.psum_pool(name="psum", bufs=1))
 
         offs_sb = keep.tile([P, S // LIST], U16, name="offs_sb")
         pos1_sb = keep.tile([P, T // LIST], U16, name="pos1_sb")
         pos2_sb = keep.tile([P, T // LIST], U16, name="pos2_sb")
-        gate_sb = keep.tile([P, SIDE], F32, name="gate_sb")
+        gate_low = keep.tile([P, POOL], F32, name="gate_low", tag="last", align_bytes=64)
+        gate_mid = keep.tile([P, POOL_LAST], F32, name="gate_mid")
+        gate_high = keep.tile([P, POOL], F32, name="gate_high")
         gate_rows = keep.tile([P, P], F32, name="gate_rows", tag="odd", align_bytes=64)
-        gate_col = keep.tile([P, (S - SIDE) // P], F32, name="gate_col")
-        gate_ps = [held.tile([P, BANK], F32, name="gate_ps%d" % m) for m in range((S - SIDE) // BANK)]
+        gate_col = keep.tile([P, ROWS], F32, name="gate_col", tag="far", align_bytes=64)
         identity = keep.tile([P, P], F32, name="identity")
         x_sb = [keep.tile([P, T], F32, name="x%d" % r, align_bytes=64) for r in range(PASSES * PACK)]
         w_sb = keep.tile([P, E * PASSES, 2 * N], U8, name="w_sb", align_bytes=64)
         ws_sb = keep.tile([P, E * PASSES, N], U8, name="ws_sb", align_bytes=64)
         b_sb = keep.tile([P, E], F32, name="b_sb")
-        y_sb = keep.tile([P, S], F32, name="y_sb")
 
         x_rows = xT.rearrange("(a p j) t -> a j p t", a=PASSES, j=PACK)
 
         def load_x(r):
             nc.sync.dma_start(out=x_sb[r][:], in_=x_rows[r // PACK, r % PACK])
-
-        def load_gate(lo, hi):
-            nc.sync.dma_start(out=gate_sb[:, lo:hi], in_=gate[0:P, lo:hi])
 
         nc.vector.memset(gate_rows[:], 0.0)
         nc.vector.memset(ws_sb[:].bitcast(I32), 0)
@@ -72,16 +74,16 @@ def tile_moe_pre_lin_silu_kernel(tc, xT, w_words, w_scales, b, gate, offs, pos1,
         nc.sync.dma_start(offs_sb[:], offs)
         for r in range(1, PACK):
             load_x(r)
-        nc.sync.dma_start(out=gate_rows[0 : (S - SIDE) // P, :], in_=gate[0, SIDE:S].rearrange("(m c) -> m c", c=P))
-        load_gate(0, CHUNK)
-        load_x(PACK)
-        load_gate(CHUNK, SIDE)
-        for r in range(PACK + 1, PASSES * PACK):
+        nc.sync.dma_start(out=gate_rows[0:ROWS, :], in_=gate[0, ROW0 * P : (ROW0 + ROWS) * P].rearrange("(m c) -> m c", c=P))
+        nc.sync.dma_start(out=gate_low[:], in_=gate[0:P, 0:POOL])
+        nc.sync.dma_start(out=gate_high[:], in_=gate[0:P, S - POOL : S])
+        for r in range(PACK, PASSES * PACK):
             load_x(r)
         nc.sync.dma_start(out=w_sb[:].bitcast(I32), in_=w_words.rearrange("e a p c -> p (e a) c").bitcast(I32))
         scale_rows = w_scales.rearrange("e a q n -> q (e a) n").bitcast(I32)
         for quad in range(4):
             nc.sync.dma_start(out=ws_sb[32 * quad : 32 * quad + 4].bitcast(I32), in_=scale_rows[4 * quad : 4 * quad + 4])
+        nc.sync.dma_start(out=gate_mid[:], in_=gate[0:P, MID : MID + POOL_LAST])
         nc.sync.dma_start(out=b_sb[:], in_=b)
         nc.sync.dma_start(pos1_sb[:], pos1)
         nc.sync.dma_start(pos2_sb[:], pos2)
@@ -90,19 +92,17 @@ def tile_moe_pre_lin_silu_kernel(tc, xT, w_words, w_scales, b, gate, offs, pos1,
             tile = keep.tile([P, PACK * slots], F32, name=tag, tag=tag, align_bytes=64)
             return tile[:].rearrange("p (j c) -> p j c", j=PACK)
 
-        def stage(slots):
-            return keep.tile([P, PACK * slots], BF16, name="stage", tag="stage", align_bytes=64)
+        def bank(tag):
+            return psum.tile([P, BANK], F32, name=tag, tag=tag)
 
         def window(a, j, lo, w):
             return x_sb[a * PACK + j][:].indirect(offs_sb[:, lo // LIST : (lo + w) // LIST])
 
-        def on_scalar(planes, a, js, lo, w):
-            for j in js:
-                nc.scalar.activation(planes[:, j, :], window(a, j, lo, w), COPY)
+        def on_scalar(planes, a, j, lo, at, to):
+            nc.scalar.activation(planes[:, j, at:to], window(a, j, lo + at, to - at), COPY)
 
-        def on_vector(planes, a, js, lo, w):
-            for j in js:
-                nc.vector.tensor_copy(planes[:, j, :], window(a, j, lo, w))
+        def on_vector(planes, a, j, lo, at, to):
+            nc.vector.tensor_copy(planes[:, j, at:to], window(a, j, lo + at, to - at))
 
         def gate_and_round(engine, into, to, planes, at, weights):
             w = weights.shape[1]
@@ -113,32 +113,25 @@ def tile_moe_pre_lin_silu_kernel(tc, xT, w_words, w_scales, b, gate, offs, pos1,
                 MULT,
             )
 
-        def gate_in_psum(lo, w):
-            return gate_ps[(lo - SIDE) // BANK][:, lo % BANK : lo % BANK + w]
-
         codes = {}
 
-        def quantize(source, at, parts):
-            w = sum(part[2] for part in parts)
-            name = "%d_%d" % parts[0][:2]
-            words = keep.tile([P, w], U32, name="codes" + name, align_bytes=64)
-            scales = keep.tile([P, w], U8, name="scales" + name, align_bytes=64)
+        def quantize(source, at, a, lo, w):
+            words = keep.tile([P, w], U32, name="codes%d_%d" % (a, lo), align_bytes=64)
+            scales = keep.tile([P, w], U8, name="scales%d_%d" % (a, lo), align_bytes=64)
             nc.vector.quantize_mx(out=words[:].bitcast(FP8X4), scales=scales[:], in_=source[:, at * PACK : (at + w) * PACK])
-            to = 0
-            for a, lo, part in parts:
-                for u in range(0, part, P):
-                    codes[a, lo + u] = (words, scales, to + u)
-                to = to + part
+            for u in range(0, w, P):
+                codes[a, lo + u] = (words, scales, u)
 
-        def finish(lo, w):
+        sums = []
+
+        def multiply(acc, lo, w):
             for at in range(lo, lo + w, C):
                 e = at // C
                 n = min(w, C)
-                acc = psum.tile([P, BANK], F32, name="bank")
                 for a in range(PASSES):
                     words, scales, to = codes[a, at]
                     nc.tensor.matmul_mx(
-                        out=acc[:, 0:n],
+                        out=acc[:, at - lo : at - lo + n],
                         lhsT=w_sb[:, e * PASSES + a, :].bitcast(FP4X4),
                         lhsT_scale=ws_sb[:, e * PASSES + a, :],
                         rhs=words[:, to : to + n].bitcast(FP8X4),
@@ -146,68 +139,86 @@ def tile_moe_pre_lin_silu_kernel(tc, xT, w_words, w_scales, b, gate, offs, pos1,
                         start=(a == 0),
                         stop=(a == PASSES - 1),
                     )
-                nc.scalar.activation(out=y_sb[:, at : at + n], in_=acc[:, 0:n], func=SILU, bias=b_sb[:, e : e + 1])
+                sums.append((acc[:, at - lo : at - lo + n], at, n))
 
-        side = room(CHUNK, "even")
-        on_vector(side, 0, range(PACK), 0, CHUNK)
-        main = room(2 * CHUNK, "near")
-        on_scalar(main, 0, range(PACK), SIDE, 2 * CHUNK)
+        rounds = [(a, lo, lo if lo == LOW else S - POOL, POOL if lo == LOW else lo) for a in range(PASSES) for lo in (LOW, HIGH)]
+        own = ROUND - POOL
 
-        turned = psum.tile([P, BANK], F32, name="bank")
+        side = room(POOL, "even")
+        main = room(own, "near")
+        for j in range(PACK):
+            on_vector(side, 0, j, 0, 0, POOL)
+            on_scalar(main, 0, j, POOL, 0, own)
+
+        turned = bank("sum4")
         nc.tensor.transpose(turned[:, 0:P], gate_rows[:], identity[:])
-        nc.vector.tensor_copy(gate_col[:], turned[:, 0 : (S - SIDE) // P])
-        for m in range((S - SIDE) // P):
-            nc.tensor.transpose(gate_ps[m // 4][:, m % 4 * P : (m % 4 + 1) * P], gate_col[:, m : m + 1].to_broadcast([P, P]), identity[:])
+        nc.vector.tensor_copy(gate_col[:], turned[:, 0:ROWS])
+        edge, low, mid, high = bank("edge"), bank("low"), bank("mid"), bank("high")
 
-        def fetch_side(a, lo, tag):
-            planes = room(CHUNK, tag)
-            on_scalar(planes, a, [PACK - 1], lo, CHUNK)
-            on_vector(planes, a, range(PACK - 1), lo, CHUNK)
-            return planes
+        def spread(into, at, row):
+            nc.tensor.transpose(into[:, at * P : (at + 1) * P], gate_col[:, row - ROW0 : row - ROW0 + 1].to_broadcast([P, P]), identity[:])
 
-        rounded = stage(2 * CHUNK)
-        gate_and_round(nc.gpsimd, rounded, 0, side, 0, gate_sb[:, 0:CHUNK])
-        side = fetch_side(0, CHUNK, "odd")
-        gate_and_round(nc.vector, rounded, CHUNK, main, 0, gate_in_psum(SIDE, CHUNK))
-        quantize(rounded, 0, [(0, 0, CHUNK), (0, SIDE, CHUNK)])
+        for m in range(4):
+            spread(low, m, 4 + m)
+        spread(edge, 0, 3)
+        spread(edge, 1, 16)
+        for m in range(4):
+            spread(high, m, 12 + m)
+        for m in range(4):
+            spread(mid, m, 8 + m)
 
-        rounded = stage(2 * CHUNK)
-        gate_and_round(nc.gpsimd, rounded, 0, side, 0, gate_sb[:, CHUNK:SIDE])
-        side = fetch_side(1, 0, "even")
-        far = room(2 * CHUNK, "far")
-        on_scalar(far, 1, range(PACK), SIDE, 2 * CHUNK)
-        gate_and_round(nc.vector, rounded, CHUNK, main, CHUNK, gate_in_psum(SIDE + CHUNK, CHUNK))
-        quantize(rounded, 0, [(0, CHUNK, CHUNK), (0, SIDE + CHUNK, CHUNK)])
+        def stage(tag):
+            return keep.tile([P, PACK * HALF], BF16, name=tag, tag=tag, align_bytes=64)
 
-        rounded = stage(2 * CHUNK)
-        gate_and_round(nc.gpsimd, rounded, 0, side, 0, gate_sb[:, 0:CHUNK])
-        side = fetch_side(1, CHUNK, "odd")
-        main = room(CHUNK, "near")
-        on_scalar(main, 0, range(PACK), S - CHUNK, CHUNK)
-        gate_and_round(nc.vector, rounded, CHUNK, far, 0, gate_in_psum(SIDE, CHUNK))
-        quantize(rounded, 0, [(1, 0, CHUNK), (1, SIDE, CHUNK)])
-        finish(0, CHUNK)
-        finish(SIDE, CHUNK)
+        for r, (a, lo, pool_lo, own_lo) in enumerate(rounds):
+            shared, alone = stage("shared"), stage("alone")
+            shared_lo, alone_lo = (lo, lo + HALF) if lo == LOW else (lo + HALF, lo)
+            gate_and_round(nc.gpsimd, shared, pool_lo - shared_lo, side, 0, (gate_low if lo == LOW else gate_high)[:])
+            side_tag, main_tag = ("odd", "far") if r % 2 == 0 else ("even", "near")
+            if r + 1 < len(rounds):
+                na, nside_lo, side_w = rounds[r + 1][0], rounds[r + 1][2], POOL
+                mains = [(room(own, main_tag), na, rounds[r + 1][3], own)]
+            else:
+                na, nside_lo, side_w = 0, MID, HALF
+                mains = [(room(C, main_tag), 1, MID, C), (room(C, "last"), 1, MID + C, C)]
+            nside = room(side_w, side_tag)
+            third = SHARE - 2 * side_w
+            on_scalar(nside, na, 2, nside_lo, third, side_w)
+            on_scalar(nside, na, 3, nside_lo, 0, side_w)
+            for planes, nb, nlo, w in mains:
+                for j in range(PACK):
+                    on_scalar(planes, nb, j, nlo, 0, w)
+            on_vector(nside, na, 0, nside_lo, 0, side_w)
+            on_vector(nside, na, 1, nside_lo, 0, side_w)
+            if lo == LOW:
+                gate_and_round(nc.vector, alone, 0, main, HALF - POOL, low[:])
+                gate_and_round(nc.vector, shared, POOL, main, 0, edge[:, POOL - ROW0 * P : P])
+            else:
+                gate_and_round(nc.vector, alone, 0, main, 0, high[:])
+                gate_and_round(nc.vector, shared, 0, main, HALF, edge[:, P : P + HALF - POOL])
+            on_vector(nside, na, 2, nside_lo, 0, third)
+            quantize(alone, 0, a, alone_lo, C)
+            quantize(shared, 0, a, shared_lo, HALF)
+            quantize(alone, C, a, alone_lo + C, C)
+            if a == PASSES - 1:
+                tags = ("sum0", "sum1") if lo == LOW else ("low", "high")
+                multiply(bank(tags[0]), shared_lo, HALF)
+                multiply(bank(tags[1]), alone_lo, HALF)
+            side, main = nside, mains[0][0]
 
-        rounded = stage(3 * CHUNK)
-        gate_and_round(nc.gpsimd, rounded, 0, side, 0, gate_sb[:, CHUNK:SIDE])
-        gate_and_round(nc.vector, rounded, CHUNK, far, CHUNK, gate_in_psum(SIDE + CHUNK, CHUNK))
-        last = room(CHUNK, "far")
-        on_scalar(last, 1, range(PACK), S - CHUNK, CHUNK)
-        gate_and_round(nc.vector, rounded, 2 * CHUNK, main, 0, gate_in_psum(S - CHUNK, CHUNK))
-        quantize(rounded, 0, [(1, CHUNK, CHUNK), (1, SIDE + CHUNK, CHUNK)])
-        quantize(rounded, 2 * CHUNK, [(0, S - CHUNK, CHUNK)])
-        finish(CHUNK, CHUNK)
-        finish(SIDE + CHUNK, CHUNK)
+        shared, alone = stage("shared"), stage("alone")
+        gate_and_round(nc.gpsimd, shared, 0, side, 0, gate_mid[:])
+        gate_and_round(nc.vector, shared, POOL_LAST, side, POOL_LAST, mid[:, POOL_LAST:HALF])
+        gate_and_round(nc.vector, alone, 0, mains[0][0], 0, mid[:, 0:C])
+        gate_and_round(nc.vector, alone, C, mains[1][0], 0, mid[:, C:HALF])
+        quantize(shared, 0, 0, MID, HALF)
+        for (at, w), tag in zip([(0, C), (C, P), (C + P, P)], ("sum4", "sum5", "edge")):
+            quantize(alone, at, 1, MID + at, w)
+            multiply(bank(tag), MID + at, w)
 
-        rounded = stage(CHUNK)
-        pieces = [(0, C), (C, P), (C + P, P)]
-        for (at, w), before in zip(pieces + [(None, None)], [None] + pieces):
-            if w:
-                gate_and_round(nc.vector, rounded, at, last, at, gate_in_psum(S - CHUNK + at, w))
-            if before:
-                quantize(rounded, before[0], [(1, S - CHUNK + before[0], before[1])])
-                finish(S - CHUNK + before[0], before[1])
+        y_sb = keep.tile([P, S], F32, name="y_sb", tag="x7", align_bytes=64)
+        for acc, at, n in sums:
+            nc.scalar.activation(out=y_sb[:, at : at + n], in_=acc, func=SILU, bias=b_sb[:, at // C : at // C + 1])
 
         first = keep.tile([P, T], F32, name="first", tag="x0", align_bytes=64)
         total = keep.tile([P, T], F32, name="total", tag="x1", align_bytes=64)

@@ -28,9 +28,9 @@ LIST = 16
 BANK = 512
 ROUND = 1024
 HALF = ROUND // 2
-POOL = 448
+POOL = 512
 POOL_LAST = 288
-SHARE = 1120
+SHARE = 1280
 ALONE = 160
 COMBINE = [0, ALONE, 480, 800, 1120, T]
 LOW, MID, HIGH = 0, ROUND, ROUND + HALF
@@ -153,15 +153,13 @@ def tile_moe_pre_lin_silu_kernel(tc, xT, w_words, w_scales, b, gate, offs, pos1,
         turned = bank("sum4")
         nc.tensor.transpose(turned[:, 0:P], gate_rows[:], identity[:])
         nc.vector.tensor_copy(gate_col[:], turned[:, 0:ROWS])
-        edge, low, mid, high = bank("edge"), bank("low"), bank("mid"), bank("high")
+        low, mid, high = bank("low"), bank("mid"), bank("high")
 
         def spread(into, at, row):
             nc.tensor.transpose(into[:, at * P : (at + 1) * P], gate_col[:, row - ROW0 : row - ROW0 + 1].to_broadcast([P, P]), identity[:])
 
         for m in range(4):
             spread(low, m, 4 + m)
-        spread(edge, 0, 3)
-        spread(edge, 1, 16)
         for m in range(4):
             spread(high, m, 12 + m)
         for m in range(4):
@@ -190,12 +188,7 @@ def tile_moe_pre_lin_silu_kernel(tc, xT, w_words, w_scales, b, gate, offs, pos1,
                     on_scalar(planes, nb, j, nlo, 0, w)
             on_vector(nside, na, 0, nside_lo, 0, side_w)
             on_vector(nside, na, 1, nside_lo, 0, side_w)
-            if lo == LOW:
-                gate_and_round(nc.vector, alone, 0, main, HALF - POOL, low[:])
-                gate_and_round(nc.vector, shared, POOL, main, 0, edge[:, POOL - ROW0 * P : P])
-            else:
-                gate_and_round(nc.vector, alone, 0, main, 0, high[:])
-                gate_and_round(nc.vector, shared, 0, main, HALF, edge[:, P : P + HALF - POOL])
+            gate_and_round(nc.vector, alone, 0, main, 0, (low if lo == LOW else high)[:])
             on_vector(nside, na, 2, nside_lo, 0, third)
             quantize(alone, 0, a, alone_lo, C)
             quantize(shared, 0, a, shared_lo, HALF)

@@ -34,6 +34,10 @@ SHARE = 1280
 ALONE = 160
 COMBINE = [0, ALONE, 480, 800, 1120, T]
 LOW, MID, HIGH = 0, ROUND, ROUND + HALF
+SIDE = PACK * ROUND * 4
+WORDS = C * 4
+STEP = SIDE - WORDS
+SIDE_AT = [2 * STEP, 3 * STEP + WORDS + STEP, STEP, 3 * STEP + WORDS, 0]
 ROW0 = POOL // P
 ROWS = S // P - 2 * ROW0
 
@@ -42,16 +46,17 @@ def tile_moe_pre_lin_silu_kernel(tc, xT, w_words, w_scales, b, gate, offs, pos1,
     nc = tc.nc
     with ExitStack() as ctx:
         keep = ctx.enter_context(tc.tile_pool(name="keep", bufs=1))
+        ring = ctx.enter_context(tc.tile_pool(name="ring", bufs=1))
         psum = ctx.enter_context(tc.psum_pool(name="psum", bufs=1))
 
         offs_sb = keep.tile([P, S // LIST], U16, name="offs_sb")
         pos1_sb = keep.tile([P, T // LIST], U16, name="pos1_sb")
         pos2_sb = keep.tile([P, T // LIST], U16, name="pos2_sb")
-        gate_low = keep.tile([P, POOL], F32, name="gate_low", tag="last", align_bytes=64)
+        gate_low = keep.tile([P, POOL], F32, name="gate_low")
         gate_mid = keep.tile([P, POOL_LAST], F32, name="gate_mid")
         gate_high = keep.tile([P, POOL], F32, name="gate_high")
-        gate_rows = keep.tile([P, P], F32, name="gate_rows", tag="odd", align_bytes=64)
-        gate_col = keep.tile([P, ROWS], F32, name="gate_col", tag="far", align_bytes=64)
+        gate_rows = ring.tile([P, P], F32, name="gate_rows", align_bytes=64, offset=SIDE_AT[1] + WORDS)
+        gate_col = keep.tile([P, ROWS], F32, name="gate_col")
         identity = keep.tile([P, P], F32, name="identity")
         x_sb = [keep.tile([P, T], F32, name="x%d" % r, align_bytes=64) for r in range(PASSES * PACK)]
         w_sb = keep.tile([P, E * PASSES, 2 * N], U8, name="w_sb", align_bytes=64)
@@ -88,9 +93,10 @@ def tile_moe_pre_lin_silu_kernel(tc, xT, w_words, w_scales, b, gate, offs, pos1,
         nc.sync.dma_start(pos1_sb[:], pos1)
         nc.sync.dma_start(pos2_sb[:], pos2)
 
-        def room(slots, tag):
-            tile = keep.tile([P, PACK * slots], F32, name=tag, tag=tag, align_bytes=64)
-            return tile[:].rearrange("p (j c) -> p j c", j=PACK)
+        def rooms(r, widths):
+            tile = ring.tile([P, PACK * ROUND], F32, name="planes%d" % r, align_bytes=64, offset=SIDE_AT[r])
+            starts = [sum(widths[:u]) for u in range(len(widths))]
+            return [tile[:, PACK * at : PACK * (at + w)].rearrange("p (j c) -> p j c", j=PACK) for at, w in zip(starts, widths)]
 
         def bank(tag):
             return psum.tile([P, BANK], F32, name=tag, tag=tag)
@@ -115,8 +121,11 @@ def tile_moe_pre_lin_silu_kernel(tc, xT, w_words, w_scales, b, gate, offs, pos1,
 
         codes = {}
 
-        def quantize(source, at, a, lo, w):
-            words = keep.tile([P, w], U32, name="codes%d_%d" % (a, lo), align_bytes=64)
+        def quantize(source, at, a, lo, w, behind=None):
+            if behind is None:
+                words = keep.tile([P, w], U32, name="codes%d_%d" % (a, lo), align_bytes=64)
+            else:
+                words = ring.tile([P, w], U32, name="codes%d_%d" % (a, lo), align_bytes=64, offset=SIDE_AT[behind] + STEP)
             scales = keep.tile([P, w], U8, name="scales%d_%d" % (a, lo), align_bytes=64)
             nc.vector.quantize_mx(out=words[:].bitcast(FP8X4), scales=scales[:], in_=source[:, at * PACK : (at + w) * PACK])
             for u in range(0, w, P):
@@ -144,8 +153,7 @@ def tile_moe_pre_lin_silu_kernel(tc, xT, w_words, w_scales, b, gate, offs, pos1,
         rounds = [(a, lo, lo if lo == LOW else S - POOL, POOL if lo == LOW else lo) for a in range(PASSES) for lo in (LOW, HIGH)]
         own = ROUND - POOL
 
-        side = room(POOL, "even")
-        main = room(own, "near")
+        side, main = rooms(0, [POOL, own])
         for j in range(PACK):
             on_vector(side, 0, j, 0, 0, POOL)
             on_scalar(main, 0, j, POOL, 0, own)
@@ -172,14 +180,14 @@ def tile_moe_pre_lin_silu_kernel(tc, xT, w_words, w_scales, b, gate, offs, pos1,
             shared, alone = stage("shared"), stage("alone")
             shared_lo, alone_lo = (lo, lo + HALF) if lo == LOW else (lo + HALF, lo)
             gate_and_round(nc.gpsimd, shared, pool_lo - shared_lo, side, 0, (gate_low if lo == LOW else gate_high)[:])
-            side_tag, main_tag = ("odd", "far") if r % 2 == 0 else ("even", "near")
             if r + 1 < len(rounds):
                 na, nside_lo, side_w = rounds[r + 1][0], rounds[r + 1][2], POOL
-                mains = [(room(own, main_tag), na, rounds[r + 1][3], own)]
+                nside, nmain = rooms(r + 1, [POOL, own])
+                mains = [(nmain, na, rounds[r + 1][3], own)]
             else:
                 na, nside_lo, side_w = 0, MID, HALF
-                mains = [(room(C, main_tag), 1, MID, C), (room(C, "last"), 1, MID + C, C)]
-            nside = room(side_w, side_tag)
+                nside, first_half, second_half = rooms(r + 1, [HALF, C, C])
+                mains = [(first_half, 1, MID, C), (second_half, 1, MID + C, C)]
             third = SHARE - 2 * side_w
             on_scalar(nside, na, 2, nside_lo, third, side_w)
             on_scalar(nside, na, 3, nside_lo, 0, side_w)
@@ -192,7 +200,7 @@ def tile_moe_pre_lin_silu_kernel(tc, xT, w_words, w_scales, b, gate, offs, pos1,
             on_vector(nside, na, 2, nside_lo, 0, third)
             quantize(alone, 0, a, alone_lo, C)
             quantize(shared, 0, a, shared_lo, HALF)
-            quantize(alone, C, a, alone_lo + C, C)
+            quantize(alone, C, a, alone_lo + C, C, behind=r)
             if a == PASSES - 1:
                 tags = ("sum0", "sum1") if lo == LOW else ("low", "high")
                 multiply(bank(tags[0]), shared_lo, HALF)

@@ -29,8 +29,8 @@ BANK = 512
 ROUND = 1024
 HALF = ROUND // 2
 POOL = 512
-POOL_LAST = 288
-SHARE = 1280
+POOL_LAST = 256
+SHARE = 1248
 ALONE = 160
 COMBINE = [0, ALONE, 480, 800, 1120, T]
 LOW, MID, HIGH = 0, ROUND, ROUND + HALF
@@ -53,7 +53,7 @@ def tile_moe_pre_lin_silu_kernel(tc, xT, w_words, w_scales, b, gate, offs, pos1,
         pos1_sb = keep.tile([P, T // LIST], U16, name="pos1_sb")
         pos2_sb = keep.tile([P, T // LIST], U16, name="pos2_sb")
         gate_low = keep.tile([P, POOL], F32, name="gate_low")
-        gate_mid = keep.tile([P, POOL_LAST], F32, name="gate_mid")
+        gate_mid = keep.tile([P, POOL_LAST], F32, name="gate_mid", tag="last", align_bytes=64)
         gate_high = keep.tile([P, POOL], F32, name="gate_high")
         gate_rows = ring.tile([P, P], F32, name="gate_rows", align_bytes=64, offset=SIDE_AT[1] + WORDS)
         gate_col = keep.tile([P, ROWS], F32, name="gate_col")
@@ -154,9 +154,12 @@ def tile_moe_pre_lin_silu_kernel(tc, xT, w_words, w_scales, b, gate, offs, pos1,
         own = ROUND - POOL
 
         side, main = rooms(0, [POOL, own])
-        for j in range(PACK):
+        for j in range(PACK - 1):
             on_vector(side, 0, j, 0, 0, POOL)
             on_scalar(main, 0, j, POOL, 0, own)
+        on_vector(side, 0, PACK - 1, 0, 0, POOL // 2)
+        on_scalar(side, 0, PACK - 1, 0, POOL // 2, POOL)
+        on_scalar(main, 0, PACK - 1, POOL, 0, own)
 
         turned = bank("sum4")
         nc.tensor.transpose(turned[:, 0:P], gate_rows[:], identity[:])
@@ -211,11 +214,16 @@ def tile_moe_pre_lin_silu_kernel(tc, xT, w_words, w_scales, b, gate, offs, pos1,
         gate_and_round(nc.gpsimd, shared, 0, side, 0, gate_mid[:])
         gate_and_round(nc.vector, shared, POOL_LAST, side, POOL_LAST, mid[:, POOL_LAST:HALF])
         gate_and_round(nc.vector, alone, 0, mains[0][0], 0, mid[:, 0:C])
-        gate_and_round(nc.vector, alone, C, mains[1][0], 0, mid[:, C:HALF])
+        gate_and_round(nc.vector, alone, C, mains[1][0], 0, mid[:, C : C + P])
         quantize(shared, 0, 0, MID, HALF)
-        for (at, w), tag in zip([(0, C), (C, P), (C + P, P)], ("sum4", "sum5", "edge")):
-            quantize(alone, at, 1, MID + at, w)
-            multiply(bank(tag), MID + at, w)
+        quantize(alone, 0, 1, MID, C)
+        multiply(bank("sum4"), MID, C)
+        last = keep.tile([P, PACK * P], BF16, name="last", tag="last", align_bytes=64)
+        gate_and_round(nc.vector, last, 0, mains[1][0], P, mid[:, C + P : HALF])
+        quantize(alone, C, 1, MID + C, P)
+        multiply(bank("sum5"), MID + C, P)
+        quantize(last, 0, 1, MID + C + P, P)
+        multiply(bank("edge"), MID + C + P, P)
 
         y_sb = keep.tile([P, S], F32, name="y_sb", tag="x7", align_bytes=64)
         for acc, at, n in sums:

@@ -30,7 +30,7 @@ ROUND = 1024
 HALF = ROUND // 2
 POOL = 512
 POOL_LAST = 256
-SHARE = 1248
+SHARE = 1280
 ALONE = 160
 COMBINE = [0, ALONE, 480, 800, 1120, T]
 LOW, MID, HIGH = 0, ROUND, ROUND + HALF
@@ -81,9 +81,9 @@ def tile_moe_pre_lin_silu_kernel(tc, xT, w_words, w_scales, b, gate, offs, pos1,
             load_x(r)
         nc.sync.dma_start(out=gate_rows[0:ROWS, :], in_=gate[0, ROW0 * P : (ROW0 + ROWS) * P].rearrange("(m c) -> m c", c=P))
         nc.sync.dma_start(out=gate_low[:], in_=gate[0:P, 0:POOL])
-        nc.sync.dma_start(out=gate_high[:], in_=gate[0:P, S - POOL : S])
         for r in range(PACK, PASSES * PACK):
             load_x(r)
+        nc.sync.dma_start(out=gate_high[:], in_=gate[0:P, S - POOL : S])
         nc.sync.dma_start(out=w_sb[:].bitcast(I32), in_=w_words.rearrange("e a p c -> p (e a) c").bitcast(I32))
         scale_rows = w_scales.rearrange("e a q n -> q (e a) n").bitcast(I32)
         for quad in range(4):
@@ -154,12 +154,9 @@ def tile_moe_pre_lin_silu_kernel(tc, xT, w_words, w_scales, b, gate, offs, pos1,
         own = ROUND - POOL
 
         side, main = rooms(0, [POOL, own])
-        for j in range(PACK - 1):
+        for j in range(PACK):
             on_vector(side, 0, j, 0, 0, POOL)
             on_scalar(main, 0, j, POOL, 0, own)
-        on_vector(side, 0, PACK - 1, 0, 0, POOL // 2)
-        on_scalar(side, 0, PACK - 1, 0, POOL // 2, POOL)
-        on_scalar(main, 0, PACK - 1, POOL, 0, own)
 
         turned = bank("sum4")
         nc.tensor.transpose(turned[:, 0:P], gate_rows[:], identity[:])
@@ -184,23 +181,24 @@ def tile_moe_pre_lin_silu_kernel(tc, xT, w_words, w_scales, b, gate, offs, pos1,
             shared_lo, alone_lo = (lo, lo + HALF) if lo == LOW else (lo + HALF, lo)
             gate_and_round(nc.gpsimd, shared, pool_lo - shared_lo, side, 0, (gate_low if lo == LOW else gate_high)[:])
             if r + 1 < len(rounds):
-                na, nside_lo, side_w = rounds[r + 1][0], rounds[r + 1][2], POOL
-                nside, nmain = rooms(r + 1, [POOL, own])
-                mains = [(nmain, na, rounds[r + 1][3], own)]
+                na, nlo = rounds[r + 1][:2]
+                (planes,) = rooms(r + 1, [ROUND])
+                halves = planes[:, :, 0:HALF], planes[:, :, HALF:ROUND]
+                nside, nmain = halves if nlo == LOW else halves[::-1]
+                on_scalar(planes, na, 1, nlo, SHARE - ROUND, ROUND)
+                on_scalar(planes, na, 2, nlo, 0, ROUND)
+                on_scalar(planes, na, 3, nlo, 0, ROUND)
+                before, after = (planes, na, 0, nlo, 0, ROUND), (planes, na, 1, nlo, 0, SHARE - ROUND)
             else:
-                na, nside_lo, side_w = 0, MID, HALF
-                nside, first_half, second_half = rooms(r + 1, [HALF, C, C])
-                mains = [(first_half, 1, MID, C), (second_half, 1, MID + C, C)]
-            third = SHARE - 2 * side_w
-            on_scalar(nside, na, 2, nside_lo, third, side_w)
-            on_scalar(nside, na, 3, nside_lo, 0, side_w)
-            for planes, nb, nlo, w in mains:
+                nside, nmain = rooms(r + 1, [HALF, HALF])
+                for j in range(2, PACK):
+                    on_scalar(nside, 0, j, MID, 0, HALF)
                 for j in range(PACK):
-                    on_scalar(planes, nb, j, nlo, 0, w)
-            on_vector(nside, na, 0, nside_lo, 0, side_w)
-            on_vector(nside, na, 1, nside_lo, 0, side_w)
+                    on_scalar(nmain, 1, j, MID, 0, HALF)
+                before, after = (nside, 0, 0, MID, 0, HALF), (nside, 0, 1, MID, 0, HALF)
+            on_vector(*before)
             gate_and_round(nc.vector, alone, 0, main, 0, (low if lo == LOW else high)[:])
-            on_vector(nside, na, 2, nside_lo, 0, third)
+            on_vector(*after)
             quantize(alone, 0, a, alone_lo, C)
             quantize(shared, 0, a, shared_lo, HALF)
             quantize(alone, C, a, alone_lo + C, C, behind=r)
@@ -208,18 +206,17 @@ def tile_moe_pre_lin_silu_kernel(tc, xT, w_words, w_scales, b, gate, offs, pos1,
                 tags = ("sum0", "sum1") if lo == LOW else ("low", "high")
                 multiply(bank(tags[0]), shared_lo, HALF)
                 multiply(bank(tags[1]), alone_lo, HALF)
-            side, main = nside, mains[0][0]
+            side, main = nside, nmain
 
         shared, alone = stage("shared"), stage("alone")
         gate_and_round(nc.gpsimd, shared, 0, side, 0, gate_mid[:])
         gate_and_round(nc.vector, shared, POOL_LAST, side, POOL_LAST, mid[:, POOL_LAST:HALF])
-        gate_and_round(nc.vector, alone, 0, mains[0][0], 0, mid[:, 0:C])
-        gate_and_round(nc.vector, alone, C, mains[1][0], 0, mid[:, C : C + P])
+        gate_and_round(nc.vector, alone, 0, main, 0, mid[:, 0 : C + P])
         quantize(shared, 0, 0, MID, HALF)
         quantize(alone, 0, 1, MID, C)
         multiply(bank("sum4"), MID, C)
         last = keep.tile([P, PACK * P], BF16, name="last", tag="last", align_bytes=64)
-        gate_and_round(nc.vector, last, 0, mains[1][0], P, mid[:, C + P : HALF])
+        gate_and_round(nc.vector, last, 0, main, C + P, mid[:, C + P : HALF])
         quantize(alone, C, 1, MID + C, P)
         multiply(bank("sum5"), MID + C, P)
         quantize(last, 0, 1, MID + C + P, P)

@@ -30,7 +30,8 @@ ROUND = 1024
 HALF = ROUND // 2
 POOL = 512
 POOL_LAST = 256
-SHARE = 1280
+SHARE = 1376
+SHARE_FOURTH = 1280
 ALONE = 160
 COMBINE = [0, ALONE, 480, 800, 1120, T]
 LOW, MID, HIGH = 0, ROUND, ROUND + HALF
@@ -191,11 +192,12 @@ def tile_moe_pre_lin_silu_kernel(tc, xT, w_words, w_scales, b, gate, offs, pos1,
                 before, after = (planes, na, 0, nlo, 0, ROUND), (planes, na, 1, nlo, 0, SHARE - ROUND)
             else:
                 nside, nmain = rooms(r + 1, [HALF, HALF])
-                for j in range(2, PACK):
-                    on_scalar(nside, 0, j, MID, 0, HALF)
+                on_scalar(nside, 0, 2, MID, SHARE_FOURTH - ROUND, HALF)
+                on_scalar(nside, 0, 3, MID, 0, HALF)
                 for j in range(PACK):
                     on_scalar(nmain, 1, j, MID, 0, HALF)
-                before, after = (nside, 0, 0, MID, 0, HALF), (nside, 0, 1, MID, 0, HALF)
+                on_vector(nside, 0, 0, MID, 0, HALF)
+                before, after = (nside, 0, 1, MID, 0, HALF), (nside, 0, 2, MID, 0, SHARE_FOURTH - ROUND)
             on_vector(*before)
             gate_and_round(nc.vector, alone, 0, main, 0, (low if lo == LOW else high)[:])
             on_vector(*after)

@@ -30,8 +30,8 @@ ROUND = 1024
 HALF = ROUND // 2
 POOL = 512
 POOL_LAST = 256
-SHARE = 1376
-SHARE_FOURTH = 1280
+SHARE = 1344
+SHARE_FOURTH = 1152
 ALONE = 160
 COMBINE = [0, ALONE, 480, 800, 1120, T]
 LOW, MID, HIGH = 0, ROUND, ROUND + HALF

@@ -28,9 +28,11 @@ LIST = 16
 BANK = 512
 ROUND = 1024
 HALF = ROUND // 2
-POOL = 512
+POOL = 576
+POOL_FOURTH = 512
+WALK = 8
 POOL_LAST = 256
-SHARE = 1344
+SHARE = 1408
 SHARE_FOURTH = 1152
 ALONE = 160
 COMBINE = [0, ALONE, 480, 800, 1120, T]
@@ -39,7 +41,7 @@ SIDE = PACK * ROUND * 4
 WORDS = C * 4
 STEP = SIDE - WORDS
 SIDE_AT = [2 * STEP, 3 * STEP + WORDS + STEP, STEP, 3 * STEP + WORDS, 0]
-ROW0 = POOL // P
+ROW0 = HALF // P
 ROWS = S // P - 2 * ROW0
 
 
@@ -111,12 +113,12 @@ def tile_moe_pre_lin_silu_kernel(tc, xT, w_words, w_scales, b, gate, offs, pos1,
         def on_vector(planes, a, j, lo, at, to):
             nc.vector.tensor_copy(planes[:, j, at:to], window(a, j, lo + at, to - at))
 
-        def gate_and_round(engine, into, to, planes, at, weights):
+        def gate_and_round(engine, into, to, planes, at, weights, run=4):
             w = weights.shape[1]
             engine.tensor_tensor(
-                into[:, to * PACK : (to + w) * PACK].rearrange("p (c i j) -> p c j i", i=4, j=PACK),
-                planes[:, :, at : at + w].rearrange("p j (c i) -> p c j i", i=4),
-                weights.rearrange("p (c i) -> p c i", i=4).unsqueeze(2).to_broadcast([P, w // 4, PACK, 4]),
+                into[:, to * PACK : (to + w) * PACK].rearrange("p (c i j) -> p c j i", i=run, j=PACK),
+                planes[:, :, at : at + w].rearrange("p j (c i) -> p c j i", i=run),
+                weights.rearrange("p (c i) -> p c i", i=run).unsqueeze(2).to_broadcast([P, w // run, PACK, run]),
                 MULT,
             )
 
@@ -174,18 +176,26 @@ def tile_moe_pre_lin_silu_kernel(tc, xT, w_words, w_scales, b, gate, offs, pos1,
         for m in range(4):
             spread(mid, m, 8 + m)
 
-        def stage(tag):
-            return keep.tile([P, PACK * HALF], BF16, name=tag, tag=tag, align_bytes=64)
+        def stage(tag, slots=HALF):
+            return keep.tile([P, PACK * slots], BF16, name=tag, tag=tag, align_bytes=64)
 
         for r, (a, lo, pool_lo, own_lo) in enumerate(rounds):
-            shared, alone = stage("shared"), stage("alone")
-            shared_lo, alone_lo = (lo, lo + HALF) if lo == LOW else (lo + HALF, lo)
-            gate_and_round(nc.gpsimd, shared, pool_lo - shared_lo, side, 0, (gate_low if lo == LOW else gate_high)[:])
+            shared, alone = stage("shared", ROUND - C), stage("alone", C)
+            pool = POOL if r + 1 < len(rounds) else POOL_FOURTH
+            rest = ROUND - C - pool
+            shared_lo, alone_lo = (lo, lo + ROUND - C) if lo == LOW else (lo + C, lo)
+            if lo == LOW:
+                gate_and_round(nc.gpsimd, shared, 0, side, 0, gate_low[:], WALK)
+            else:
+                gate_and_round(nc.gpsimd, shared, rest, side, 0, gate_high[:, POOL - pool :], WALK)
             if r + 1 < len(rounds):
                 na, nlo = rounds[r + 1][:2]
                 (planes,) = rooms(r + 1, [ROUND])
-                halves = planes[:, :, 0:HALF], planes[:, :, HALF:ROUND]
-                nside, nmain = halves if nlo == LOW else halves[::-1]
+                npool = POOL if r + 2 < len(rounds) else POOL_FOURTH
+                if nlo == LOW:
+                    nside, nmain = planes[:, :, 0:npool], planes[:, :, npool:ROUND]
+                else:
+                    nside, nmain = planes[:, :, ROUND - npool : ROUND], planes[:, :, 0 : ROUND - npool]
                 on_scalar(planes, na, 1, nlo, SHARE - ROUND, ROUND)
                 on_scalar(planes, na, 2, nlo, 0, ROUND)
                 on_scalar(planes, na, 3, nlo, 0, ROUND)
@@ -199,19 +209,24 @@ def tile_moe_pre_lin_silu_kernel(tc, xT, w_words, w_scales, b, gate, offs, pos1,
                 on_vector(nside, 0, 0, MID, 0, HALF)
                 before, after = (nside, 0, 1, MID, 0, HALF), (nside, 0, 2, MID, 0, SHARE_FOURTH - ROUND)
             on_vector(*before)
-            gate_and_round(nc.vector, alone, 0, main, 0, (low if lo == LOW else high)[:])
+            if lo == LOW:
+                gate_and_round(nc.vector, shared, pool, main, 0, low[:, pool - HALF : C])
+                gate_and_round(nc.vector, alone, 0, main, rest, low[:, C:HALF])
+            else:
+                gate_and_round(nc.vector, shared, 0, main, C, high[:, C : C + rest])
+                gate_and_round(nc.vector, alone, 0, main, 0, high[:, 0:C])
             on_vector(*after)
-            quantize(alone, 0, a, alone_lo, C)
             quantize(shared, 0, a, shared_lo, HALF)
-            quantize(alone, C, a, alone_lo + C, C, behind=r)
+            quantize(shared, HALF, a, shared_lo + HALF, C)
+            quantize(alone, 0, a, alone_lo, C, behind=r)
             if a == PASSES - 1:
                 tags = ("sum0", "sum1") if lo == LOW else ("low", "high")
-                multiply(bank(tags[0]), shared_lo, HALF)
-                multiply(bank(tags[1]), alone_lo, HALF)
+                multiply(bank(tags[0]), lo, HALF)
+                multiply(bank(tags[1]), lo + HALF, HALF)
             side, main = nside, nmain
 
         shared, alone = stage("shared"), stage("alone")
-        gate_and_round(nc.gpsimd, shared, 0, side, 0, gate_mid[:])
+        gate_and_round(nc.gpsimd, shared, 0, side, 0, gate_mid[:], WALK)
         gate_and_round(nc.vector, shared, POOL_LAST, side, POOL_LAST, mid[:, POOL_LAST:HALF])
         gate_and_round(nc.vector, alone, 0, main, 0, mid[:, 0 : C + P])
         quantize(shared, 0, 0, MID, HALF)
@@ -224,7 +239,7 @@ def tile_moe_pre_lin_silu_kernel(tc, xT, w_words, w_scales, b, gate, offs, pos1,
         quantize(last, 0, 1, MID + C + P, P)
         multiply(bank("edge"), MID + C + P, P)
 
-        y_sb = keep.tile([P, S], F32, name="y_sb", tag="x7", align_bytes=64)
+        y_sb = keep.tile([P, S], F32, name="y_sb", tag="x6", align_bytes=64)
         for acc, at, n in sums:
             nc.scalar.activation(out=y_sb[:, at : at + n], in_=acc, func=SILU, bias=b_sb[:, at // C : at // C + 1])
 

@@ -28,12 +28,12 @@ LIST = 16
 BANK = 512
 ROUND = 1024
 HALF = ROUND // 2
-POOL = 576
-POOL_FOURTH = 512
+POOL = 560
+POOL_FOURTH = 528
 WALK = 8
-POOL_LAST = 256
-SHARE = 1408
-SHARE_FOURTH = 1152
+POOL_LAST = 288
+SHARE = 1376
+SHARE_FOURTH = 1184
 ALONE = 160
 COMBINE = [0, ALONE, 480, 800, 1120, T]
 LOW, MID, HIGH = 0, ROUND, ROUND + HALF
@@ -124,15 +124,18 @@ def tile_moe_pre_lin_silu_kernel(tc, xT, w_words, w_scales, b, gate, offs, pos1,
 
         codes = {}
 
-        def quantize(source, at, a, lo, w, behind=None):
+        def code_tiles(a, lo, w, behind=None):
             if behind is None:
                 words = keep.tile([P, w], U32, name="codes%d_%d" % (a, lo), align_bytes=64)
             else:
-                words = ring.tile([P, w], U32, name="codes%d_%d" % (a, lo), align_bytes=64, offset=SIDE_AT[behind] + STEP)
+                words = ring.tile([P, w], U32, name="codes%d_%d" % (a, lo), align_bytes=64, offset=SIDE_AT[behind] + SIDE - 4 * w)
             scales = keep.tile([P, w], U8, name="scales%d_%d" % (a, lo), align_bytes=64)
-            nc.vector.quantize_mx(out=words[:].bitcast(FP8X4), scales=scales[:], in_=source[:, at * PACK : (at + w) * PACK])
             for u in range(0, w, P):
                 codes[a, lo + u] = (words, scales, u)
+
+        def quantize(source, at, a, lo, w):
+            words, scales, to = codes[a, lo]
+            nc.vector.quantize_mx(out=words[:, to : to + w].bitcast(FP8X4), scales=scales[:, to : to + w], in_=source[:, at * PACK : (at + w) * PACK])
 
         sums = []
 
@@ -156,10 +159,11 @@ def tile_moe_pre_lin_silu_kernel(tc, xT, w_words, w_scales, b, gate, offs, pos1,
         rounds = [(a, lo, lo if lo == LOW else S - POOL, POOL if lo == LOW else lo) for a in range(PASSES) for lo in (LOW, HIGH)]
         own = ROUND - POOL
 
-        side, main = rooms(0, [POOL, own])
+        (planes,) = rooms(0, [ROUND])
+        side, main = planes[:, :, 0:POOL], planes[:, :, POOL:ROUND]
         for j in range(PACK):
-            on_vector(side, 0, j, 0, 0, POOL)
-            on_scalar(main, 0, j, POOL, 0, own)
+            on_vector(planes, 0, j, 0, 0, HALF)
+            on_scalar(planes, 0, j, 0, HALF, ROUND)
 
         turned = bank("sum4")
         nc.tensor.transpose(turned[:, 0:P], gate_rows[:], identity[:])
@@ -180,10 +184,9 @@ def tile_moe_pre_lin_silu_kernel(tc, xT, w_words, w_scales, b, gate, offs, pos1,
             return keep.tile([P, PACK * slots], BF16, name=tag, tag=tag, align_bytes=64)
 
         for r, (a, lo, pool_lo, own_lo) in enumerate(rounds):
-            shared, alone = stage("shared", ROUND - C), stage("alone", C)
+            shared, alone = stage("shared", HALF + P), stage("alone", HALF - P)
             pool = POOL if r + 1 < len(rounds) else POOL_FOURTH
-            rest = ROUND - C - pool
-            shared_lo, alone_lo = (lo, lo + ROUND - C) if lo == LOW else (lo + C, lo)
+            rest = HALF + P - pool
             if lo == LOW:
                 gate_and_round(nc.gpsimd, shared, 0, side, 0, gate_low[:], WALK)
             else:
@@ -210,15 +213,24 @@ def tile_moe_pre_lin_silu_kernel(tc, xT, w_words, w_scales, b, gate, offs, pos1,
                 before, after = (nside, 0, 1, MID, 0, HALF), (nside, 0, 2, MID, 0, SHARE_FOURTH - ROUND)
             on_vector(*before)
             if lo == LOW:
-                gate_and_round(nc.vector, shared, pool, main, 0, low[:, pool - HALF : C])
-                gate_and_round(nc.vector, alone, 0, main, rest, low[:, C:HALF])
+                gate_and_round(nc.vector, alone, 0, main, rest, low[:, P:HALF])
+                gate_and_round(nc.vector, shared, pool, main, 0, low[:, P - rest : P])
             else:
-                gate_and_round(nc.vector, shared, 0, main, C, high[:, C : C + rest])
-                gate_and_round(nc.vector, alone, 0, main, 0, high[:, 0:C])
+                gate_and_round(nc.vector, alone, 0, main, 0, high[:, 0 : HALF - P])
+                gate_and_round(nc.vector, shared, 0, main, HALF - P, high[:, HALF - P : HALF - P + rest])
             on_vector(*after)
-            quantize(shared, 0, a, shared_lo, HALF)
-            quantize(shared, HALF, a, shared_lo + HALF, C)
-            quantize(alone, 0, a, alone_lo, C, behind=r)
+            if lo == LOW:
+                code_tiles(a, lo, HALF)
+                code_tiles(a, lo + HALF, HALF, behind=r)
+                quantize(shared, 0, a, lo, HALF)
+                quantize(shared, HALF, a, lo + HALF, P)
+                quantize(alone, 0, a, lo + HALF + P, HALF - P)
+            else:
+                code_tiles(a, lo + HALF, HALF)
+                code_tiles(a, lo, HALF, behind=r)
+                quantize(shared, P, a, lo + HALF, HALF)
+                quantize(shared, 0, a, lo + HALF - P, P)
+                quantize(alone, 0, a, lo, HALF - P)
             if a == PASSES - 1:
                 tags = ("sum0", "sum1") if lo == LOW else ("low", "high")
                 multiply(bank(tags[0]), lo, HALF)
@@ -229,6 +241,10 @@ def tile_moe_pre_lin_silu_kernel(tc, xT, w_words, w_scales, b, gate, offs, pos1,
         gate_and_round(nc.gpsimd, shared, 0, side, 0, gate_mid[:], WALK)
         gate_and_round(nc.vector, shared, POOL_LAST, side, POOL_LAST, mid[:, POOL_LAST:HALF])
         gate_and_round(nc.vector, alone, 0, main, 0, mid[:, 0 : C + P])
+        code_tiles(0, MID, HALF)
+        code_tiles(1, MID, C)
+        code_tiles(1, MID + C, P)
+        code_tiles(1, MID + C + P, P)
         quantize(shared, 0, 0, MID, HALF)
         quantize(alone, 0, 1, MID, C)
         multiply(bank("sum4"), MID, C)

@@ -25,24 +25,25 @@ P = 128
 PACK = 4
 PASSES = K // (P * PACK)
 LIST = 16
-BANK = 512
+VECTOR_RUN, GPSIMD_RUN = 4, 8
 ROUND = 1024
 HALF = ROUND // 2
-POOL = 560
-POOL_FOURTH = 528
-WALK = 8
-POOL_LAST = 288
-SHARE = 1376
-SHARE_FOURTH = 1184
-ALONE = 160
-COMBINE = [0, ALONE, 480, 800, 1120, T]
 LOW, MID, HIGH = 0, ROUND, ROUND + HALF
-SIDE = PACK * ROUND * 4
-WORDS = C * 4
-STEP = SIDE - WORDS
-SIDE_AT = [2 * STEP, 3 * STEP + WORDS + STEP, STEP, 3 * STEP + WORDS, 0]
-ROW0 = HALF // P
-ROWS = S // P - 2 * ROW0
+GPSIMD_SLOTS = [544, 544, 544, 528, 272]
+GPSIMD_MOST, GPSIMD_LAST = max(GPSIMD_SLOTS), GPSIMD_SLOTS[-1]
+SHARED = HALF + P
+OWN = ROUND - SHARED
+VECTOR_SHARE = 1344
+VECTOR_SHARE_LAST = 1184
+ALONE = 160
+COMBINE = [0, ALONE, 3 * ALONE, 5 * ALONE, 7 * ALONE, T]
+FIRST_ROW, ROWS = HALF // P, (S - ROUND) // P
+
+TILE_BYTES = PACK * ROUND * 4
+OVERLAP = 1024
+STEP = TILE_BYTES - OVERLAP
+ODD = 2 * STEP + TILE_BYTES
+PLANES_AT = [2 * STEP, ODD + STEP, STEP, ODD, 0]
 
 
 def tile_moe_pre_lin_silu_kernel(tc, xT, w_words, w_scales, b, gate, offs, pos1, pos2, out):
@@ -55,21 +56,16 @@ def tile_moe_pre_lin_silu_kernel(tc, xT, w_words, w_scales, b, gate, offs, pos1,
         offs_sb = keep.tile([P, S // LIST], U16, name="offs_sb")
         pos1_sb = keep.tile([P, T // LIST], U16, name="pos1_sb")
         pos2_sb = keep.tile([P, T // LIST], U16, name="pos2_sb")
-        gate_low = keep.tile([P, POOL], F32, name="gate_low")
-        gate_mid = keep.tile([P, POOL_LAST], F32, name="gate_mid", tag="last", align_bytes=64)
-        gate_high = keep.tile([P, POOL], F32, name="gate_high")
-        gate_rows = ring.tile([P, P], F32, name="gate_rows", align_bytes=64, offset=SIDE_AT[1] + WORDS)
+        gate_low = keep.tile([P, GPSIMD_MOST], F32, name="gate_low")
+        gate_mid = keep.tile([P, GPSIMD_LAST], F32, name="gate_mid", tag="last", align_bytes=64)
+        gate_high = keep.tile([P, GPSIMD_MOST], F32, name="gate_high")
+        gate_rows = ring.tile([P, P], F32, name="gate_rows", align_bytes=64, offset=PLANES_AT[1] + OVERLAP)
         gate_col = keep.tile([P, ROWS], F32, name="gate_col")
         identity = keep.tile([P, P], F32, name="identity")
-        x_sb = [keep.tile([P, T], F32, name="x%d" % r, align_bytes=64) for r in range(PASSES * PACK)]
+        x_sb = [keep.tile([P, T], F32, name="x%d" % u, align_bytes=64) for u in range(PASSES * PACK)]
         w_sb = keep.tile([P, E * PASSES, 2 * N], U8, name="w_sb", align_bytes=64)
         ws_sb = keep.tile([P, E * PASSES, N], U8, name="ws_sb", align_bytes=64)
         b_sb = keep.tile([P, E], F32, name="b_sb")
-
-        x_rows = xT.rearrange("(a p j) t -> a j p t", a=PASSES, j=PACK)
-
-        def load_x(r):
-            nc.sync.dma_start(out=x_sb[r][:], in_=x_rows[r // PACK, r % PACK])
 
         nc.vector.memset(gate_rows[:], 0.0)
         nc.vector.memset(ws_sb[:].bitcast(I32), 0)
@@ -78,186 +74,183 @@ def tile_moe_pre_lin_silu_kernel(tc, xT, w_words, w_scales, b, gate, offs, pos1,
         nc.scalar.activation(out=warm[:, 1:2], in_=warm[:, 0:1], func=SILU)
         make_identity(nc, identity[:])
 
-        load_x(0)
+        x_rows = xT.rearrange("(a p j) t -> a j p t", a=PASSES, j=PACK)
+        nc.sync.dma_start(out=x_sb[0][:], in_=x_rows[0, 0])
         nc.sync.dma_start(offs_sb[:], offs)
-        for r in range(1, PACK):
-            load_x(r)
-        nc.sync.dma_start(out=gate_rows[0:ROWS, :], in_=gate[0, ROW0 * P : (ROW0 + ROWS) * P].rearrange("(m c) -> m c", c=P))
-        nc.sync.dma_start(out=gate_low[:], in_=gate[0:P, 0:POOL])
-        for r in range(PACK, PASSES * PACK):
-            load_x(r)
-        nc.sync.dma_start(out=gate_high[:], in_=gate[0:P, S - POOL : S])
+        for j in range(1, PACK):
+            nc.sync.dma_start(out=x_sb[j][:], in_=x_rows[0, j])
+        nc.sync.dma_start(out=gate_rows[0:ROWS, :], in_=gate[0, FIRST_ROW * P : (FIRST_ROW + ROWS) * P].rearrange("(m c) -> m c", c=P))
+        nc.sync.dma_start(out=gate_low[:], in_=gate[0:P, 0:GPSIMD_MOST])
+        for j in range(PACK):
+            nc.sync.dma_start(out=x_sb[PACK + j][:], in_=x_rows[1, j])
+        nc.sync.dma_start(out=gate_high[:], in_=gate[0:P, S - GPSIMD_MOST : S])
         nc.sync.dma_start(out=w_sb[:].bitcast(I32), in_=w_words.rearrange("e a p c -> p (e a) c").bitcast(I32))
         scale_rows = w_scales.rearrange("e a q n -> q (e a) n").bitcast(I32)
         for quad in range(4):
             nc.sync.dma_start(out=ws_sb[32 * quad : 32 * quad + 4].bitcast(I32), in_=scale_rows[4 * quad : 4 * quad + 4])
-        nc.sync.dma_start(out=gate_mid[:], in_=gate[0:P, MID : MID + POOL_LAST])
+        nc.sync.dma_start(out=gate_mid[:], in_=gate[0:P, MID : MID + GPSIMD_LAST])
         nc.sync.dma_start(out=b_sb[:], in_=b)
         nc.sync.dma_start(pos1_sb[:], pos1)
         nc.sync.dma_start(pos2_sb[:], pos2)
 
-        def rooms(r, widths):
-            tile = ring.tile([P, PACK * ROUND], F32, name="planes%d" % r, align_bytes=64, offset=SIDE_AT[r])
-            starts = [sum(widths[:u]) for u in range(len(widths))]
-            return [tile[:, PACK * at : PACK * (at + w)].rearrange("p (j c) -> p j c", j=PACK) for at, w in zip(starts, widths)]
+        def planes_of(r, slots):
+            tile = ring.tile([P, PACK * ROUND], F32, name="planes%d" % r, align_bytes=64, offset=PLANES_AT[r])
+            return [tile[:, PACK * at : PACK * (at + slots)].rearrange("p (j c) -> p j c", j=PACK) for at in range(0, ROUND, slots)]
 
         def bank(tag):
-            return psum.tile([P, BANK], F32, name=tag, tag=tag)
+            return psum.tile([P, HALF], F32, name=tag, tag=tag)
 
-        def window(a, j, lo, w):
-            return x_sb[a * PACK + j][:].indirect(offs_sb[:, lo // LIST : (lo + w) // LIST])
+        def stage(tag, slots):
+            return keep.tile([P, PACK * slots], BF16, name=tag, tag=tag, align_bytes=64)
 
-        def on_scalar(planes, a, j, lo, at, to):
-            nc.scalar.activation(planes[:, j, at:to], window(a, j, lo + at, to - at), COPY)
+        def tokens(a, j, slot, count):
+            return x_sb[a * PACK + j][:].indirect(offs_sb[:, slot // LIST : (slot + count) // LIST])
 
-        def on_vector(planes, a, j, lo, at, to):
-            nc.vector.tensor_copy(planes[:, j, at:to], window(a, j, lo + at, to - at))
+        def gather_on_scalar(planes, a, j, base, at, to):
+            nc.scalar.activation(planes[:, j, at:to], tokens(a, j, base + at, to - at), COPY)
 
-        def gate_and_round(engine, into, to, planes, at, weights, run=4):
-            w = weights.shape[1]
+        def gather_on_vector(planes, a, j, base, at, to):
+            nc.vector.tensor_copy(planes[:, j, at:to], tokens(a, j, base + at, to - at))
+
+        def gate_and_round(engine, run, staged, to, planes, at, weights):
+            count = weights.shape[1]
             engine.tensor_tensor(
-                into[:, to * PACK : (to + w) * PACK].rearrange("p (c i j) -> p c j i", i=run, j=PACK),
-                planes[:, :, at : at + w].rearrange("p j (c i) -> p c j i", i=run),
-                weights.rearrange("p (c i) -> p c i", i=run).unsqueeze(2).to_broadcast([P, w // run, PACK, run]),
+                staged[:, to * PACK : (to + count) * PACK].rearrange("p (c i j) -> p c j i", i=run, j=PACK),
+                planes[:, :, at : at + count].rearrange("p j (c i) -> p c j i", i=run),
+                weights.rearrange("p (c i) -> p c i", i=run).unsqueeze(2).to_broadcast([P, count // run, PACK, run]),
                 MULT,
             )
 
+        def on_gpsimd(staged, to, planes, at, weights):
+            gate_and_round(nc.gpsimd, GPSIMD_RUN, staged, to, planes, at, weights)
+
+        def on_vector(staged, to, planes, at, weights):
+            gate_and_round(nc.vector, VECTOR_RUN, staged, to, planes, at, weights)
+
         codes = {}
 
-        def code_tiles(a, lo, w, behind=None):
-            if behind is None:
-                words = keep.tile([P, w], U32, name="codes%d_%d" % (a, lo), align_bytes=64)
-            else:
-                words = ring.tile([P, w], U32, name="codes%d_%d" % (a, lo), align_bytes=64, offset=SIDE_AT[behind] + SIDE - 4 * w)
-            scales = keep.tile([P, w], U8, name="scales%d_%d" % (a, lo), align_bytes=64)
-            for u in range(0, w, P):
-                codes[a, lo + u] = (words, scales, u)
+        def code_tiles(a, slot, count, pool=keep, offset=None):
+            words = pool.tile([P, count], U32, name="codes%d_%d" % (a, slot), align_bytes=64, offset=offset)
+            scales = keep.tile([P, count], U8, name="scales%d_%d" % (a, slot), align_bytes=64)
+            for u in range(0, count, P):
+                codes[a, slot + u] = (words, scales, u)
 
-        def quantize(source, at, a, lo, w):
-            words, scales, to = codes[a, lo]
-            nc.vector.quantize_mx(out=words[:, to : to + w].bitcast(FP8X4), scales=scales[:, to : to + w], in_=source[:, at * PACK : (at + w) * PACK])
+        def quantize(staged, at, a, slot, count):
+            words, scales, col = codes[a, slot]
+            nc.vector.quantize_mx(
+                out=words[:, col : col + count].bitcast(FP8X4),
+                scales=scales[:, col : col + count],
+                in_=staged[:, at * PACK : (at + count) * PACK],
+            )
 
         sums = []
 
-        def multiply(acc, lo, w):
-            for at in range(lo, lo + w, C):
-                e = at // C
-                n = min(w, C)
+        def multiply(acc, slot, count):
+            width = min(count, C)
+            for at in range(0, count, width):
+                e = (slot + at) // C
                 for a in range(PASSES):
-                    words, scales, to = codes[a, at]
+                    words, scales, col = codes[a, slot + at]
                     nc.tensor.matmul_mx(
-                        out=acc[:, at - lo : at - lo + n],
+                        out=acc[:, at : at + width],
                         lhsT=w_sb[:, e * PASSES + a, :].bitcast(FP4X4),
                         lhsT_scale=ws_sb[:, e * PASSES + a, :],
-                        rhs=words[:, to : to + n].bitcast(FP8X4),
-                        rhs_scale=scales[:, to : to + n],
+                        rhs=words[:, col : col + width].bitcast(FP8X4),
+                        rhs_scale=scales[:, col : col + width],
                         start=(a == 0),
                         stop=(a == PASSES - 1),
                     )
-                sums.append((acc[:, at - lo : at - lo + n], at, n))
+                sums.append((acc[:, at : at + width], slot + at, width))
 
-        rounds = [(a, lo, lo if lo == LOW else S - POOL, POOL if lo == LOW else lo) for a in range(PASSES) for lo in (LOW, HIGH)]
-        own = ROUND - POOL
-
-        (planes,) = rooms(0, [ROUND])
-        side, main = planes[:, :, 0:POOL], planes[:, :, POOL:ROUND]
+        (planes,) = planes_of(0, ROUND)
         for j in range(PACK):
-            on_vector(planes, 0, j, 0, 0, HALF)
-            on_scalar(planes, 0, j, 0, HALF, ROUND)
+            gather_on_vector(planes, 0, j, LOW, 0, HALF)
+            gather_on_scalar(planes, 0, j, LOW, HALF, ROUND)
 
-        turned = bank("sum4")
+        turned = bank("mid_a")
         nc.tensor.transpose(turned[:, 0:P], gate_rows[:], identity[:])
         nc.vector.tensor_copy(gate_col[:], turned[:, 0:ROWS])
-        low, mid, high = bank("low"), bank("mid"), bank("high")
+        psum_low, psum_mid, psum_high = bank("gate_low"), bank("gate_mid"), bank("gate_high")
+        for into, slot in ((psum_low, LOW + HALF), (psum_high, HIGH), (psum_mid, MID)):
+            for m in range(HALF // P):
+                col = slot // P - FIRST_ROW + m
+                nc.tensor.transpose(into[:, m * P : (m + 1) * P], gate_col[:, col : col + 1].to_broadcast([P, P]), identity[:])
 
-        def spread(into, at, row):
-            nc.tensor.transpose(into[:, at * P : (at + 1) * P], gate_col[:, row - ROW0 : row - ROW0 + 1].to_broadcast([P, P]), identity[:])
-
-        for m in range(4):
-            spread(low, m, 4 + m)
-        for m in range(4):
-            spread(high, m, 12 + m)
-        for m in range(4):
-            spread(mid, m, 8 + m)
-
-        def stage(tag, slots=HALF):
-            return keep.tile([P, PACK * slots], BF16, name=tag, tag=tag, align_bytes=64)
-
-        for r, (a, lo, pool_lo, own_lo) in enumerate(rounds):
-            shared, alone = stage("shared", HALF + P), stage("alone", HALF - P)
-            pool = POOL if r + 1 < len(rounds) else POOL_FOURTH
-            rest = HALF + P - pool
-            if lo == LOW:
-                gate_and_round(nc.gpsimd, shared, 0, side, 0, gate_low[:], WALK)
+        rounds = [(a, base) for a in range(PASSES) for base in (LOW, HIGH)]
+        for r, (a, base) in enumerate(rounds):
+            shared, own = stage("shared", SHARED), stage("own", OWN)
+            count = GPSIMD_SLOTS[r]
+            fill = SHARED - count
+            if base == LOW:
+                on_gpsimd(shared, 0, planes, 0, gate_low[:, 0:count])
             else:
-                gate_and_round(nc.gpsimd, shared, rest, side, 0, gate_high[:, POOL - pool :], WALK)
+                on_gpsimd(shared, fill, planes, ROUND - count, gate_high[:, GPSIMD_MOST - count :])
+
             if r + 1 < len(rounds):
-                na, nlo = rounds[r + 1][:2]
-                (planes,) = rooms(r + 1, [ROUND])
-                npool = POOL if r + 2 < len(rounds) else POOL_FOURTH
-                if nlo == LOW:
-                    nside, nmain = planes[:, :, 0:npool], planes[:, :, npool:ROUND]
-                else:
-                    nside, nmain = planes[:, :, ROUND - npool : ROUND], planes[:, :, 0 : ROUND - npool]
-                on_scalar(planes, na, 1, nlo, SHARE - ROUND, ROUND)
-                on_scalar(planes, na, 2, nlo, 0, ROUND)
-                on_scalar(planes, na, 3, nlo, 0, ROUND)
-                before, after = (planes, na, 0, nlo, 0, ROUND), (planes, na, 1, nlo, 0, SHARE - ROUND)
+                next_a, next_base = rounds[r + 1]
+                (next_planes,) = planes_of(r + 1, ROUND)
+                cut = VECTOR_SHARE - ROUND
+                gather_on_scalar(next_planes, next_a, 1, next_base, cut, ROUND)
+                gather_on_scalar(next_planes, next_a, 2, next_base, 0, ROUND)
+                gather_on_scalar(next_planes, next_a, 3, next_base, 0, ROUND)
+                gather_on_vector(next_planes, next_a, 0, next_base, 0, ROUND)
+                last_gather = (next_planes, next_a, 1, next_base, 0, cut)
             else:
-                nside, nmain = rooms(r + 1, [HALF, HALF])
-                on_scalar(nside, 0, 2, MID, SHARE_FOURTH - ROUND, HALF)
-                on_scalar(nside, 0, 3, MID, 0, HALF)
+                next_planes, mid_pass1 = planes_of(r + 1, HALF)
+                cut = VECTOR_SHARE_LAST - 2 * HALF
+                gather_on_scalar(next_planes, 0, 2, MID, cut, HALF)
+                gather_on_scalar(next_planes, 0, 3, MID, 0, HALF)
                 for j in range(PACK):
-                    on_scalar(nmain, 1, j, MID, 0, HALF)
-                on_vector(nside, 0, 0, MID, 0, HALF)
-                before, after = (nside, 0, 1, MID, 0, HALF), (nside, 0, 2, MID, 0, SHARE_FOURTH - ROUND)
-            on_vector(*before)
-            if lo == LOW:
-                gate_and_round(nc.vector, alone, 0, main, rest, low[:, P:HALF])
-                gate_and_round(nc.vector, shared, pool, main, 0, low[:, P - rest : P])
+                    gather_on_scalar(mid_pass1, 1, j, MID, 0, HALF)
+                gather_on_vector(next_planes, 0, 0, MID, 0, HALF)
+                gather_on_vector(next_planes, 0, 1, MID, 0, HALF)
+                last_gather = (next_planes, 0, 2, MID, 0, cut)
+            if base == LOW:
+                on_vector(own, 0, planes, SHARED, psum_low[:, SHARED - HALF : HALF])
+                on_vector(shared, count, planes, count, psum_low[:, count - HALF : SHARED - HALF])
             else:
-                gate_and_round(nc.vector, alone, 0, main, 0, high[:, 0 : HALF - P])
-                gate_and_round(nc.vector, shared, 0, main, HALF - P, high[:, HALF - P : HALF - P + rest])
-            on_vector(*after)
-            if lo == LOW:
-                code_tiles(a, lo, HALF)
-                code_tiles(a, lo + HALF, HALF, behind=r)
-                quantize(shared, 0, a, lo, HALF)
-                quantize(shared, HALF, a, lo + HALF, P)
-                quantize(alone, 0, a, lo + HALF + P, HALF - P)
-            else:
-                code_tiles(a, lo + HALF, HALF)
-                code_tiles(a, lo, HALF, behind=r)
-                quantize(shared, P, a, lo + HALF, HALF)
-                quantize(shared, 0, a, lo + HALF - P, P)
-                quantize(alone, 0, a, lo, HALF - P)
-            if a == PASSES - 1:
-                tags = ("sum0", "sum1") if lo == LOW else ("low", "high")
-                multiply(bank(tags[0]), lo, HALF)
-                multiply(bank(tags[1]), lo + HALF, HALF)
-            side, main = nside, nmain
+                on_vector(own, 0, planes, 0, psum_high[:, 0:OWN])
+                on_vector(shared, 0, planes, OWN, psum_high[:, OWN : OWN + fill])
+            gather_on_vector(*last_gather)
 
-        shared, alone = stage("shared"), stage("alone")
-        gate_and_round(nc.gpsimd, shared, 0, side, 0, gate_mid[:], WALK)
-        gate_and_round(nc.vector, shared, POOL_LAST, side, POOL_LAST, mid[:, POOL_LAST:HALF])
-        gate_and_round(nc.vector, alone, 0, main, 0, mid[:, 0 : C + P])
+            gpsimd_half, vector_half = (base, base + HALF) if base == LOW else (base + HALF, base)
+            code_tiles(a, gpsimd_half, HALF)
+            code_tiles(a, vector_half, HALF, pool=ring, offset=PLANES_AT[r] + TILE_BYTES - 4 * HALF)
+            if base == LOW:
+                quantize(shared, 0, a, base, HALF)
+                quantize(shared, HALF, a, base + HALF, SHARED - HALF)
+                quantize(own, 0, a, base + SHARED, OWN)
+            else:
+                quantize(shared, SHARED - HALF, a, base + HALF, HALF)
+                quantize(shared, 0, a, base + OWN, SHARED - HALF)
+                quantize(own, 0, a, base, OWN)
+            if a == PASSES - 1:
+                tags = ("low_a", "low_b") if base == LOW else ("gate_low", "gate_high")
+                multiply(bank(tags[0]), base, HALF)
+                multiply(bank(tags[1]), base + HALF, HALF)
+            planes = next_planes
+
+        staged0, staged1 = stage("shared", HALF), stage("own", HALF)
+        on_gpsimd(staged0, 0, planes, 0, gate_mid[:])
+        on_vector(staged0, GPSIMD_LAST, planes, GPSIMD_LAST, psum_mid[:, GPSIMD_LAST:HALF])
+        on_vector(staged1, 0, mid_pass1, 0, psum_mid[:, 0 : C + P])
         code_tiles(0, MID, HALF)
         code_tiles(1, MID, C)
         code_tiles(1, MID + C, P)
         code_tiles(1, MID + C + P, P)
-        quantize(shared, 0, 0, MID, HALF)
-        quantize(alone, 0, 1, MID, C)
-        multiply(bank("sum4"), MID, C)
-        last = keep.tile([P, PACK * P], BF16, name="last", tag="last", align_bytes=64)
-        gate_and_round(nc.vector, last, 0, main, C + P, mid[:, C + P : HALF])
-        quantize(alone, C, 1, MID + C, P)
-        multiply(bank("sum5"), MID + C, P)
-        quantize(last, 0, 1, MID + C + P, P)
-        multiply(bank("edge"), MID + C + P, P)
+        quantize(staged0, 0, 0, MID, HALF)
+        quantize(staged1, 0, 1, MID, C)
+        multiply(bank("mid_a"), MID, C)
+        staged_last = stage("last", P)
+        on_vector(staged_last, 0, mid_pass1, C + P, psum_mid[:, C + P : HALF])
+        quantize(staged1, C, 1, MID + C, P)
+        multiply(bank("mid_b"), MID + C, P)
+        quantize(staged_last, 0, 1, MID + C + P, P)
+        multiply(bank("mid_c"), MID + C + P, P)
 
         y_sb = keep.tile([P, S], F32, name="y_sb", tag="x6", align_bytes=64)
-        for acc, at, n in sums:
-            nc.scalar.activation(out=y_sb[:, at : at + n], in_=acc, func=SILU, bias=b_sb[:, at // C : at // C + 1])
+        for acc, slot, count in sums:
+            nc.scalar.activation(out=y_sb[:, slot : slot + count], in_=acc, func=SILU, bias=b_sb[:, slot // C : slot // C + 1])
 
         first = keep.tile([P, T], F32, name="first", tag="x0", align_bytes=64)
         total = keep.tile([P, T], F32, name="total", tag="x1", align_bytes=64)

@@ -25,25 +25,28 @@ P = 128
 PACK = 4
 PASSES = K // (P * PACK)
 LIST = 16
+BANK = 512
 VECTOR_RUN, GPSIMD_RUN = 4, 8
-ROUND = 1024
-HALF = ROUND // 2
-LOW, MID, HIGH = 0, ROUND, ROUND + HALF
-GPSIMD_SLOTS = [544, 544, 544, 528, 272]
-GPSIMD_MOST, GPSIMD_LAST = max(GPSIMD_SLOTS), GPSIMD_SLOTS[-1]
-SHARED = HALF + P
-OWN = ROUND - SHARED
-VECTOR_SHARE = 1344
-VECTOR_SHARE_LAST = 1184
+MID, HIGH = 2 * BANK, 3 * BANK
+
+ROUNDS = [(0, 0, HIGH), (0, HIGH, S), (1, 0, MID), (1, HIGH, S), (1, MID, HIGH)]
+GPSIMD_SLOTS = [944, 544, 544, 384, 128]
+SHARED_SLOTS = [1024, 640, 640, 512, 128]
+HEAD_SCALAR = 736
+VECTOR_OFFSETS = [1024, 1344, 1344, 160]
 ALONE = 160
 COMBINE = [0, ALONE, 3 * ALONE, 5 * ALONE, 7 * ALONE, T]
-FIRST_ROW, ROWS = HALF // P, (S - ROUND) // P
 
-TILE_BYTES = PACK * ROUND * 4
+LOW_GATE = max(GPSIMD_SLOTS[0], GPSIMD_SLOTS[2])
+HIGH_GATE = max(GPSIMD_SLOTS[1], GPSIMD_SLOTS[3])
+MID_GATE = GPSIMD_SLOTS[4]
+FIRST_ROW = BANK // P
+ROWS = -(-(S - min(GPSIMD_SLOTS[1], GPSIMD_SLOTS[3])) // P) - FIRST_ROW
+
 OVERLAP = 1024
-STEP = TILE_BYTES - OVERLAP
-ODD = 2 * STEP + TILE_BYTES
-PLANES_AT = [2 * STEP, ODD + STEP, STEP, ODD, 0]
+TILE_BYTES = [4 * PACK * (end - first) for a, first, end in ROUNDS]
+EVEN = TILE_BYTES[4] + TILE_BYTES[2] + TILE_BYTES[0] - 2 * OVERLAP
+PLANES_AT = [EVEN - TILE_BYTES[0], EVEN + TILE_BYTES[3] - OVERLAP, TILE_BYTES[4] - OVERLAP, EVEN, 0]
 
 
 def tile_moe_pre_lin_silu_kernel(tc, xT, w_words, w_scales, b, gate, offs, pos1, pos2, out):
@@ -56,9 +59,9 @@ def tile_moe_pre_lin_silu_kernel(tc, xT, w_words, w_scales, b, gate, offs, pos1,
         offs_sb = keep.tile([P, S // LIST], U16, name="offs_sb")
         pos1_sb = keep.tile([P, T // LIST], U16, name="pos1_sb")
         pos2_sb = keep.tile([P, T // LIST], U16, name="pos2_sb")
-        gate_low = keep.tile([P, GPSIMD_MOST], F32, name="gate_low")
-        gate_mid = keep.tile([P, GPSIMD_LAST], F32, name="gate_mid", tag="last", align_bytes=64)
-        gate_high = keep.tile([P, GPSIMD_MOST], F32, name="gate_high")
+        gate_low = keep.tile([P, LOW_GATE], F32, name="gate_low")
+        gate_mid = keep.tile([P, MID_GATE], F32, name="gate_mid")
+        gate_high = keep.tile([P, HIGH_GATE], F32, name="gate_high")
         gate_rows = ring.tile([P, P], F32, name="gate_rows", align_bytes=64, offset=PLANES_AT[1] + OVERLAP)
         gate_col = keep.tile([P, ROWS], F32, name="gate_col")
         identity = keep.tile([P, P], F32, name="identity")
@@ -77,55 +80,57 @@ def tile_moe_pre_lin_silu_kernel(tc, xT, w_words, w_scales, b, gate, offs, pos1,
         x_rows = xT.rearrange("(a p j) t -> a j p t", a=PASSES, j=PACK)
         nc.sync.dma_start(out=x_sb[0][:], in_=x_rows[0, 0])
         nc.sync.dma_start(offs_sb[:], offs)
-        for j in range(1, PACK):
-            nc.sync.dma_start(out=x_sb[j][:], in_=x_rows[0, j])
+        nc.sync.dma_start(out=x_sb[1][:], in_=x_rows[0, 1])
+        nc.sync.dma_start(out=gate_low[:], in_=gate[0:P, 0:LOW_GATE])
+        nc.sync.dma_start(out=x_sb[2][:], in_=x_rows[0, 2])
+        nc.sync.dma_start(out=x_sb[3][:], in_=x_rows[0, 3])
         nc.sync.dma_start(out=gate_rows[0:ROWS, :], in_=gate[0, FIRST_ROW * P : (FIRST_ROW + ROWS) * P].rearrange("(m c) -> m c", c=P))
-        nc.sync.dma_start(out=gate_low[:], in_=gate[0:P, 0:GPSIMD_MOST])
         for j in range(PACK):
             nc.sync.dma_start(out=x_sb[PACK + j][:], in_=x_rows[1, j])
-        nc.sync.dma_start(out=gate_high[:], in_=gate[0:P, S - GPSIMD_MOST : S])
+        nc.sync.dma_start(out=gate_high[:], in_=gate[0:P, S - HIGH_GATE : S])
         nc.sync.dma_start(out=w_sb[:].bitcast(I32), in_=w_words.rearrange("e a p c -> p (e a) c").bitcast(I32))
         scale_rows = w_scales.rearrange("e a q n -> q (e a) n").bitcast(I32)
         for quad in range(4):
             nc.sync.dma_start(out=ws_sb[32 * quad : 32 * quad + 4].bitcast(I32), in_=scale_rows[4 * quad : 4 * quad + 4])
-        nc.sync.dma_start(out=gate_mid[:], in_=gate[0:P, MID : MID + GPSIMD_LAST])
+        nc.sync.dma_start(out=gate_mid[:], in_=gate[0:P, MID : MID + MID_GATE])
         nc.sync.dma_start(out=b_sb[:], in_=b)
         nc.sync.dma_start(pos1_sb[:], pos1)
         nc.sync.dma_start(pos2_sb[:], pos2)
 
-        def planes_of(r, slots):
-            tile = ring.tile([P, PACK * ROUND], F32, name="planes%d" % r, align_bytes=64, offset=PLANES_AT[r])
-            return [tile[:, PACK * at : PACK * (at + slots)].rearrange("p (j c) -> p j c", j=PACK) for at in range(0, ROUND, slots)]
+        def planes_of(r):
+            tile = ring.tile([P, TILE_BYTES[r] // 4], F32, name="planes%d" % r, align_bytes=64, offset=PLANES_AT[r])
+            return tile[:].rearrange("p (j c) -> p j c", j=PACK)
 
         def bank(tag):
-            return psum.tile([P, HALF], F32, name=tag, tag=tag)
+            return psum.tile([P, BANK], F32, name=tag, tag=tag)
 
         def stage(tag, slots):
             return keep.tile([P, PACK * slots], BF16, name=tag, tag=tag, align_bytes=64)
 
-        def tokens(a, j, slot, count):
-            return x_sb[a * PACK + j][:].indirect(offs_sb[:, slot // LIST : (slot + count) // LIST])
+        def tokens(r, j, at, to):
+            a, first, end = ROUNDS[r]
+            return x_sb[a * PACK + j][:].indirect(offs_sb[:, (first + at) // LIST : (first + to) // LIST])
 
-        def gather_on_scalar(planes, a, j, base, at, to):
-            nc.scalar.activation(planes[:, j, at:to], tokens(a, j, base + at, to - at), COPY)
+        def gather_on_scalar(planes, r, j, at, to):
+            nc.scalar.activation(planes[:, j, at:to], tokens(r, j, at, to), COPY)
 
-        def gather_on_vector(planes, a, j, base, at, to):
-            nc.vector.tensor_copy(planes[:, j, at:to], tokens(a, j, base + at, to - at))
+        def gather_on_vector(planes, r, j, at, to):
+            nc.vector.tensor_copy(planes[:, j, at:to], tokens(r, j, at, to))
 
-        def gate_and_round(engine, run, staged, to, planes, at, weights):
+        def gate_and_round(engine, run, staged, to, planes, at, weights, j0=0, j1=PACK):
             count = weights.shape[1]
             engine.tensor_tensor(
-                staged[:, to * PACK : (to + count) * PACK].rearrange("p (c i j) -> p c j i", i=run, j=PACK),
-                planes[:, :, at : at + count].rearrange("p j (c i) -> p c j i", i=run),
-                weights.rearrange("p (c i) -> p c i", i=run).unsqueeze(2).to_broadcast([P, count // run, PACK, run]),
+                staged[:, to * PACK : (to + count) * PACK].rearrange("p (c i j) -> p c j i", i=run, j=PACK)[:, :, j0:j1, :],
+                planes[:, j0:j1, at : at + count].rearrange("p j (c i) -> p c j i", i=run),
+                weights.rearrange("p (c i) -> p c i", i=run).unsqueeze(2).to_broadcast([P, count // run, j1 - j0, run]),
                 MULT,
             )
 
-        def on_gpsimd(staged, to, planes, at, weights):
-            gate_and_round(nc.gpsimd, GPSIMD_RUN, staged, to, planes, at, weights)
+        gate_banks = []
 
-        def on_vector(staged, to, planes, at, weights):
-            gate_and_round(nc.vector, VECTOR_RUN, staged, to, planes, at, weights)
+        def on_vector(staged, to, planes, r, at, count):
+            col = ROUNDS[r][1] + at - FIRST_ROW * P
+            gate_and_round(nc.vector, VECTOR_RUN, staged, to, planes, at, gate_banks[col // BANK][:, col % BANK : col % BANK + count])
 
         codes = {}
 
@@ -162,103 +167,89 @@ def tile_moe_pre_lin_silu_kernel(tc, xT, w_words, w_scales, b, gate, offs, pos1,
                     )
                 sums.append((acc[:, at : at + width], slot + at, width))
 
-        (planes,) = planes_of(0, ROUND)
+        planes = planes_of(0)
         for j in range(PACK):
-            gather_on_vector(planes, 0, j, LOW, 0, HALF)
-            gather_on_scalar(planes, 0, j, LOW, HALF, ROUND)
+            gather_on_scalar(planes, 0, j, 0, HEAD_SCALAR)
+            gather_on_vector(planes, 0, j, HEAD_SCALAR, HIGH)
 
-        turned = bank("mid_a")
+        turned = bank("sums0")
         nc.tensor.transpose(turned[:, 0:P], gate_rows[:], identity[:])
         nc.vector.tensor_copy(gate_col[:], turned[:, 0:ROWS])
-        psum_low, psum_mid, psum_high = bank("gate_low"), bank("gate_mid"), bank("gate_high")
-        for into, slot in ((psum_low, LOW + HALF), (psum_high, HIGH), (psum_mid, MID)):
-            for m in range(HALF // P):
-                col = slot // P - FIRST_ROW + m
-                nc.tensor.transpose(into[:, m * P : (m + 1) * P], gate_col[:, col : col + 1].to_broadcast([P, P]), identity[:])
+        for m in range(ROWS):
+            if m % (BANK // P) == 0:
+                gate_banks.append(bank("gate%d" % len(gate_banks)))
+            col = m % (BANK // P) * P
+            nc.tensor.transpose(gate_banks[-1][:, col : col + P], gate_col[:, m : m + 1].to_broadcast([P, P]), identity[:])
 
-        rounds = [(a, base) for a in range(PASSES) for base in (LOW, HIGH)]
-        for r, (a, base) in enumerate(rounds):
-            shared, own = stage("shared", SHARED), stage("own", OWN)
-            count = GPSIMD_SLOTS[r]
-            fill = SHARED - count
-            if base == LOW:
-                on_gpsimd(shared, 0, planes, 0, gate_low[:, 0:count])
+        for r, (a, first, end) in enumerate(ROUNDS):
+            slots, count, filled = end - first, GPSIMD_SLOTS[r], SHARED_SLOTS[r]
+            fill, rest = filled - count, slots - filled
+            shared, own = stage("shared", filled), stage("own", rest)
+            high = first == HIGH
+            if high:
+                gate_and_round(nc.gpsimd, GPSIMD_RUN, shared, fill, planes, slots - count, gate_high[:, HIGH_GATE - count :])
+            elif first == MID:
+                gate_and_round(nc.gpsimd, GPSIMD_RUN, shared, 0, planes, 0, gate_mid[:])
+            elif r == 0:
+                for j in range(0, PACK, 2):
+                    gate_and_round(nc.gpsimd, GPSIMD_RUN, shared, 0, planes, 0, gate_low[:, 0:count], j, j + 2)
             else:
-                on_gpsimd(shared, fill, planes, ROUND - count, gate_high[:, GPSIMD_MOST - count :])
+                gate_and_round(nc.gpsimd, GPSIMD_RUN, shared, 0, planes, 0, gate_low[:, 0:count])
 
-            if r + 1 < len(rounds):
-                next_a, next_base = rounds[r + 1]
-                (next_planes,) = planes_of(r + 1, ROUND)
-                cut = VECTOR_SHARE - ROUND
-                gather_on_scalar(next_planes, next_a, 1, next_base, cut, ROUND)
-                gather_on_scalar(next_planes, next_a, 2, next_base, 0, ROUND)
-                gather_on_scalar(next_planes, next_a, 3, next_base, 0, ROUND)
-                gather_on_vector(next_planes, next_a, 0, next_base, 0, ROUND)
-                last_gather = (next_planes, next_a, 1, next_base, 0, cut)
-            else:
-                next_planes, mid_pass1 = planes_of(r + 1, HALF)
-                cut = VECTOR_SHARE_LAST - 2 * HALF
-                gather_on_scalar(next_planes, 0, 2, MID, cut, HALF)
-                gather_on_scalar(next_planes, 0, 3, MID, 0, HALF)
-                for j in range(PACK):
-                    gather_on_scalar(mid_pass1, 1, j, MID, 0, HALF)
-                gather_on_vector(next_planes, 0, 0, MID, 0, HALF)
-                gather_on_vector(next_planes, 0, 1, MID, 0, HALF)
-                last_gather = (next_planes, 0, 2, MID, 0, cut)
-            if base == LOW:
-                on_vector(own, 0, planes, SHARED, psum_low[:, SHARED - HALF : HALF])
-                on_vector(shared, count, planes, count, psum_low[:, count - HALF : SHARED - HALF])
-            else:
-                on_vector(own, 0, planes, 0, psum_high[:, 0:OWN])
-                on_vector(shared, 0, planes, OWN, psum_high[:, OWN : OWN + fill])
-            gather_on_vector(*last_gather)
+            whole, cut = 0, 0
+            if r + 1 < len(ROUNDS):
+                next_planes = planes_of(r + 1)
+                next_slots = ROUNDS[r + 1][2] - ROUNDS[r + 1][1]
+                whole, cut = divmod(VECTOR_OFFSETS[r], next_slots)
+                gather_on_scalar(next_planes, r + 1, whole, cut, next_slots)
+                for j in range(whole + 1, PACK):
+                    gather_on_scalar(next_planes, r + 1, j, 0, next_slots)
+                for j in range(whole):
+                    gather_on_vector(next_planes, r + 1, j, 0, next_slots)
+            if fill:
+                on_vector(shared, 0 if high else count, planes, r, rest if high else count, fill)
+            on_vector(own, 0, planes, r, 0 if high else filled, rest)
+            if cut:
+                gather_on_vector(next_planes, r + 1, whole, 0, cut)
 
-            gpsimd_half, vector_half = (base, base + HALF) if base == LOW else (base + HALF, base)
-            code_tiles(a, gpsimd_half, HALF)
-            code_tiles(a, vector_half, HALF, pool=ring, offset=PLANES_AT[r] + TILE_BYTES - 4 * HALF)
-            if base == LOW:
-                quantize(shared, 0, a, base, HALF)
-                quantize(shared, HALF, a, base + HALF, SHARED - HALF)
-                quantize(own, 0, a, base + SHARED, OWN)
+            early = filled if filled < BANK else filled // BANK * BANK
+            late = slots - early
+            code_tiles(a, end - early if high else first, early)
+            code_tiles(a, first if high else first + early, late, pool=ring, offset=PLANES_AT[r] + TILE_BYTES[r] - 4 * late)
+            if high:
+                quantize(shared, filled - early, a, end - early, early)
+                if filled > early:
+                    quantize(shared, 0, a, first + rest, filled - early)
+                quantize(own, 0, a, first, rest)
             else:
-                quantize(shared, SHARED - HALF, a, base + HALF, HALF)
-                quantize(shared, 0, a, base + OWN, SHARED - HALF)
-                quantize(own, 0, a, base, OWN)
-            if a == PASSES - 1:
-                tags = ("low_a", "low_b") if base == LOW else ("gate_low", "gate_high")
-                multiply(bank(tags[0]), base, HALF)
-                multiply(bank(tags[1]), base + HALF, HALF)
-            planes = next_planes
+                quantize(shared, 0, a, first, early)
+                if filled > early:
+                    quantize(shared, early, a, first + early, filled - early)
+                if first != MID:
+                    quantize(own, 0, a, first + filled, rest)
+            if a == PASSES - 1 and first != MID:
+                multiply(bank("sums%d" % (2 * high)), end - BANK if high else first, BANK)
+                multiply(bank("sums%d" % (2 * high + 1)), first if high else first + BANK, BANK)
+            if r + 1 < len(ROUNDS):
+                planes = next_planes
 
-        staged0, staged1 = stage("shared", HALF), stage("own", HALF)
-        on_gpsimd(staged0, 0, planes, 0, gate_mid[:])
-        on_vector(staged0, GPSIMD_LAST, planes, GPSIMD_LAST, psum_mid[:, GPSIMD_LAST:HALF])
-        on_vector(staged1, 0, mid_pass1, 0, psum_mid[:, 0 : C + P])
-        code_tiles(0, MID, HALF)
-        code_tiles(1, MID, C)
-        code_tiles(1, MID + C, P)
-        code_tiles(1, MID + C + P, P)
-        quantize(staged0, 0, 0, MID, HALF)
-        quantize(staged1, 0, 1, MID, C)
-        multiply(bank("mid_a"), MID, C)
-        staged_last = stage("last", P)
-        on_vector(staged_last, 0, mid_pass1, C + P, psum_mid[:, C + P : HALF])
-        quantize(staged1, C, 1, MID + C, P)
-        multiply(bank("mid_b"), MID + C, P)
-        quantize(staged_last, 0, 1, MID + C + P, P)
-        multiply(bank("mid_c"), MID + C + P, P)
+        multiply(bank("gate3"), MID, P)
+        quantize(own, P, 1, MID + C, C)
+        multiply(bank("gate0"), MID + C, C)
+        quantize(own, 0, 1, MID + P, P)
+        multiply(bank("gate2"), MID + P, P)
 
         y_sb = keep.tile([P, S], F32, name="y_sb", tag="x6", align_bytes=64)
         for acc, slot, count in sums:
             nc.scalar.activation(out=y_sb[:, slot : slot + count], in_=acc, func=SILU, bias=b_sb[:, slot // C : slot // C + 1])
 
-        first = keep.tile([P, T], F32, name="first", tag="x0", align_bytes=64)
+        first_result = keep.tile([P, T], F32, name="first_result", tag="x0", align_bytes=64)
         total = keep.tile([P, T], F32, name="total", tag="x1", align_bytes=64)
         for lo, hi in zip(COMBINE, COMBINE[1:]):
             fetched = y_sb[:].indirect(pos1_sb[:, lo // LIST : hi // LIST])
             if hi == ALONE:
-                nc.vector.tensor_copy(first[:, lo:hi], fetched)
+                nc.vector.tensor_copy(first_result[:, lo:hi], fetched)
             else:
-                nc.scalar.activation(first[:, lo:hi], fetched, COPY)
-            nc.vector.tensor_tensor(total[:, lo:hi], y_sb[:].indirect(pos2_sb[:, lo // LIST : hi // LIST]), first[:, lo:hi], ADD)
+                nc.scalar.activation(first_result[:, lo:hi], fetched, COPY)
+            nc.vector.tensor_tensor(total[:, lo:hi], y_sb[:].indirect(pos2_sb[:, lo // LIST : hi // LIST]), first_result[:, lo:hi], ADD)
             nc.sync.dma_start(out=out[:, lo:hi], in_=total[:, lo:hi])

@@ -30,10 +30,10 @@ VECTOR_RUN, GPSIMD_RUN = 4, 8
 MID, HIGH = 2 * BANK, 3 * BANK
 
 ROUNDS = [(0, 0, HIGH), (0, HIGH, S), (1, 0, MID), (1, HIGH, S), (1, MID, HIGH)]
-GPSIMD_SLOTS = [944, 544, 544, 384, 128]
+GPSIMD_SLOTS = [944, 560, 560, 384, 128]
 SHARED_SLOTS = [1024, 640, 640, 512, 128]
-HEAD_SCALAR = 736
-VECTOR_OFFSETS = [1024, 1344, 1344, 160]
+HEAD_SCALAR = [704, 704, 672, 672]
+VECTOR_OFFSETS = [1024, 1408, 1408, 224]
 ALONE = 160
 COMBINE = [0, ALONE, 3 * ALONE, 5 * ALONE, 7 * ALONE, T]
 
@@ -169,8 +169,8 @@ def tile_moe_pre_lin_silu_kernel(tc, xT, w_words, w_scales, b, gate, offs, pos1,
 
         planes = planes_of(0)
         for j in range(PACK):
-            gather_on_scalar(planes, 0, j, 0, HEAD_SCALAR)
-            gather_on_vector(planes, 0, j, HEAD_SCALAR, HIGH)
+            gather_on_scalar(planes, 0, j, 0, HEAD_SCALAR[j])
+            gather_on_vector(planes, 0, j, HEAD_SCALAR[j], HIGH)
 
         turned = bank("sums0")
         nc.tensor.transpose(turned[:, 0:P], gate_rows[:], identity[:])

@@ -30,10 +30,10 @@ VECTOR_RUN, GPSIMD_RUN = 4, 8
 MID, HIGH = 2 * BANK, 3 * BANK
 
 ROUNDS = [(0, 0, HIGH), (0, HIGH, S), (1, 0, MID), (1, HIGH, S), (1, MID, HIGH)]
-GPSIMD_SLOTS = [944, 560, 560, 384, 128]
+GPSIMD_SLOTS = [880, 544, 544, 352, 128]
 SHARED_SLOTS = [1024, 640, 640, 512, 128]
-HEAD_SCALAR = [704, 704, 672, 672]
-VECTOR_OFFSETS = [1024, 1408, 1408, 224]
+HEAD_SCALAR = [736, 736, 704, 704]
+VECTOR_OFFSETS = [1024, 1376, 1376, 192]
 ALONE = 160
 COMBINE = [0, ALONE, 3 * ALONE, 5 * ALONE, 7 * ALONE, T]
 

@@ -30,18 +30,17 @@ VECTOR_RUN, GPSIMD_RUN = 4, 8
 MID, HIGH = 2 * BANK, 3 * BANK
 
 ROUNDS = [(0, 0, HIGH), (0, HIGH, S), (1, 0, MID), (1, HIGH, S), (1, MID, HIGH)]
-GPSIMD_SLOTS = [880, 544, 544, 352, 128]
-SHARED_SLOTS = [1024, 640, 640, 512, 128]
-HEAD_SCALAR = [736, 736, 704, 704]
-VECTOR_OFFSETS = [1024, 1376, 1376, 192]
+GPSIMD_SLOTS = [880, 552, 552, 360, 128]
+LAST_SLOTS = 3
+EARLY = [BANK, BANK, BANK, BANK, P]
+STAGE_AT = [P, P // 2, 0, 0, 0]
+HEAD_SCALAR = [736, 704, 704, 704]
+VECTOR_OFFSETS = [1024, 1440, 1440, 192]
 ALONE = 160
 COMBINE = [0, ALONE, 3 * ALONE, 5 * ALONE, 7 * ALONE, T]
 
-LOW_GATE = max(GPSIMD_SLOTS[0], GPSIMD_SLOTS[2])
-HIGH_GATE = max(GPSIMD_SLOTS[1], GPSIMD_SLOTS[3])
-MID_GATE = GPSIMD_SLOTS[4]
 FIRST_ROW = BANK // P
-ROWS = -(-(S - min(GPSIMD_SLOTS[1], GPSIMD_SLOTS[3])) // P) - FIRST_ROW
+ROWS = S // P - FIRST_ROW
 
 OVERLAP = 1024
 TILE_BYTES = [4 * PACK * (end - first) for a, first, end in ROUNDS]
@@ -59,9 +58,8 @@ def tile_moe_pre_lin_silu_kernel(tc, xT, w_words, w_scales, b, gate, offs, pos1,
         offs_sb = keep.tile([P, S // LIST], U16, name="offs_sb")
         pos1_sb = keep.tile([P, T // LIST], U16, name="pos1_sb")
         pos2_sb = keep.tile([P, T // LIST], U16, name="pos2_sb")
-        gate_low = keep.tile([P, LOW_GATE], F32, name="gate_low")
-        gate_mid = keep.tile([P, MID_GATE], F32, name="gate_mid")
-        gate_high = keep.tile([P, HIGH_GATE], F32, name="gate_high")
+        gate_sb = {r: keep.tile([P, GPSIMD_SLOTS[r]], F32, name="gate_sb%d" % r) for r in (0, 1, 3, 4)}
+        gate_sb[2] = gate_sb[0]
         gate_rows = ring.tile([P, P], F32, name="gate_rows", align_bytes=64, offset=PLANES_AT[1] + OVERLAP)
         gate_col = keep.tile([P, ROWS], F32, name="gate_col")
         identity = keep.tile([P, P], F32, name="identity")
@@ -69,6 +67,12 @@ def tile_moe_pre_lin_silu_kernel(tc, xT, w_words, w_scales, b, gate, offs, pos1,
         w_sb = keep.tile([P, E * PASSES, 2 * N], U8, name="w_sb", align_bytes=64)
         ws_sb = keep.tile([P, E * PASSES, N], U8, name="ws_sb", align_bytes=64)
         b_sb = keep.tile([P, E], F32, name="b_sb")
+        staged = keep.tile([P, PACK * (STAGE_AT[0] + HIGH)], BF16, name="staged", align_bytes=64)
+
+        def load_gate(r):
+            a, first, end = ROUNDS[r]
+            at = end - GPSIMD_SLOTS[r] if r == LAST_SLOTS else first
+            nc.sync.dma_start(out=gate_sb[r][:], in_=gate[0:P, at : at + GPSIMD_SLOTS[r]])
 
         nc.vector.memset(gate_rows[:], 0.0)
         nc.vector.memset(ws_sb[:].bitcast(I32), 0)
@@ -81,18 +85,19 @@ def tile_moe_pre_lin_silu_kernel(tc, xT, w_words, w_scales, b, gate, offs, pos1,
         nc.sync.dma_start(out=x_sb[0][:], in_=x_rows[0, 0])
         nc.sync.dma_start(offs_sb[:], offs)
         nc.sync.dma_start(out=x_sb[1][:], in_=x_rows[0, 1])
-        nc.sync.dma_start(out=gate_low[:], in_=gate[0:P, 0:LOW_GATE])
+        load_gate(0)
         nc.sync.dma_start(out=x_sb[2][:], in_=x_rows[0, 2])
         nc.sync.dma_start(out=x_sb[3][:], in_=x_rows[0, 3])
         nc.sync.dma_start(out=gate_rows[0:ROWS, :], in_=gate[0, FIRST_ROW * P : (FIRST_ROW + ROWS) * P].rearrange("(m c) -> m c", c=P))
         for j in range(PACK):
             nc.sync.dma_start(out=x_sb[PACK + j][:], in_=x_rows[1, j])
-        nc.sync.dma_start(out=gate_high[:], in_=gate[0:P, S - HIGH_GATE : S])
+        load_gate(1)
         nc.sync.dma_start(out=w_sb[:].bitcast(I32), in_=w_words.rearrange("e a p c -> p (e a) c").bitcast(I32))
         scale_rows = w_scales.rearrange("e a q n -> q (e a) n").bitcast(I32)
         for quad in range(4):
             nc.sync.dma_start(out=ws_sb[32 * quad : 32 * quad + 4].bitcast(I32), in_=scale_rows[4 * quad : 4 * quad + 4])
-        nc.sync.dma_start(out=gate_mid[:], in_=gate[0:P, MID : MID + MID_GATE])
+        load_gate(3)
+        load_gate(4)
         nc.sync.dma_start(out=b_sb[:], in_=b)
         nc.sync.dma_start(pos1_sb[:], pos1)
         nc.sync.dma_start(pos2_sb[:], pos2)
@@ -104,9 +109,6 @@ def tile_moe_pre_lin_silu_kernel(tc, xT, w_words, w_scales, b, gate, offs, pos1,
         def bank(tag):
             return psum.tile([P, BANK], F32, name=tag, tag=tag)
 
-        def stage(tag, slots):
-            return keep.tile([P, PACK * slots], BF16, name=tag, tag=tag, align_bytes=64)
-
         def tokens(r, j, at, to):
             a, first, end = ROUNDS[r]
             return x_sb[a * PACK + j][:].indirect(offs_sb[:, (first + at) // LIST : (first + to) // LIST])
@@ -117,7 +119,7 @@ def tile_moe_pre_lin_silu_kernel(tc, xT, w_words, w_scales, b, gate, offs, pos1,
         def gather_on_vector(planes, r, j, at, to):
             nc.vector.tensor_copy(planes[:, j, at:to], tokens(r, j, at, to))
 
-        def gate_and_round(engine, run, staged, to, planes, at, weights, j0=0, j1=PACK):
+        def gate_and_round(engine, run, to, planes, at, weights, j0=0, j1=PACK):
             count = weights.shape[1]
             engine.tensor_tensor(
                 staged[:, to * PACK : (to + count) * PACK].rearrange("p (c i j) -> p c j i", i=run, j=PACK)[:, :, j0:j1, :],
@@ -128,9 +130,17 @@ def tile_moe_pre_lin_silu_kernel(tc, xT, w_words, w_scales, b, gate, offs, pos1,
 
         gate_banks = []
 
-        def on_vector(staged, to, planes, r, at, count):
-            col = ROUNDS[r][1] + at - FIRST_ROW * P
-            gate_and_round(nc.vector, VECTOR_RUN, staged, to, planes, at, gate_banks[col // BANK][:, col % BANK : col % BANK + count])
+        def place(r, at):
+            if r == LAST_SLOTS:
+                return (at + BANK) % (2 * BANK)
+            return STAGE_AT[r] + (at if r < LAST_SLOTS or at < EARLY[r] else at - EARLY[r] + BANK)
+
+        def on_vector(planes, r, at, to):
+            while at < to:
+                col = ROUNDS[r][1] + at - FIRST_ROW * P
+                count = min(to - at, BANK - col % BANK)
+                gate_and_round(nc.vector, VECTOR_RUN, place(r, at), planes, at, gate_banks[col // BANK][:, col % BANK : col % BANK + count])
+                at = at + count
 
         codes = {}
 
@@ -140,7 +150,9 @@ def tile_moe_pre_lin_silu_kernel(tc, xT, w_words, w_scales, b, gate, offs, pos1,
             for u in range(0, count, P):
                 codes[a, slot + u] = (words, scales, u)
 
-        def quantize(staged, at, a, slot, count):
+        def quantize(r, slot, count):
+            a, first, end = ROUNDS[r]
+            at = place(r, slot - first)
             words, scales, col = codes[a, slot]
             nc.vector.quantize_mx(
                 out=words[:, col : col + count].bitcast(FP8X4),
@@ -182,19 +194,11 @@ def tile_moe_pre_lin_silu_kernel(tc, xT, w_words, w_scales, b, gate, offs, pos1,
             nc.tensor.transpose(gate_banks[-1][:, col : col + P], gate_col[:, m : m + 1].to_broadcast([P, P]), identity[:])
 
         for r, (a, first, end) in enumerate(ROUNDS):
-            slots, count, filled = end - first, GPSIMD_SLOTS[r], SHARED_SLOTS[r]
-            fill, rest = filled - count, slots - filled
-            shared, own = stage("shared", filled), stage("own", rest)
-            high = first == HIGH
-            if high:
-                gate_and_round(nc.gpsimd, GPSIMD_RUN, shared, fill, planes, slots - count, gate_high[:, HIGH_GATE - count :])
-            elif first == MID:
-                gate_and_round(nc.gpsimd, GPSIMD_RUN, shared, 0, planes, 0, gate_mid[:])
-            elif r == 0:
-                for j in range(0, PACK, 2):
-                    gate_and_round(nc.gpsimd, GPSIMD_RUN, shared, 0, planes, 0, gate_low[:, 0:count], j, j + 2)
-            else:
-                gate_and_round(nc.gpsimd, GPSIMD_RUN, shared, 0, planes, 0, gate_low[:, 0:count])
+            slots, count = end - first, GPSIMD_SLOTS[r]
+            at = slots - count if r == LAST_SLOTS else 0
+            step = 2 if r == 0 else PACK
+            for j in range(0, PACK, step):
+                gate_and_round(nc.gpsimd, GPSIMD_RUN, place(r, at), planes, at, gate_sb[r][:, 0:count], j, j + step)
 
             whole, cut = 0, 0
             if r + 1 < len(ROUNDS):
@@ -206,37 +210,33 @@ def tile_moe_pre_lin_silu_kernel(tc, xT, w_words, w_scales, b, gate, offs, pos1,
                     gather_on_scalar(next_planes, r + 1, j, 0, next_slots)
                 for j in range(whole):
                     gather_on_vector(next_planes, r + 1, j, 0, next_slots)
-            if fill:
-                on_vector(shared, 0 if high else count, planes, r, rest if high else count, fill)
-            on_vector(own, 0, planes, r, 0 if high else filled, rest)
+            if r == LAST_SLOTS:
+                on_vector(planes, r, 0, at)
+            else:
+                on_vector(planes, r, count, slots)
             if cut:
                 gather_on_vector(next_planes, r + 1, whole, 0, cut)
 
-            early = filled if filled < BANK else filled // BANK * BANK
-            late = slots - early
-            code_tiles(a, end - early if high else first, early)
-            code_tiles(a, first if high else first + early, late, pool=ring, offset=PLANES_AT[r] + TILE_BYTES[r] - 4 * late)
-            if high:
-                quantize(shared, filled - early, a, end - early, early)
-                if filled > early:
-                    quantize(shared, 0, a, first + rest, filled - early)
-                quantize(own, 0, a, first, rest)
+            early, late = EARLY[r], slots - EARLY[r]
+            early_at, late_at = (first + late, first) if r == LAST_SLOTS else (first, first + early)
+            code_tiles(a, early_at, early)
+            if count > early:
+                code_tiles(a, late_at, late)
             else:
-                quantize(shared, 0, a, first, early)
-                if filled > early:
-                    quantize(shared, early, a, first + early, filled - early)
-                if first != MID:
-                    quantize(own, 0, a, first + filled, rest)
+                code_tiles(a, late_at, late, pool=ring, offset=PLANES_AT[r] + TILE_BYTES[r] - 4 * late)
+            quantize(r, early_at, early)
+            if first != MID:
+                quantize(r, late_at, late)
             if a == PASSES - 1 and first != MID:
-                multiply(bank("sums%d" % (2 * high)), end - BANK if high else first, BANK)
-                multiply(bank("sums%d" % (2 * high + 1)), first if high else first + BANK, BANK)
+                multiply(bank("sums%d" % (2 * r - 4)), early_at, BANK)
+                multiply(bank("sums%d" % (2 * r - 3)), late_at, BANK)
             if r + 1 < len(ROUNDS):
                 planes = next_planes
 
         multiply(bank("gate3"), MID, P)
-        quantize(own, P, 1, MID + C, C)
+        quantize(4, MID + C, C)
         multiply(bank("gate0"), MID + C, C)
-        quantize(own, 0, 1, MID + P, P)
+        quantize(4, MID + P, P)
         multiply(bank("gate2"), MID + P, P)
 
         y_sb = keep.tile([P, S], F32, name="y_sb", tag="x6", align_bytes=64)

@@ -30,14 +30,13 @@ VECTOR_RUN, GPSIMD_RUN = 4, 8
 MID, HIGH = 2 * BANK, 3 * BANK
 
 ROUNDS = [(0, 0, HIGH), (0, HIGH, S), (1, 0, MID), (1, HIGH, S), (1, MID, HIGH)]
-GPSIMD_SLOTS = [880, 552, 552, 360, 128]
+GPSIMD_SLOTS = [888, 552, 552, 360, 160]
 LAST_SLOTS = 3
 EARLY = [BANK, BANK, BANK, BANK, P]
-STAGE_AT = [P, P // 2, 0, 0, 0]
-HEAD_SCALAR = [736, 704, 704, 704]
-VECTOR_OFFSETS = [1024, 1440, 1440, 192]
-ALONE = 160
-COMBINE = [0, ALONE, 3 * ALONE, 5 * ALONE, 7 * ALONE, T]
+STAGE_AT = [P, P // 2, 0, 0, C]
+HEAD_SCALAR = [736, 736, 704, 704]
+VECTOR_OFFSETS = [1024, 1408, 1408, 192]
+COMBINE = [0, 160, 544, 896, 1152, T]
 
 FIRST_ROW = BANK // P
 ROWS = S // P - FIRST_ROW
@@ -133,7 +132,7 @@ def tile_moe_pre_lin_silu_kernel(tc, xT, w_words, w_scales, b, gate, offs, pos1,
         def place(r, at):
             if r == LAST_SLOTS:
                 return (at + BANK) % (2 * BANK)
-            return STAGE_AT[r] + (at if r < LAST_SLOTS or at < EARLY[r] else at - EARLY[r] + BANK)
+            return STAGE_AT[r] + at
 
         def on_vector(planes, r, at, to):
             while at < to:
@@ -220,7 +219,7 @@ def tile_moe_pre_lin_silu_kernel(tc, xT, w_words, w_scales, b, gate, offs, pos1,
             early, late = EARLY[r], slots - EARLY[r]
             early_at, late_at = (first + late, first) if r == LAST_SLOTS else (first, first + early)
             code_tiles(a, early_at, early)
-            if count > early:
+            if r < LAST_SLOTS:
                 code_tiles(a, late_at, late)
             else:
                 code_tiles(a, late_at, late, pool=ring, offset=PLANES_AT[r] + TILE_BYTES[r] - 4 * late)
@@ -244,12 +243,17 @@ def tile_moe_pre_lin_silu_kernel(tc, xT, w_words, w_scales, b, gate, offs, pos1,
             nc.scalar.activation(out=y_sb[:, slot : slot + count], in_=acc, func=SILU, bias=b_sb[:, slot // C : slot // C + 1])
 
         first_result = keep.tile([P, T], F32, name="first_result", tag="x0", align_bytes=64)
+        second_result = keep.tile([P, T - COMBINE[-2]], F32, name="second_result", tag="x2", align_bytes=64)
         total = keep.tile([P, T], F32, name="total", tag="x1", align_bytes=64)
         for lo, hi in zip(COMBINE, COMBINE[1:]):
-            fetched = y_sb[:].indirect(pos1_sb[:, lo // LIST : hi // LIST])
-            if hi == ALONE:
-                nc.vector.tensor_copy(first_result[:, lo:hi], fetched)
+            first_of = y_sb[:].indirect(pos1_sb[:, lo // LIST : hi // LIST])
+            second_of = y_sb[:].indirect(pos2_sb[:, lo // LIST : hi // LIST])
+            if lo == 0:
+                nc.vector.tensor_copy(first_result[:, lo:hi], first_of)
             else:
-                nc.scalar.activation(first_result[:, lo:hi], fetched, COPY)
-            nc.vector.tensor_tensor(total[:, lo:hi], y_sb[:].indirect(pos2_sb[:, lo // LIST : hi // LIST]), first_result[:, lo:hi], ADD)
+                nc.scalar.activation(first_result[:, lo:hi], first_of, COPY)
+            if hi == T:
+                nc.scalar.activation(second_result[:], second_of, COPY)
+                second_of = second_result[:]
+            nc.vector.tensor_tensor(total[:, lo:hi], second_of, first_result[:, lo:hi], ADD)
             nc.sync.dma_start(out=out[:, lo:hi], in_=total[:, lo:hi])

@@ -42,7 +42,8 @@ FIRST_ROW = BANK // P
 ROWS = S // P - FIRST_ROW
 
 OVERLAP = 1024
-TILE_BYTES = [4 * PACK * (end - first) for a, first, end in ROUNDS]
+GAP = 16
+TILE_BYTES = [4 * PACK * (end - first + GAP) for a, first, end in ROUNDS]
 EVEN = TILE_BYTES[4] + TILE_BYTES[2] + TILE_BYTES[0] - 2 * OVERLAP
 PLANES_AT = [EVEN - TILE_BYTES[0], EVEN + TILE_BYTES[3] - OVERLAP, TILE_BYTES[4] - OVERLAP, EVEN, 0]
 

@@ -27,25 +27,22 @@ PASSES = K // (P * PACK)
 LIST = 16
 BANK = 512
 VECTOR_RUN, GPSIMD_RUN = 4, 8
-MID, HIGH = 2 * BANK, 3 * BANK
 
-ROUNDS = [(0, 0, HIGH), (0, HIGH, S), (1, 0, MID), (1, HIGH, S), (1, MID, HIGH)]
-GPSIMD_SLOTS = [888, 552, 552, 360, 160]
-LAST_SLOTS = 3
-EARLY = [BANK, BANK, BANK, BANK, P]
-STAGE_AT = [P, P // 2, 0, 0, C]
-HEAD_SCALAR = [736, 736, 704, 704]
-VECTOR_OFFSETS = [1024, 1408, 1408, 192]
+ROUNDS = [(0, 0, S), (1, 0, 2 * BANK), (1, 2 * BANK, 4 * BANK), (1, 4 * BANK, S)]
+GPSIMD_SLOTS = [1568, 552, 360, 160]
+FRONT = GPSIMD_SLOTS[0]
+FRONT_GATHERS = [
+    ("vector", 0, 0, 800), ("scalar", 0, 800, FRONT),
+    ("vector", 1, 0, 256), ("scalar", 1, 256, 512),
+    ("vector", 1, 512, 1056), ("scalar", 1, 1056, FRONT),
+    ("vector", 2, 0, 1024), ("scalar", 2, 1024, FRONT),
+    ("scalar", 3, 0, 1024), ("vector", 3, 1024, FRONT),
+]
+FRONT_PRODUCTS = [(0, 512, 0, 2), (512, 1024, 0, 2), (0, 1024, 2, 4), (1024, FRONT, 0, 4)]
+VECTOR_OFFSETS = [672, 1408, 192]
+STAGE_AT = [0, 3 * BANK, 3 * BANK, 3 * BANK]
 COMBINE = [0, 160, 544, 896, 1152, T]
-
-FIRST_ROW = BANK // P
-ROWS = S // P - FIRST_ROW
-
-OVERLAP = 1024
 GAP = 16
-TILE_BYTES = [4 * PACK * (end - first + GAP) for a, first, end in ROUNDS]
-EVEN = TILE_BYTES[4] + TILE_BYTES[2] + TILE_BYTES[0] - 2 * OVERLAP
-PLANES_AT = [EVEN - TILE_BYTES[0], EVEN + TILE_BYTES[3] - OVERLAP, TILE_BYTES[4] - OVERLAP, EVEN, 0]
 
 
 def tile_moe_pre_lin_silu_kernel(tc, xT, w_words, w_scales, b, gate, offs, pos1, pos2, out):
@@ -55,69 +52,72 @@ def tile_moe_pre_lin_silu_kernel(tc, xT, w_words, w_scales, b, gate, offs, pos1,
         ring = ctx.enter_context(tc.tile_pool(name="ring", bufs=1))
         psum = ctx.enter_context(tc.psum_pool(name="psum", bufs=1))
 
+        def span(slots):
+            return 4 * PACK * (slots + GAP)
+
+        front_at = 0
+        back_at = front_at + span(FRONT)
+        round1_at = back_at + span(S - FRONT)
+        planes_at = [None, round1_at, front_at, round1_at]
+
         offs_sb = keep.tile([P, S // LIST], U16, name="offs_sb")
         pos1_sb = keep.tile([P, T // LIST], U16, name="pos1_sb")
         pos2_sb = keep.tile([P, T // LIST], U16, name="pos2_sb")
-        gate_sb = {r: keep.tile([P, GPSIMD_SLOTS[r]], F32, name="gate_sb%d" % r) for r in (0, 1, 3, 4)}
-        gate_sb[2] = gate_sb[0]
-        gate_rows = ring.tile([P, P], F32, name="gate_rows", align_bytes=64, offset=PLANES_AT[1] + OVERLAP)
-        gate_col = keep.tile([P, ROWS], F32, name="gate_col")
+        gate_front = keep.tile([P, FRONT], F32, name="gate_front", align_bytes=64)
+        gate_last = keep.tile([P, GPSIMD_SLOTS[3]], F32, name="gate_last", align_bytes=64)
+        col_last = ring.tile([P, PACK], F32, name="col_last", align_bytes=64, offset=back_at)
+        col_mid = ring.tile([P, 3, PACK], F32, name="col_mid", align_bytes=64, offset=round1_at)
         identity = keep.tile([P, P], F32, name="identity")
         x_sb = [keep.tile([P, T], F32, name="x%d" % u, align_bytes=64) for u in range(PASSES * PACK)]
         w_sb = keep.tile([P, E * PASSES, 2 * N], U8, name="w_sb", align_bytes=64)
         ws_sb = keep.tile([P, E * PASSES, N], U8, name="ws_sb", align_bytes=64)
         b_sb = keep.tile([P, E], F32, name="b_sb")
-        staged = keep.tile([P, PACK * (STAGE_AT[0] + HIGH)], BF16, name="staged", align_bytes=64)
+        staged = keep.tile([P, PACK * S], BF16, name="staged", align_bytes=64)
 
-        def load_gate(r):
-            a, first, end = ROUNDS[r]
-            at = end - GPSIMD_SLOTS[r] if r == LAST_SLOTS else first
-            nc.sync.dma_start(out=gate_sb[r][:], in_=gate[0:P, at : at + GPSIMD_SLOTS[r]])
-
-        nc.vector.memset(gate_rows[:], 0.0)
         nc.vector.memset(ws_sb[:].bitcast(I32), 0)
         warm = keep.tile([P, 2], F32, name="warm")
         nc.vector.memset(warm[:, 0:1], 0.0)
         nc.scalar.activation(out=warm[:, 1:2], in_=warm[:, 0:1], func=SILU)
         make_identity(nc, identity[:])
 
+        def load_gate(at, to):
+            nc.sync.dma_start(out=gate_front[:, at:to], in_=gate[0:P, at:to])
+
         x_rows = xT.rearrange("(a p j) t -> a j p t", a=PASSES, j=PACK)
         nc.sync.dma_start(out=x_sb[0][:], in_=x_rows[0, 0])
         nc.sync.dma_start(offs_sb[:], offs)
         nc.sync.dma_start(out=x_sb[1][:], in_=x_rows[0, 1])
-        load_gate(0)
+        load_gate(0, BANK)
         nc.sync.dma_start(out=x_sb[2][:], in_=x_rows[0, 2])
+        load_gate(BANK, 2 * BANK)
         nc.sync.dma_start(out=x_sb[3][:], in_=x_rows[0, 3])
-        nc.sync.dma_start(out=gate_rows[0:ROWS, :], in_=gate[0, FIRST_ROW * P : (FIRST_ROW + ROWS) * P].rearrange("(m c) -> m c", c=P))
+        nc.sync.dma_start(out=col_last[:], in_=gate[0, 4 * BANK : S].rearrange("(n i) -> n i", i=PACK))
+        nc.sync.dma_start(out=col_mid[:], in_=gate[1, BANK : 4 * BANK].rearrange("(m n i) -> n m i", m=3, i=PACK))
         for j in range(PACK):
             nc.sync.dma_start(out=x_sb[PACK + j][:], in_=x_rows[1, j])
-        load_gate(1)
+        load_gate(2 * BANK, FRONT)
         nc.sync.dma_start(out=w_sb[:].bitcast(I32), in_=w_words.rearrange("e a p c -> p (e a) c").bitcast(I32))
         scale_rows = w_scales.rearrange("e a q n -> q (e a) n").bitcast(I32)
         for quad in range(4):
             nc.sync.dma_start(out=ws_sb[32 * quad : 32 * quad + 4].bitcast(I32), in_=scale_rows[4 * quad : 4 * quad + 4])
-        load_gate(3)
-        load_gate(4)
+        nc.sync.dma_start(out=gate_last[:], in_=gate[0:P, 4 * BANK : 4 * BANK + GPSIMD_SLOTS[3]])
         nc.sync.dma_start(out=b_sb[:], in_=b)
         nc.sync.dma_start(pos1_sb[:], pos1)
         nc.sync.dma_start(pos2_sb[:], pos2)
 
-        def planes_of(r):
-            tile = ring.tile([P, TILE_BYTES[r] // 4], F32, name="planes%d" % r, align_bytes=64, offset=PLANES_AT[r])
+        def planes_tile(name, slots, at):
+            tile = ring.tile([P, span(slots) // 4], F32, name=name, align_bytes=64, offset=at)
             return tile[:].rearrange("p (j c) -> p j c", j=PACK)
 
         def bank(tag):
             return psum.tile([P, BANK], F32, name=tag, tag=tag)
 
-        def tokens(r, j, at, to):
-            a, first, end = ROUNDS[r]
-            return x_sb[a * PACK + j][:].indirect(offs_sb[:, (first + at) // LIST : (first + to) // LIST])
-
-        def gather_on_scalar(planes, r, j, at, to):
-            nc.scalar.activation(planes[:, j, at:to], tokens(r, j, at, to), COPY)
-
-        def gather_on_vector(planes, r, j, at, to):
-            nc.vector.tensor_copy(planes[:, j, at:to], tokens(r, j, at, to))
+        def gather(engine, planes, base, a, j, at, to):
+            tokens = x_sb[a * PACK + j][:].indirect(offs_sb[:, at // LIST : to // LIST])
+            if engine == "vector":
+                nc.vector.tensor_copy(planes[:, j, at - base : to - base], tokens)
+            else:
+                nc.scalar.activation(planes[:, j, at - base : to - base], tokens, COPY)
 
         def gate_and_round(engine, run, to, planes, at, weights, j0=0, j1=PACK):
             count = weights.shape[1]
@@ -128,37 +128,32 @@ def tile_moe_pre_lin_silu_kernel(tc, xT, w_words, w_scales, b, gate, offs, pos1,
                 MULT,
             )
 
-        gate_banks = []
+        gate_banks = {}
 
-        def place(r, at):
-            if r == LAST_SLOTS:
-                return (at + BANK) % (2 * BANK)
-            return STAGE_AT[r] + at
+        def spread_gate(m, columns):
+            gate_banks[m] = bank("gate%d" % m)
+            for i in range(PACK):
+                nc.tensor.transpose(gate_banks[m][:, i:BANK:PACK], columns[:, i : i + 1].to_broadcast([P, P]), identity[:])
 
-        def on_vector(planes, r, at, to):
+        def on_vector(planes, base, r, at, to):
             while at < to:
-                col = ROUNDS[r][1] + at - FIRST_ROW * P
-                count = min(to - at, BANK - col % BANK)
-                gate_and_round(nc.vector, VECTOR_RUN, place(r, at), planes, at, gate_banks[col // BANK][:, col % BANK : col % BANK + count])
+                col = at % BANK
+                count = min(to - at, BANK - col)
+                gate_and_round(
+                    nc.vector, VECTOR_RUN, STAGE_AT[r] + at - ROUNDS[r][1], planes, at - base, gate_banks[at // BANK][:, col : col + count]
+                )
                 at = at + count
 
         codes = {}
 
-        def code_tiles(a, slot, count, pool=keep, offset=None):
+        def quantize(r, slot, count, pool=keep, offset=None):
+            a, first, end = ROUNDS[r]
             words = pool.tile([P, count], U32, name="codes%d_%d" % (a, slot), align_bytes=64, offset=offset)
             scales = keep.tile([P, count], U8, name="scales%d_%d" % (a, slot), align_bytes=64)
             for u in range(0, count, P):
                 codes[a, slot + u] = (words, scales, u)
-
-        def quantize(r, slot, count):
-            a, first, end = ROUNDS[r]
-            at = place(r, slot - first)
-            words, scales, col = codes[a, slot]
-            nc.vector.quantize_mx(
-                out=words[:, col : col + count].bitcast(FP8X4),
-                scales=scales[:, col : col + count],
-                in_=staged[:, at * PACK : (at + count) * PACK],
-            )
+            at = STAGE_AT[r] + slot - first
+            nc.vector.quantize_mx(out=words[:].bitcast(FP8X4), scales=scales[:], in_=staged[:, at * PACK : (at + count) * PACK])
 
         sums = []
 
@@ -179,65 +174,60 @@ def tile_moe_pre_lin_silu_kernel(tc, xT, w_words, w_scales, b, gate, offs, pos1,
                     )
                 sums.append((acc[:, at : at + width], slot + at, width))
 
-        planes = planes_of(0)
+        def gather_round(r):
+            a, first, end = ROUNDS[r]
+            planes = planes_tile("planes%d" % r, end - first, planes_at[r])
+            whole, cut = divmod(VECTOR_OFFSETS[r - 1], end - first)
+            gather("scalar", planes, first, a, whole, first + cut, end)
+            for j in range(whole + 1, PACK):
+                gather("scalar", planes, first, a, j, first, end)
+            for j in range(whole):
+                gather("vector", planes, first, a, j, first, end)
+            return planes, whole, cut
+
+        front = planes_tile("front", FRONT, front_at)
+        for engine, j, at, to in FRONT_GATHERS:
+            gather(engine, front, 0, 0, j, at, to)
+        for at, to, j0, j1 in FRONT_PRODUCTS:
+            gate_and_round(nc.gpsimd, GPSIMD_RUN, at, front, at, gate_front[:, at:to], j0, j1)
+        spread_gate(4, col_last)
+        for m in (3, 1, 2):
+            spread_gate(m, col_mid[:, m - 1, :])
+        back = planes_tile("back", S - FRONT, back_at)
         for j in range(PACK):
-            gather_on_scalar(planes, 0, j, 0, HEAD_SCALAR[j])
-            gather_on_vector(planes, 0, j, HEAD_SCALAR[j], HIGH)
+            gather("vector" if j % 2 == 0 else "scalar", back, FRONT, 0, j, FRONT, S)
+        planes, whole, cut = gather_round(1)
+        on_vector(back, FRONT, 0, FRONT, S)
+        gather("vector", planes, ROUNDS[1][1], 1, whole, ROUNDS[1][1], ROUNDS[1][1] + cut)
+        quantize(0, 0, 2 * BANK)
+        quantize(0, 3 * BANK, 2 * BANK)
+        quantize(0, 2 * BANK, BANK)
 
-        turned = bank("sums0")
-        nc.tensor.transpose(turned[:, 0:P], gate_rows[:], identity[:])
-        nc.vector.tensor_copy(gate_col[:], turned[:, 0:ROWS])
-        for m in range(ROWS):
-            if m % (BANK // P) == 0:
-                gate_banks.append(bank("gate%d" % len(gate_banks)))
-            col = m % (BANK // P) * P
-            nc.tensor.transpose(gate_banks[-1][:, col : col + P], gate_col[:, m : m + 1].to_broadcast([P, P]), identity[:])
-
-        for r, (a, first, end) in enumerate(ROUNDS):
-            slots, count = end - first, GPSIMD_SLOTS[r]
-            at = slots - count if r == LAST_SLOTS else 0
-            step = 2 if r == 0 else PACK
-            for j in range(0, PACK, step):
-                gate_and_round(nc.gpsimd, GPSIMD_RUN, place(r, at), planes, at, gate_sb[r][:, 0:count], j, j + step)
-
-            whole, cut = 0, 0
-            if r + 1 < len(ROUNDS):
-                next_planes = planes_of(r + 1)
-                next_slots = ROUNDS[r + 1][2] - ROUNDS[r + 1][1]
-                whole, cut = divmod(VECTOR_OFFSETS[r], next_slots)
-                gather_on_scalar(next_planes, r + 1, whole, cut, next_slots)
-                for j in range(whole + 1, PACK):
-                    gather_on_scalar(next_planes, r + 1, j, 0, next_slots)
-                for j in range(whole):
-                    gather_on_vector(next_planes, r + 1, j, 0, next_slots)
-            if r == LAST_SLOTS:
-                on_vector(planes, r, 0, at)
+        for r in (1, 2):
+            a, first, end = ROUNDS[r]
+            count = GPSIMD_SLOTS[r]
+            gate_and_round(nc.gpsimd, GPSIMD_RUN, STAGE_AT[r], planes, 0, gate_front[:, first : first + count])
+            next_planes, whole, cut = gather_round(r + 1)
+            on_vector(planes, first, r, first + count, end)
+            gather("vector", next_planes, ROUNDS[r + 1][1], 1, whole, ROUNDS[r + 1][1], ROUNDS[r + 1][1] + cut)
+            quantize(r, first, BANK)
+            if r == 1:
+                quantize(r, first + BANK, BANK)
             else:
-                on_vector(planes, r, count, slots)
-            if cut:
-                gather_on_vector(next_planes, r + 1, whole, 0, cut)
+                quantize(r, first + BANK, BANK, pool=ring, offset=planes_at[r] + span(end - first) - 4 * BANK)
+            for slot in (first, first + BANK):
+                multiply(bank("sums%d" % (slot // BANK)), slot, BANK)
+            planes = next_planes
 
-            early, late = EARLY[r], slots - EARLY[r]
-            early_at, late_at = (first + late, first) if r == LAST_SLOTS else (first, first + early)
-            code_tiles(a, early_at, early)
-            if r < LAST_SLOTS:
-                code_tiles(a, late_at, late)
-            else:
-                code_tiles(a, late_at, late, pool=ring, offset=PLANES_AT[r] + TILE_BYTES[r] - 4 * late)
-            quantize(r, early_at, early)
-            if first != MID:
-                quantize(r, late_at, late)
-            if a == PASSES - 1 and first != MID:
-                multiply(bank("sums%d" % (2 * r - 4)), early_at, BANK)
-                multiply(bank("sums%d" % (2 * r - 3)), late_at, BANK)
-            if r + 1 < len(ROUNDS):
-                planes = next_planes
-
-        multiply(bank("gate3"), MID, P)
-        quantize(4, MID + C, C)
-        multiply(bank("gate0"), MID + C, C)
-        quantize(4, MID + P, P)
-        multiply(bank("gate2"), MID + P, P)
+        a, first, end = ROUNDS[3]
+        gate_and_round(nc.gpsimd, GPSIMD_RUN, STAGE_AT[3], planes, 0, gate_last[:])
+        on_vector(planes, first, 3, first + GPSIMD_SLOTS[3], end)
+        quantize(3, first, P)
+        multiply(bank("gate1"), first, P)
+        quantize(3, first + C, C, pool=ring, offset=planes_at[3] + span(end - first) - 4 * C)
+        multiply(bank("gate2"), first + C, C)
+        quantize(3, first + P, P)
+        multiply(bank("gate3"), first + P, P)
 
         y_sb = keep.tile([P, S], F32, name="y_sb", tag="x6", align_bytes=64)
         for acc, slot, count in sums:

@@ -43,6 +43,8 @@ VECTOR_OFFSETS = [672, 1408, 192]
 STAGE_AT = [0, 3 * BANK, 3 * BANK, 3 * BANK]
 COMBINE = [0, 160, 544, 896, 1152, T]
 GAP = 16
+FIRST_ROW = BANK // P
+ROWS = S // P - FIRST_ROW
 
 
 def tile_moe_pre_lin_silu_kernel(tc, xT, w_words, w_scales, b, gate, offs, pos1, pos2, out):
@@ -65,8 +67,8 @@ def tile_moe_pre_lin_silu_kernel(tc, xT, w_words, w_scales, b, gate, offs, pos1,
         pos2_sb = keep.tile([P, T // LIST], U16, name="pos2_sb")
         gate_front = keep.tile([P, FRONT], F32, name="gate_front", align_bytes=64)
         gate_last = keep.tile([P, GPSIMD_SLOTS[3]], F32, name="gate_last", align_bytes=64)
-        col_last = ring.tile([P, PACK], F32, name="col_last", align_bytes=64, offset=back_at)
-        col_mid = ring.tile([P, 3, PACK], F32, name="col_mid", align_bytes=64, offset=round1_at)
+        gate_rows = ring.tile([P, P], F32, name="gate_rows", align_bytes=64, offset=back_at)
+        gate_col = keep.tile([P, ROWS], F32, name="gate_col")
         identity = keep.tile([P, P], F32, name="identity")
         x_sb = [keep.tile([P, T], F32, name="x%d" % u, align_bytes=64) for u in range(PASSES * PACK)]
         w_sb = keep.tile([P, E * PASSES, 2 * N], U8, name="w_sb", align_bytes=64)
@@ -74,6 +76,7 @@ def tile_moe_pre_lin_silu_kernel(tc, xT, w_words, w_scales, b, gate, offs, pos1,
         b_sb = keep.tile([P, E], F32, name="b_sb")
         staged = keep.tile([P, PACK * S], BF16, name="staged", align_bytes=64)
 
+        nc.vector.memset(gate_rows[:], 0.0)
         nc.vector.memset(ws_sb[:].bitcast(I32), 0)
         warm = keep.tile([P, 2], F32, name="warm")
         nc.vector.memset(warm[:, 0:1], 0.0)
@@ -91,8 +94,7 @@ def tile_moe_pre_lin_silu_kernel(tc, xT, w_words, w_scales, b, gate, offs, pos1,
         nc.sync.dma_start(out=x_sb[2][:], in_=x_rows[0, 2])
         load_gate(BANK, 2 * BANK)
         nc.sync.dma_start(out=x_sb[3][:], in_=x_rows[0, 3])
-        nc.sync.dma_start(out=col_last[:], in_=gate[0, 4 * BANK : S].rearrange("(n i) -> n i", i=PACK))
-        nc.sync.dma_start(out=col_mid[:], in_=gate[1, BANK : 4 * BANK].rearrange("(m n i) -> n m i", m=3, i=PACK))
+        nc.sync.dma_start(out=gate_rows[0:ROWS, :], in_=gate[0, FIRST_ROW * P : S].rearrange("(m c) -> m c", c=P))
         for j in range(PACK):
             nc.sync.dma_start(out=x_sb[PACK + j][:], in_=x_rows[1, j])
         load_gate(2 * BANK, FRONT)
@@ -130,10 +132,11 @@ def tile_moe_pre_lin_silu_kernel(tc, xT, w_words, w_scales, b, gate, offs, pos1,
 
         gate_banks = {}
 
-        def spread_gate(m, columns):
+        def spread_gate(m):
             gate_banks[m] = bank("gate%d" % m)
-            for i in range(PACK):
-                nc.tensor.transpose(gate_banks[m][:, i:BANK:PACK], columns[:, i : i + 1].to_broadcast([P, P]), identity[:])
+            for col in range(0, BANK, P):
+                row = (m * BANK + col) // P - FIRST_ROW
+                nc.tensor.transpose(gate_banks[m][:, col : col + P], gate_col[:, row : row + 1].to_broadcast([P, P]), identity[:])
 
         def on_vector(planes, base, r, at, to):
             while at < to:
@@ -190,16 +193,18 @@ def tile_moe_pre_lin_silu_kernel(tc, xT, w_words, w_scales, b, gate, offs, pos1,
             gather(engine, front, 0, 0, j, at, to)
         for at, to, j0, j1 in FRONT_PRODUCTS:
             gate_and_round(nc.gpsimd, GPSIMD_RUN, at, front, at, gate_front[:, at:to], j0, j1)
-        spread_gate(4, col_last)
-        for m in (3, 1, 2):
-            spread_gate(m, col_mid[:, m - 1, :])
+        turned = bank("sums0")
+        nc.tensor.transpose(turned[:, 0:P], gate_rows[:], identity[:])
+        nc.vector.tensor_copy(gate_col[:], turned[:, 0:ROWS])
+        for m in (3, 4, 1, 2):
+            spread_gate(m)
         back = planes_tile("back", S - FRONT, back_at)
         for j in range(PACK):
             gather("vector" if j % 2 == 0 else "scalar", back, FRONT, 0, j, FRONT, S)
         planes, whole, cut = gather_round(1)
         on_vector(back, FRONT, 0, FRONT, S)
         gather("vector", planes, ROUNDS[1][1], 1, whole, ROUNDS[1][1], ROUNDS[1][1] + cut)
-        quantize(0, 0, 2 * BANK)
+        quantize(0, 0, 2 * BANK, pool=ring, offset=back_at - 4 * 2 * BANK)
         quantize(0, 3 * BANK, 2 * BANK)
         quantize(0, 2 * BANK, BANK)
 

@@ -29,17 +29,17 @@ BANK = 512
 VECTOR_RUN, GPSIMD_RUN = 4, 8
 
 ROUNDS = [(0, 0, S), (1, 0, 2 * BANK), (1, 2 * BANK, 4 * BANK), (1, 4 * BANK, S)]
-GPSIMD_SLOTS = [1568, 552, 360, 160]
+GPSIMD_SLOTS = [1632, 552, 360, 160]
 FRONT = GPSIMD_SLOTS[0]
 FRONT_GATHERS = [
-    ("vector", 0, 0, 800), ("scalar", 0, 800, FRONT),
+    ("vector", 0, 0, 832), ("scalar", 0, 832, FRONT),
     ("vector", 1, 0, 256), ("scalar", 1, 256, 512),
-    ("vector", 1, 512, 1056), ("scalar", 1, 1056, FRONT),
+    ("vector", 1, 512, 1088), ("scalar", 1, 1088, FRONT),
     ("vector", 2, 0, 1024), ("scalar", 2, 1024, FRONT),
     ("scalar", 3, 0, 1024), ("vector", 3, 1024, FRONT),
 ]
 FRONT_PRODUCTS = [(0, 512, 0, 2), (512, 1024, 0, 2), (0, 1024, 2, 4), (1024, FRONT, 0, 4)]
-VECTOR_OFFSETS = [672, 1408, 192]
+VECTOR_OFFSETS = [704, 1408, 192]
 STAGE_AT = [0, 3 * BANK, 3 * BANK, 3 * BANK]
 COMBINE = [0, 160, 544, 896, 1152, T]
 GAP = 16

from contextlib import ExitStack

import concourse.mybir as mybir
from concourse.masks import make_identity

K, T, E, C, N = 1024, 1280, 10, 256, 128
S = E * C
FLOPS = 2 * K * N * S
BYTES = 4 * K * T + E * K * N // 2 + E * K * N // 32 + 4 * N * E + 4 * S + 2 * 128 * (S + 2 * T) // 16 + 4 * N * T

F32 = mybir.dt.float32
BF16 = mybir.dt.bfloat16
I32 = mybir.dt.int32
U32 = mybir.dt.uint32
U16 = mybir.dt.uint16
U8 = mybir.dt.uint8
FP8X4 = mybir.dt.float8_e4m3fn_x4
FP4X4 = mybir.dt.float4_e2m1fn_x4
MULT = mybir.AluOpType.mult
ADD = mybir.AluOpType.add
COPY = mybir.ActivationFunctionType.Copy
SILU = mybir.ActivationFunctionType.Silu

P = 128
PACK = 4
PASSES = K // (P * PACK)
LIST = 16
BANK = 512
VECTOR_RUN, GPSIMD_RUN = 4, 8

ROUNDS = [(0, 0, S), (1, 0, 2 * BANK), (1, 2 * BANK, 4 * BANK), (1, 4 * BANK, S)]
GPSIMD_SLOTS = [1632, 552, 360, 160]
FRONT = GPSIMD_SLOTS[0]
FRONT_GATHERS = [
    ("vector", 0, 0, 832), ("scalar", 0, 832, FRONT),
    ("vector", 1, 0, 256), ("scalar", 1, 256, 512),
    ("vector", 1, 512, 1088), ("scalar", 1, 1088, FRONT),
    ("vector", 2, 0, 1024), ("scalar", 2, 1024, FRONT),
    ("scalar", 3, 0, 1024), ("vector", 3, 1024, FRONT),
]
FRONT_PRODUCTS = [(0, 512, 0, 2), (512, 1024, 0, 2), (0, 1024, 2, 4), (1024, FRONT, 0, 4)]
VECTOR_OFFSETS = [704, 1408, 192]
STAGE_AT = [0, 3 * BANK, 3 * BANK, 3 * BANK]
COMBINE = [0, 160, 544, 896, 1152, T]
GAP = 16
FIRST_ROW = BANK // P
ROWS = S // P - FIRST_ROW


def tile_moe_pre_lin_silu_kernel(tc, xT, w_words, w_scales, b, gate, offs, pos1, pos2, out):
    nc = tc.nc
    with ExitStack() as ctx:
        keep = ctx.enter_context(tc.tile_pool(name="keep", bufs=1))
        ring = ctx.enter_context(tc.tile_pool(name="ring", bufs=1))
        psum = ctx.enter_context(tc.psum_pool(name="psum", bufs=1))

        def span(slots):
            return 4 * PACK * (slots + GAP)

        front_at = 0
        back_at = front_at + span(FRONT)
        round1_at = back_at + span(S - FRONT)
        planes_at = [None, round1_at, front_at, round1_at]

        offs_sb = keep.tile([P, S // LIST], U16, name="offs_sb")
        pos1_sb = keep.tile([P, T // LIST], U16, name="pos1_sb")
        pos2_sb = keep.tile([P, T // LIST], U16, name="pos2_sb")
        gate_front = keep.tile([P, FRONT], F32, name="gate_front", align_bytes=64)
        gate_last = keep.tile([P, GPSIMD_SLOTS[3]], F32, name="gate_last", align_bytes=64)
        gate_rows = ring.tile([P, P], F32, name="gate_rows", align_bytes=64, offset=back_at)
        gate_col = keep.tile([P, ROWS], F32, name="gate_col")
        identity = keep.tile([P, P], F32, name="identity")
        x_sb = [keep.tile([P, T], F32, name="x%d" % u, align_bytes=64) for u in range(PASSES * PACK)]
        w_sb = keep.tile([P, E * PASSES, 2 * N], U8, name="w_sb", align_bytes=64)
        ws_sb = keep.tile([P, E * PASSES, N], U8, name="ws_sb", align_bytes=64)
        b_sb = keep.tile([P, E], F32, name="b_sb")
        staged = keep.tile([P, PACK * S], BF16, name="staged", align_bytes=64)

        nc.vector.memset(gate_rows[:], 0.0)
        nc.vector.memset(ws_sb[:].bitcast(I32), 0)
        warm = keep.tile([P, 2], F32, name="warm")
        nc.vector.memset(warm[:, 0:1], 0.0)
        nc.scalar.activation(out=warm[:, 1:2], in_=warm[:, 0:1], func=SILU)
        make_identity(nc, identity[:])

        def load_gate(at, to):
            nc.sync.dma_start(out=gate_front[:, at:to], in_=gate[0:P, at:to])

        x_rows = xT.rearrange("(a p j) t -> a j p t", a=PASSES, j=PACK)
        nc.sync.dma_start(out=x_sb[0][:], in_=x_rows[0, 0])
        nc.sync.dma_start(offs_sb[:], offs)
        nc.sync.dma_start(out=x_sb[1][:], in_=x_rows[0, 1])
        load_gate(0, BANK)
        nc.sync.dma_start(out=x_sb[2][:], in_=x_rows[0, 2])
        load_gate(BANK, 2 * BANK)
        nc.sync.dma_start(out=x_sb[3][:], in_=x_rows[0, 3])
        nc.sync.dma_start(out=gate_rows[0:ROWS, :], in_=gate[0, FIRST_ROW * P : S].rearrange("(m c) -> m c", c=P))
        for j in range(PACK):
            nc.sync.dma_start(out=x_sb[PACK + j][:], in_=x_rows[1, j])
        load_gate(2 * BANK, FRONT)
        nc.sync.dma_start(out=w_sb[:].bitcast(I32), in_=w_words.rearrange("e a p c -> p (e a) c").bitcast(I32))
        scale_rows = w_scales.rearrange("e a q n -> q (e a) n").bitcast(I32)
        for quad in range(4):
            nc.sync.dma_start(out=ws_sb[32 * quad : 32 * quad + 4].bitcast(I32), in_=scale_rows[4 * quad : 4 * quad + 4])
        nc.sync.dma_start(out=gate_last[:], in_=gate[0:P, 4 * BANK : 4 * BANK + GPSIMD_SLOTS[3]])
        nc.sync.dma_start(out=b_sb[:], in_=b)
        nc.sync.dma_start(pos1_sb[:], pos1)
        nc.sync.dma_start(pos2_sb[:], pos2)

        def planes_tile(name, slots, at):
            tile = ring.tile([P, span(slots) // 4], F32, name=name, align_bytes=64, offset=at)
            return tile[:].rearrange("p (j c) -> p j c", j=PACK)

        def bank(tag):
            return psum.tile([P, BANK], F32, name=tag, tag=tag)

        def gather(engine, planes, base, a, j, at, to):
            tokens = x_sb[a * PACK + j][:].indirect(offs_sb[:, at // LIST : to // LIST])
            if engine == "vector":
                nc.vector.tensor_copy(planes[:, j, at - base : to - base], tokens)
            else:
                nc.scalar.activation(planes[:, j, at - base : to - base], tokens, COPY)

        def gate_and_round(engine, run, to, planes, at, weights, j0=0, j1=PACK):
            count = weights.shape[1]
            engine.tensor_tensor(
                staged[:, to * PACK : (to + count) * PACK].rearrange("p (c i j) -> p c j i", i=run, j=PACK)[:, :, j0:j1, :],
                planes[:, j0:j1, at : at + count].rearrange("p j (c i) -> p c j i", i=run),
                weights.rearrange("p (c i) -> p c i", i=run).unsqueeze(2).to_broadcast([P, count // run, j1 - j0, run]),
                MULT,
            )

        gate_banks = {}

        def spread_gate(m):
            gate_banks[m] = bank("gate%d" % m)
            for col in range(0, BANK, P):
                row = (m * BANK + col) // P - FIRST_ROW
                nc.tensor.transpose(gate_banks[m][:, col : col + P], gate_col[:, row : row + 1].to_broadcast([P, P]), identity[:])

        def on_vector(planes, base, r, at, to):
            while at < to:
                col = at % BANK
                count = min(to - at, BANK - col)
                gate_and_round(
                    nc.vector, VECTOR_RUN, STAGE_AT[r] + at - ROUNDS[r][1], planes, at - base, gate_banks[at // BANK][:, col : col + count]
                )
                at = at + count

        codes = {}

        def quantize(r, slot, count, pool=keep, offset=None):
            a, first, end = ROUNDS[r]
            words = pool.tile([P, count], U32, name="codes%d_%d" % (a, slot), align_bytes=64, offset=offset)
            scales = keep.tile([P, count], U8, name="scales%d_%d" % (a, slot), align_bytes=64)
            for u in range(0, count, P):
                codes[a, slot + u] = (words, scales, u)
            at = STAGE_AT[r] + slot - first
            nc.vector.quantize_mx(out=words[:].bitcast(FP8X4), scales=scales[:], in_=staged[:, at * PACK : (at + count) * PACK])

        sums = []

        def multiply(acc, slot, count):
            width = min(count, C)
            for at in range(0, count, width):
                e = (slot + at) // C
                for a in range(PASSES):
                    words, scales, col = codes[a, slot + at]
                    nc.tensor.matmul_mx(
                        out=acc[:, at : at + width],
                        lhsT=w_sb[:, e * PASSES + a, :].bitcast(FP4X4),
                        lhsT_scale=ws_sb[:, e * PASSES + a, :],
                        rhs=words[:, col : col + width].bitcast(FP8X4),
                        rhs_scale=scales[:, col : col + width],
                        start=(a == 0),
                        stop=(a == PASSES - 1),
                    )
                sums.append((acc[:, at : at + width], slot + at, width))

        def gather_round(r):
            a, first, end = ROUNDS[r]
            planes = planes_tile("planes%d" % r, end - first, planes_at[r])
            whole, cut = divmod(VECTOR_OFFSETS[r - 1], end - first)
            gather("scalar", planes, first, a, whole, first + cut, end)
            for j in range(whole + 1, PACK):
                gather("scalar", planes, first, a, j, first, end)
            for j in range(whole):
                gather("vector", planes, first, a, j, first, end)
            return planes, whole, cut

        front = planes_tile("front", FRONT, front_at)
        for engine, j, at, to in FRONT_GATHERS:
            gather(engine, front, 0, 0, j, at, to)
        for at, to, j0, j1 in FRONT_PRODUCTS:
            gate_and_round(nc.gpsimd, GPSIMD_RUN, at, front, at, gate_front[:, at:to], j0, j1)
        turned = bank("sums0")
        nc.tensor.transpose(turned[:, 0:P], gate_rows[:], identity[:])
        nc.vector.tensor_copy(gate_col[:], turned[:, 0:ROWS])
        for m in (3, 4, 1, 2):
            spread_gate(m)
        back = planes_tile("back", S - FRONT, back_at)
        for j in range(PACK):
            gather("vector" if j % 2 == 0 else "scalar", back, FRONT, 0, j, FRONT, S)
        planes, whole, cut = gather_round(1)
        on_vector(back, FRONT, 0, FRONT, S)
        gather("vector", planes, ROUNDS[1][1], 1, whole, ROUNDS[1][1], ROUNDS[1][1] + cut)
        quantize(0, 0, 2 * BANK, pool=ring, offset=back_at - 4 * 2 * BANK)
        quantize(0, 3 * BANK, 2 * BANK)
        quantize(0, 2 * BANK, BANK)

        for r in (1, 2):
            a, first, end = ROUNDS[r]
            count = GPSIMD_SLOTS[r]
            gate_and_round(nc.gpsimd, GPSIMD_RUN, STAGE_AT[r], planes, 0, gate_front[:, first : first + count])
            next_planes, whole, cut = gather_round(r + 1)
            on_vector(planes, first, r, first + count, end)
            gather("vector", next_planes, ROUNDS[r + 1][1], 1, whole, ROUNDS[r + 1][1], ROUNDS[r + 1][1] + cut)
            quantize(r, first, BANK)
            if r == 1:
                quantize(r, first + BANK, BANK)
            else:
                quantize(r, first + BANK, BANK, pool=ring, offset=planes_at[r] + span(end - first) - 4 * BANK)
            for slot in (first, first + BANK):
                multiply(bank("sums%d" % (slot // BANK)), slot, BANK)
            planes = next_planes

        a, first, end = ROUNDS[3]
        gate_and_round(nc.gpsimd, GPSIMD_RUN, STAGE_AT[3], planes, 0, gate_last[:])
        on_vector(planes, first, 3, first + GPSIMD_SLOTS[3], end)
        quantize(3, first, P)
        multiply(bank("gate1"), first, P)
        quantize(3, first + C, C, pool=ring, offset=planes_at[3] + span(end - first) - 4 * C)
        multiply(bank("gate2"), first + C, C)
        quantize(3, first + P, P)
        multiply(bank("gate3"), first + P, P)

        y_sb = keep.tile([P, S], F32, name="y_sb", tag="x6", align_bytes=64)
        for acc, slot, count in sums:
            nc.scalar.activation(out=y_sb[:, slot : slot + count], in_=acc, func=SILU, bias=b_sb[:, slot // C : slot // C + 1])

        first_result = keep.tile([P, T], F32, name="first_result", tag="x0", align_bytes=64)
        second_result = keep.tile([P, T - COMBINE[-2]], F32, name="second_result", tag="x2", align_bytes=64)
        total = keep.tile([P, T], F32, name="total", tag="x1", align_bytes=64)
        for lo, hi in zip(COMBINE, COMBINE[1:]):
            first_of = y_sb[:].indirect(pos1_sb[:, lo // LIST : hi // LIST])
            second_of = y_sb[:].indirect(pos2_sb[:, lo // LIST : hi // LIST])
            if lo == 0:
                nc.vector.tensor_copy(first_result[:, lo:hi], first_of)
            else:
                nc.scalar.activation(first_result[:, lo:hi], first_of, COPY)
            if hi == T:
                nc.scalar.activation(second_result[:], second_of, COPY)
                second_of = second_result[:]
            nc.vector.tensor_tensor(total[:, lo:hi], second_of, first_result[:, lo:hi], ADD)
            nc.sync.dma_start(out=out[:, lo:hi], in_=total[:, lo:hi])
